import numpy as np
import ml_dtypes


def mxq(x, axis, fmt="e4m3"):
    dtype, down = {"e4m3": (ml_dtypes.float8_e4m3fn, 7), "e5m2": (ml_dtypes.float8_e5m2, 14)}[fmt]
    v = np.moveaxis(np.asarray(x, np.float32).astype(ml_dtypes.bfloat16).astype(np.float64), axis, -1)
    blocks = v.reshape(v.shape[:-1] + (-1, 32))
    amax = np.abs(blocks).max(-1, keepdims=True)
    byte = np.maximum(np.where(amax > 0, np.frexp(amax)[1] - 1 + 127, 0) - down, 1)
    scale = np.exp2(byte - 127.0)
    codes = (blocks / scale).astype(np.float32).astype(dtype).astype(np.float64)
    return np.moveaxis((codes * scale).reshape(v.shape), -1, axis)


WIDE = False


def mx_kscale(k):
    if not WIDE:
        return np.ones(k)
    levels = np.array([10, -10, 5, -5, 0])
    if k % 512:
        return np.exp2(np.random.permutation(np.resize(levels, k // 32))).repeat(32)
    a = np.empty((k // 512, 16))
    for p in range(k // 512):
        a[p, :8] = np.random.permutation(np.resize(levels, 8))
        for g in range(8):
            far = levels[np.abs(levels - a[p, g]) >= 10]
            a[p, g + 8] = far[np.random.randint(len(far))]
    return np.exp2(a.ravel()).repeat(32)


def f64(x):
    return np.asarray(x).astype(np.float64)


def striped(idx):
    return np.tile(np.asarray(idx).reshape(-1, 16).T, (8, 1)).astype(np.uint16)


def unstriped(offs):
    return offs[:16].T.reshape(-1).astype(np.int64)


B, N, T, D, DV, NQ = 4, 512, 4096, 512, 512, 128


def setup_inputs():
    n = np.random.standard_normal
    seg = T // B
    idx = np.concatenate([b * seg + np.random.permutation(seg)[:N] for b in range(B)])
    s = mx_kscale(D)[:, None]
    u = np.ones(T)
    u[idx] = mx_kscale(B * N)
    r = np.random.uniform(0.5, 2.0, T)
    raw = n((D, T)) / s / (u * r)
    return {
        "qT": (n((B, D, NQ)) * s * (1.00 / np.sqrt(D))).astype(np.float32),
        "cT": raw.astype(np.float32),
        "ts": np.tile(u * r, (128, 1)).astype(np.float32),
        "kb": np.tile(n(T), (128, 1)).astype(np.float32),
        "ch": np.tile(s[:, 0] * np.random.uniform(0.5, 2.0, D), (128, 1)).astype(np.float32),
        "offs": striped(idx),
    }


def reference(qT, cT, ts, kb, ch, offs):
    idx = unstriped(offs)
    c = f64(cT)
    pick = lambda x: x[:, idx].reshape(x.shape[0], B, N).transpose(1, 0, 2)
    q = f64(qT)
    score = mxq(q, 1, "e4m3").transpose(0, 2, 1) @ mxq(pick(c), 1, "e4m3")
    score = score * pick(f64(ts))[:, :1, :]
    score = score + pick(f64(kb))[:, :1, :]
    p = 1.0 / (1.0 + np.exp(-score))
    w = p * pick(f64(ts))[:, :1, :]
    y = mxq(w, 2, "e4m3") @ mxq(pick(c).transpose(0, 2, 1), 1, "e4m3")
    y = y / 16.0
    y = y * f64(ch)[:1]
    return y

@@ -1,0 +1,264 @@
+from contextlib import ExitStack
+
+import concourse.mybir as mybir
+from concourse.masks import make_identity
+
+B, N, T, D, NQ = 4, 512, 4096, 512, 128
+P = 128
+SEG = T // B
+LANES = 4
+LIST_COLUMNS = N // 16
+
+FLOPS = B * 2 * (2 * N * D * NQ)
+BYTES = 4 * (B * D * NQ + D * T + 2 * T + D + B * NQ * D) + 2 * P * (B * N // 16)
+
+CAST_ON_VECTOR = ((1, 1), (3, 1))
+
+F32 = mybir.dt.float32
+BF16 = mybir.dt.bfloat16
+U32 = mybir.dt.uint32
+U16 = mybir.dt.uint16
+U8 = mybir.dt.uint8
+FP8X4 = mybir.dt.float8_e4m3fn_x4
+MULT = mybir.AluOpType.mult
+COPY = mybir.ActivationFunctionType.Copy
+SIGMOID = mybir.ActivationFunctionType.Sigmoid
+
+
+def tile_attend_x_mla_sigmoid_seg_kernel(tc, qT, cT, ts, kb, ch, offs, out):
+    nc = tc.nc
+    with ExitStack() as ctx:
+        keep = ctx.enter_context(tc.tile_pool(name="keep", bufs=1))
+        ring3 = ctx.enter_context(tc.tile_pool(name="ring3", bufs=3))
+        ring2 = ctx.enter_context(tc.tile_pool(name="ring2", bufs=2))
+        psum2 = ctx.enter_context(tc.psum_pool(name="psum2", bufs=2))
+        psum4 = ctx.enter_context(tc.psum_pool(name="psum4", bufs=4))
+
+        lists = keep.tile([P, B * N // 16], U16, name="lists")
+        nc.sync.dma_start(lists[:], offs)
+
+        warm = keep.tile([P, 1], F32, name="warm")
+        nc.vector.memset(warm[:], 0.0)
+        warm_out = keep.tile([P, 1], F32, name="warm_out")
+        nc.scalar.activation(warm_out[:], warm[:], SIGMOID)
+
+        windows = {}
+        for name in ("ts", "kb"):
+            windows[name] = keep.tile([P, T], F32, name="window_" + name)
+        raw_first = keep.tile([P, 2, 2, SEG], F32, name="raw_first")
+        raw_later = keep.tile([P, 2 * (B - 1), 2, SEG], F32, name="raw_later")
+        q_raw = keep.tile([P, B, LANES, NQ], F32, name="q_raw")
+        chans = keep.tile([P, D], F32, name="chans")
+
+        def raw(b, u):
+            return raw_first[:, u] if b == 0 else raw_later[:, 2 * (b - 1) + u]
+
+        nc.vector.memset(windows["kb"][:, 0:SEG], 0.0)
+        nc.gpsimd.memset(windows["ts"][:, 0:SEG], 0.0)
+        nc.vector.memset(windows["kb"][:, SEG:T], 0.0)
+        nc.gpsimd.memset(windows["ts"][:, SEG:T], 0.0)
+        ident = keep.tile([P, P], F32, name="ident")
+        make_identity(nc, ident[:])
+
+        def load_rows(c0, c1):
+            for name, src in (("kb", kb), ("ts", ts)):
+                nc.sync.dma_start(windows[name][0:1, c0:c1], src[0:1, c0:c1])
+
+        cT_view = cT.rearrange("(p j) w -> p j w", j=LANES)
+
+        def load_pool(b, u, pieces=1):
+            w = SEG // pieces
+            for i in range(pieces):
+                nc.sync.dma_start(
+                    raw(b, u)[:, :, i * w : (i + 1) * w],
+                    cT_view[:, 2 * u : 2 * u + 2, b * SEG + i * w : b * SEG + (i + 1) * w],
+                )
+
+        load_rows(0, SEG)
+        load_pool(0, 0, pieces=2)
+        load_pool(0, 1)
+        load_rows(SEG, T)
+        load_pool(1, 0)
+        nc.sync.dma_start(
+            q_raw[:].rearrange("p b j q -> p b (j q)"),
+            qT.rearrange("b (p j) q -> p b (j q)", j=LANES),
+        )
+        load_pool(1, 1)
+        for b in range(2, B):
+            load_pool(b, 0)
+            load_pool(b, 1)
+        nc.sync.dma_start(chans[:], ch)
+
+        q_grp = keep.tile([P, B * NQ * LANES], BF16, align_bytes=64, name="q_grp")
+        q_codes = keep.tile([P, B * NQ], U32, align_bytes=64, name="q_codes")
+        q_scales = keep.tile([P, B * NQ], U8, align_bytes=64, name="q_scales")
+
+        pool = [keep.tile([P, 2 * T], BF16, name=f"pool{u}") for u in range(2)]
+        k_grp, tokens, scores, turned, acc = {}, {}, {}, {}, {}
+        v_codes, v_scales = {}, {}
+        token_rows = {}
+
+        def gather_tokens(b0, b1):
+            for name in ("kb", "ts"):
+                row = keep.tile([P, (b1 - b0) * N], F32, name=f"row_{name}{b0}")
+                window = windows[name][:, 0 : b1 * SEG]
+                nc.vector.tensor_copy(row[:], window.indirect(lists[:, b0 * LIST_COLUMNS : b1 * LIST_COLUMNS]))
+                token_rows[name, b0] = row
+
+        def turn_tokens(b0, b1, bank):
+            n = b1 - b0
+            for i, name in enumerate(("kb", "ts")):
+                view = token_rows[name, b0][:].rearrange("p (b s t) -> p b t s", t=LANES, b=n)
+                for b in range(n):
+                    for t in range(LANES):
+                        c0 = 2 * ((i * n + b) * LANES + t)
+                        nc.tensor.transpose(bank[:, c0 : c0 + P], view[:, b, t, :], ident[:])
+            columns = keep.tile([P, 2, n, LANES], F32, name=f"columns{b0}")
+            nc.vector.tensor_copy(
+                columns[:].rearrange("s i b t -> s (i b t)"),
+                bank[:, 0 : 4 * LANES * n].rearrange("s (i z) -> s i z", z=2)[:, :, 0],
+            )
+            for b in range(n):
+                tokens[b0 + b] = columns[:, :, b, :]
+
+        def cast(b, u, pieces=1):
+            w = SEG // pieces
+            for i in range(pieces):
+                c0 = 2 * (b * SEG + i * w)
+                pair_out = pool[u][:, c0 : c0 + 2 * w].rearrange("p (w e) -> p w e", e=2)
+                pair_in = raw(b, u)[:, :, i * w : (i + 1) * w].rearrange("p e w -> p w e")
+                if (b, u) in CAST_ON_VECTOR:
+                    nc.vector.tensor_copy(pair_out, pair_in)
+                else:
+                    nc.scalar.activation(pair_out, pair_in, COPY)
+
+        def gather(b, u):
+            if u == 0:
+                k_grp[b] = ring3.tile([P, N * LANES], BF16, align_bytes=64, name="k_grp")
+            words = k_grp[b][:].bitcast(U32).rearrange("p (t s u) -> p s t u", t=LANES, u=2)
+            window = pool[u][:].bitcast(U32)[:, 0 : (b + 1) * SEG]
+            nc.vector.tensor_copy(
+                words[:, :, :, u], window.indirect(lists[:, b * LIST_COLUMNS : (b + 1) * LIST_COLUMNS])
+            )
+
+        def turn(b, u):
+            words = k_grp[b][:].bitcast(F32).rearrange("p (t s u) -> p t s u", t=LANES, u=2)
+            turned[b, u] = psum4.tile([P, LANES, P], F32, tag="turned", name=f"turned{b}{u}")
+            for t in range(LANES):
+                nc.tensor.transpose(turned[b, u][:, t, :], words[:, t, :, u], ident[:])
+
+        def cast_queries():
+            nc.scalar.activation(
+                q_grp[:].rearrange("p (b q j) -> p b q j", b=B, j=LANES), q_raw[:].rearrange("p b j q -> p b q j"), COPY
+            )
+
+        def score(b):
+            cols = slice(b * NQ, (b + 1) * NQ)
+            if b == 0:
+                nc.vector.quantize_mx(out=q_codes[:].bitcast(FP8X4), scales=q_scales[:], in_=q_grp[:])
+            k_codes = ring3.tile([P, N], U32, align_bytes=64, name="k_codes")
+            k_scales = ring3.tile([P, N], U8, align_bytes=64, name="k_scales")
+            nc.vector.quantize_mx(out=k_codes[:].bitcast(FP8X4), scales=k_scales[:], in_=k_grp[b][:])
+            scores[b] = psum2.tile([P, LANES, NQ], F32, name="scores")
+            for t in range(LANES):
+                nc.tensor.matmul_mx(
+                    out=scores[b][:, t, :],
+                    lhsT=k_codes[:, t * P : (t + 1) * P].bitcast(FP8X4),
+                    lhsT_scale=k_scales[:, t * P : (t + 1) * P],
+                    rhs=q_codes[:, cols].bitcast(FP8X4),
+                    rhs_scale=q_scales[:, cols],
+                    start=True,
+                    stop=True,
+                )
+
+        def values(b):
+            v_grp = ring3.tile([P, D * LANES], BF16, align_bytes=64, name="v_grp")
+            half = D * LANES // 2
+            for u in range(2):
+                nc.scalar.copy(
+                    v_grp[:, u * half : (u + 1) * half].rearrange("s (e m t) -> s e m t", e=2, t=LANES),
+                    turned[b, u][:].bitcast(BF16).rearrange("s t (m e) -> s e m t", e=2),
+                )
+            v_codes[b] = ring3.tile([P, D], U32, align_bytes=64, name="v_codes")
+            v_scales[b] = ring3.tile([P, D], U8, align_bytes=64, name="v_scales")
+            nc.vector.quantize_mx(out=v_codes[b][:].bitcast(FP8X4), scales=v_scales[b][:], in_=v_grp[:])
+
+        def weights(b):
+            bias, scale = tokens[b][:, 0, :], tokens[b][:, 1, :]
+            p = ring2.tile([P, LANES, NQ], F32, name="p")
+            for t in range(LANES):
+                nc.scalar.activation(
+                    p[:, t, :],
+                    scores[b][:, t, :],
+                    SIGMOID,
+                    bias=bias[:, t : t + 1],
+                    scale=scale[:, t : t + 1],
+                )
+            w_grp = ring2.tile([P, NQ, LANES], BF16, align_bytes=64, name="w_grp")
+            nc.vector.tensor_tensor(
+                w_grp[:],
+                p[:].rearrange("s t q -> s q t"),
+                scale.unsqueeze(1).to_broadcast([P, NQ, LANES]),
+                MULT,
+            )
+            w_codes = ring2.tile([P, NQ], U32, align_bytes=64, name="w_codes")
+            w_scales = ring2.tile([P, NQ], U8, align_bytes=64, name="w_scales")
+            nc.vector.quantize_mx(
+                out=w_codes[:].bitcast(FP8X4), scales=w_scales[:], in_=w_grp[:].rearrange("s q t -> s (q t)")
+            )
+            acc[b] = psum2.tile([P, D], F32, tag="acc", name=f"acc{b}")
+            nc.tensor.matmul_mx(
+                out=acc[b][:],
+                lhsT=w_codes[:].bitcast(FP8X4),
+                lhsT_scale=w_scales[:],
+                rhs=v_codes[b][:].bitcast(FP8X4),
+                rhs_scale=v_scales[b][:],
+                start=True,
+                stop=True,
+            )
+
+        def finish(b):
+            y = ring2.tile([P, D], F32, name="y")
+            nc.vector.scalar_tensor_tensor(
+                out=y[:].rearrange("q (m j) -> q m j", j=LANES),
+                in0=acc[b][:].rearrange("q (j m) -> q m j", j=LANES),
+                scalar=1.0 / 16.0,
+                in1=chans[:].rearrange("q (m j) -> q m j", j=LANES),
+                op0=MULT,
+                op1=MULT,
+            )
+            nc.sync.dma_start(out[b], y[:])
+
+        gather_tokens(0, 1)
+        bank0 = psum2.tile([P, 512], F32, tag="acc", name="bank0")
+        turn_tokens(0, 1, bank0)
+        cast(0, 0, pieces=2)
+        cast(0, 1)
+        gather(0, 0)
+        turn(0, 0)
+        gather(0, 1)
+        turn(0, 1)
+        gather_tokens(1, B)
+        cast_queries()
+        score(0)
+        for b in range(1, B):
+            cast(b, 0)
+            cast(b, 1)
+            gather(b, 0)
+            gather(b, 1)
+            if b >= 2:
+                weights(b - 2)
+            values(b - 1)
+            turn(b, 0)
+            turn(b, 1)
+            if b == 1:
+                bank1 = psum4.tile([P, 512], F32, tag="turned", name="bank1")
+                turn_tokens(1, B, bank1)
+            score(b)
+            if b >= 2:
+                finish(b - 2)
+        weights(B - 2)
+        values(B - 1)
+        finish(B - 2)
+        weights(B - 1)
+        finish(B - 1)

@@ -7,6 +7,7 @@ B, N, T, D, NQ = 4, 512, 4096, 512, 128
 P = 128
 SEG = T // B
 LANES = 4
+RUN = 8
 LIST_COLUMNS = N // 16
 
 FLOPS = B * 2 * (2 * N * D * NQ)
@@ -17,6 +18,7 @@ CAST_ON_VECTOR = ((1, 1), (3, 1))
 F32 = mybir.dt.float32
 BF16 = mybir.dt.bfloat16
 U32 = mybir.dt.uint32
+I32 = mybir.dt.int32
 U16 = mybir.dt.uint16
 U8 = mybir.dt.uint8
 FP8X4 = mybir.dt.float8_e4m3fn_x4
@@ -45,13 +47,12 @@ def tile_attend_x_mla_sigmoid_seg_kernel(tc, qT, cT, ts, kb, ch, offs, out):
         windows = {}
         for name in ("ts", "kb"):
             windows[name] = keep.tile([P, T], F32, name="window_" + name)
-        raw_first = keep.tile([P, 2, 2, SEG], F32, name="raw_first")
-        raw_later = keep.tile([P, 2 * (B - 1), 2, SEG], F32, name="raw_later")
+        raws = {(b, u): keep.tile([P, 2, SEG], F32, name=f"raw{b}{u}") for b in range(B) for u in range(2)}
         q_raw = keep.tile([P, B, LANES, NQ], F32, name="q_raw")
         chans = keep.tile([P, D], F32, name="chans")
 
         def raw(b, u):
-            return raw_first[:, u] if b == 0 else raw_later[:, 2 * (b - 1) + u]
+            return raws[b, u][:]
 
         nc.vector.memset(windows["kb"][:, 0:SEG], 0.0)
         nc.gpsimd.memset(windows["ts"][:, 0:SEG], 0.0)
@@ -96,19 +97,22 @@ def tile_attend_x_mla_sigmoid_seg_kernel(tc, qT, cT, ts, kb, ch, offs, out):
         pool = [keep.tile([P, 2 * T], BF16, name=f"pool{u}") for u in range(2)]
         k_grp, tokens, scores, turned, acc = {}, {}, {}, {}, {}
         v_codes, v_scales = {}, {}
-        token_rows = {}
+        token_rows, picked = {}, {}
 
         def gather_tokens(b0, b1):
             for name in ("kb", "ts"):
                 row = keep.tile([P, (b1 - b0) * N], F32, name=f"row_{name}{b0}")
-                window = windows[name][:, 0 : b1 * SEG]
-                nc.vector.tensor_copy(row[:], window.indirect(lists[:, b0 * LIST_COLUMNS : b1 * LIST_COLUMNS]))
+                window = windows[name][:].bitcast(U32)[:, 0 : b1 * SEG]
+                nc.vector.tensor_copy(
+                    row[:].bitcast(U32).rearrange("p (b t g r) -> p b g t r", t=LANES, r=RUN, b=b1 - b0),
+                    window.indirect(lists[:, b0 * LIST_COLUMNS : b1 * LIST_COLUMNS]),
+                )
                 token_rows[name, b0] = row
 
         def turn_tokens(b0, b1, bank):
             n = b1 - b0
             for i, name in enumerate(("kb", "ts")):
-                view = token_rows[name, b0][:].rearrange("p (b s t) -> p b t s", t=LANES, b=n)
+                view = token_rows[name, b0][:].rearrange("p (b t s) -> p b t s", t=LANES, b=n)
                 for b in range(n):
                     for t in range(LANES):
                         c0 = 2 * ((i * n + b) * LANES + t)
@@ -134,18 +138,25 @@ def tile_attend_x_mla_sigmoid_seg_kernel(tc, qT, cT, ts, kb, ch, offs, out):
 
         def gather(b, u):
             if u == 0:
-                k_grp[b] = ring3.tile([P, N * LANES], BF16, align_bytes=64, name="k_grp")
-            words = k_grp[b][:].bitcast(U32).rearrange("p (t s u) -> p s t u", t=LANES, u=2)
+                picked[b] = ring3.tile([P, 2 * N], U32, name="picked")
             window = pool[u][:].bitcast(U32)[:, 0 : (b + 1) * SEG]
             nc.vector.tensor_copy(
-                words[:, :, :, u], window.indirect(lists[:, b * LIST_COLUMNS : (b + 1) * LIST_COLUMNS])
+                picked[b][:, u * N : (u + 1) * N].rearrange("p (t g r) -> p g t r", t=LANES, r=RUN),
+                window.indirect(lists[:, b * LIST_COLUMNS : (b + 1) * LIST_COLUMNS]),
+            )
+
+        def weave(b):
+            k_grp[b] = ring3.tile([P, N * LANES], BF16, align_bytes=64, name="k_grp")
+            nc.vector.tensor_copy(
+                k_grp[b][:].bitcast(I32).rearrange("p (c u) -> p c u", u=2),
+                picked[b][:].bitcast(I32).rearrange("p (u c) -> p c u", u=2),
             )
 
         def turn(b, u):
-            words = k_grp[b][:].bitcast(F32).rearrange("p (t s u) -> p t s u", t=LANES, u=2)
+            words = picked[b][:].bitcast(F32).rearrange("p (u t s) -> p u t s", t=LANES, u=2)
             turned[b, u] = psum4.tile([P, LANES, P], F32, tag="turned", name=f"turned{b}{u}")
             for t in range(LANES):
-                nc.tensor.transpose(turned[b, u][:, t, :], words[:, t, :, u], ident[:])
+                nc.tensor.transpose(turned[b, u][:, t, :], words[:, u, t, :], ident[:])
 
         def cast_queries():
             nc.scalar.activation(
@@ -238,6 +249,7 @@ def tile_attend_x_mla_sigmoid_seg_kernel(tc, qT, cT, ts, kb, ch, offs, out):
         turn(0, 0)
         gather(0, 1)
         turn(0, 1)
+        weave(0)
         gather_tokens(1, B)
         cast_queries()
         score(0)
@@ -246,6 +258,7 @@ def tile_attend_x_mla_sigmoid_seg_kernel(tc, qT, cT, ts, kb, ch, offs, out):
             cast(b, 1)
             gather(b, 0)
             gather(b, 1)
+            weave(b)
             if b >= 2:
                 weights(b - 2)
             values(b - 1)

@@ -13,7 +13,8 @@ LIST_COLUMNS = N // 16
 FLOPS = B * 2 * (2 * N * D * NQ)
 BYTES = 4 * (B * D * NQ + D * T + 2 * T + D + B * NQ * D) + 2 * P * (B * N // 16)
 
-CAST_ON_VECTOR = ((1, 1), (3, 1))
+CAST_ON_VECTOR = ()
+HALVES = ((0, 0), (0, 1),)
 
 F32 = mybir.dt.float32
 BF16 = mybir.dt.bfloat16
@@ -22,6 +23,7 @@ I32 = mybir.dt.int32
 U16 = mybir.dt.uint16
 U8 = mybir.dt.uint8
 FP8X4 = mybir.dt.float8_e4m3fn_x4
+ADD = mybir.AluOpType.add
 MULT = mybir.AluOpType.mult
 COPY = mybir.ActivationFunctionType.Copy
 SIGMOID = mybir.ActivationFunctionType.Sigmoid
@@ -31,6 +33,7 @@ def tile_attend_x_mla_sigmoid_seg_kernel(tc, qT, cT, ts, kb, ch, offs, out):
     nc = tc.nc
     with ExitStack() as ctx:
         keep = ctx.enter_context(tc.tile_pool(name="keep", bufs=1))
+        stage = ctx.enter_context(tc.tile_pool(name="stage", bufs=1))
         ring3 = ctx.enter_context(tc.tile_pool(name="ring3", bufs=3))
         ring2 = ctx.enter_context(tc.tile_pool(name="ring2", bufs=2))
         psum2 = ctx.enter_context(tc.psum_pool(name="psum2", bufs=2))
@@ -40,24 +43,22 @@ def tile_attend_x_mla_sigmoid_seg_kernel(tc, qT, cT, ts, kb, ch, offs, out):
         nc.sync.dma_start(lists[:], offs)
 
         warm = keep.tile([P, 1], F32, name="warm")
-        nc.vector.memset(warm[:], 0.0)
+        nc.gpsimd.memset(warm[:], 0.0)
         warm_out = keep.tile([P, 1], F32, name="warm_out")
         nc.scalar.activation(warm_out[:], warm[:], SIGMOID)
 
-        windows = {}
-        for name in ("ts", "kb"):
-            windows[name] = keep.tile([P, T], F32, name="window_" + name)
-        raws = {(b, u): keep.tile([P, 2, SEG], F32, name=f"raw{b}{u}") for b in range(B) for u in range(2)}
+        windows = {name: keep.tile([P, T], F32, name="window_" + name) for name in ("kb", "ts")}
+        raw = {
+            (b, u): stage.tile([P, 2, SEG], F32, align_bytes=64, tag=f"raw{b}{u}", name=f"raw{b}{u}")
+            for b in range(B)
+            for u in range(2)
+        }
         q_raw = keep.tile([P, B, LANES, NQ], F32, name="q_raw")
         chans = keep.tile([P, D], F32, name="chans")
 
-        def raw(b, u):
-            return raws[b, u][:]
-
-        nc.vector.memset(windows["kb"][:, 0:SEG], 0.0)
-        nc.gpsimd.memset(windows["ts"][:, 0:SEG], 0.0)
-        nc.vector.memset(windows["kb"][:, SEG:T], 0.0)
-        nc.gpsimd.memset(windows["ts"][:, SEG:T], 0.0)
+        for c0, c1 in ((0, SEG + 1), (SEG + 1, T)):
+            nc.vector.memset(windows["kb"][:, c0:c1], 0.0)
+            nc.gpsimd.memset(windows["ts"][:, c0:c1], 0.0)
         ident = keep.tile([P, P], F32, name="ident")
         make_identity(nc, ident[:])
 
@@ -67,23 +68,27 @@ def tile_attend_x_mla_sigmoid_seg_kernel(tc, qT, cT, ts, kb, ch, offs, out):
 
         cT_view = cT.rearrange("(p j) w -> p j w", j=LANES)
 
-        def load_pool(b, u, pieces=1):
+        def load_pool(b, u):
+            pieces = 2 if (b, u) in HALVES else 1
             w = SEG // pieces
             for i in range(pieces):
                 nc.sync.dma_start(
-                    raw(b, u)[:, :, i * w : (i + 1) * w],
+                    raw[b, u][:, :, i * w : (i + 1) * w],
                     cT_view[:, 2 * u : 2 * u + 2, b * SEG + i * w : b * SEG + (i + 1) * w],
                 )
 
+        def load_queries():
+            nc.sync.dma_start(
+                q_raw[:].rearrange("p b j q -> p b (j q)"),
+                qT.rearrange("b (p j) q -> p b (j q)", j=LANES),
+            )
+
+        load_pool(0, 0)
         load_rows(0, SEG)
-        load_pool(0, 0, pieces=2)
         load_pool(0, 1)
         load_rows(SEG, T)
         load_pool(1, 0)
-        nc.sync.dma_start(
-            q_raw[:].rearrange("p b j q -> p b (j q)"),
-            qT.rearrange("b (p j) q -> p b (j q)", j=LANES),
-        )
+        load_queries()
         load_pool(1, 1)
         for b in range(2, B):
             load_pool(b, 0)
@@ -95,42 +100,44 @@ def tile_attend_x_mla_sigmoid_seg_kernel(tc, qT, cT, ts, kb, ch, offs, out):
         q_scales = keep.tile([P, B * NQ], U8, align_bytes=64, name="q_scales")
 
         pool = [keep.tile([P, 2 * T], BF16, name=f"pool{u}") for u in range(2)]
-        k_grp, tokens, scores, turned, acc = {}, {}, {}, {}, {}
-        v_codes, v_scales = {}, {}
-        token_rows, picked = {}, {}
+        picked, k_grp, tokens, scores, turned, acc = {}, {}, {}, {}, {}, {}
+        v_codes, v_scales, w_grp = {}, {}, {}
 
         def gather_tokens(b0, b1):
-            for name in ("kb", "ts"):
-                row = keep.tile([P, (b1 - b0) * N], F32, name=f"row_{name}{b0}")
-                window = windows[name][:].bitcast(U32)[:, 0 : b1 * SEG]
-                nc.vector.tensor_copy(
-                    row[:].bitcast(U32).rearrange("p (b t g r) -> p b g t r", t=LANES, r=RUN, b=b1 - b0),
-                    window.indirect(lists[:, b0 * LIST_COLUMNS : b1 * LIST_COLUMNS]),
-                )
-                token_rows[name, b0] = row
-
-        def turn_tokens(b0, b1, bank):
             n = b1 - b0
+            if b0 == 0:
+                rows = keep.tile([P, 2, n * N], F32, name="rows_first")
+            else:
+                rows = stage.tile([P, 2, n * N], F32, align_bytes=64, tag="raw00", name="rows_later")
             for i, name in enumerate(("kb", "ts")):
-                view = token_rows[name, b0][:].rearrange("p (b t s) -> p b t s", t=LANES, b=n)
-                for b in range(n):
-                    for t in range(LANES):
-                        c0 = 2 * ((i * n + b) * LANES + t)
-                        nc.tensor.transpose(bank[:, c0 : c0 + P], view[:, b, t, :], ident[:])
-            columns = keep.tile([P, 2, n, LANES], F32, name=f"columns{b0}")
+                nc.vector.tensor_copy(
+                    rows[:, i].bitcast(U32).rearrange("p (b t g r) -> p b g t r", b=n, t=LANES, r=RUN),
+                    windows[name][:].bitcast(U32)[:, 0 : b1 * SEG].indirect(
+                        lists[:, b0 * LIST_COLUMNS : b1 * LIST_COLUMNS]
+                    ),
+                )
+            bank = psum2.tile([P, 512], F32, tag="acc", name=f"bank{b0}")
+            blocks = rows[:].rearrange("p i (c s) -> p (i c) s", s=P)
+            for c in range(2 * n * LANES):
+                nc.tensor.transpose(bank[:, 2 * c : 2 * c + P], blocks[:, c, :], ident[:])
+            if b0 == 0:
+                columns = keep.tile([P, 2, n, LANES], F32, name="columns_first")
+            else:
+                columns = stage.tile([P, 2, n, LANES], F32, align_bytes=64, tag="raw11", name="columns_later")
             nc.vector.tensor_copy(
                 columns[:].rearrange("s i b t -> s (i b t)"),
-                bank[:, 0 : 4 * LANES * n].rearrange("s (i z) -> s i z", z=2)[:, :, 0],
+                bank[:, 0 : 4 * LANES * n].rearrange("s (c z) -> s c z", z=2)[:, :, 0],
             )
             for b in range(n):
                 tokens[b0 + b] = columns[:, :, b, :]
 
-        def cast(b, u, pieces=1):
+        def cast(b, u):
+            pieces = 2 if (b, u) in HALVES else 1
             w = SEG // pieces
             for i in range(pieces):
                 c0 = 2 * (b * SEG + i * w)
                 pair_out = pool[u][:, c0 : c0 + 2 * w].rearrange("p (w e) -> p w e", e=2)
-                pair_in = raw(b, u)[:, :, i * w : (i + 1) * w].rearrange("p e w -> p w e")
+                pair_in = raw[b, u][:, :, i * w : (i + 1) * w].rearrange("p e w -> p w e")
                 if (b, u) in CAST_ON_VECTOR:
                     nc.vector.tensor_copy(pair_out, pair_in)
                 else:
@@ -159,14 +166,16 @@ def tile_attend_x_mla_sigmoid_seg_kernel(tc, qT, cT, ts, kb, ch, offs, out):
                 nc.tensor.transpose(turned[b, u][:, t, :], words[:, u, t, :], ident[:])
 
         def cast_queries():
-            nc.scalar.activation(
-                q_grp[:].rearrange("p (b q j) -> p b q j", b=B, j=LANES), q_raw[:].rearrange("p b j q -> p b q j"), COPY
+            nc.scalar.copy(
+                q_grp[:].rearrange("p (b c i j) -> p b c j i", b=B, i=4, j=LANES),
+                q_raw[:].rearrange("p b j (c i) -> p b c j i", i=4),
             )
+
+        def quantize_queries():
+            nc.vector.quantize_mx(out=q_codes[:].bitcast(FP8X4), scales=q_scales[:], in_=q_grp[:])
 
         def score(b):
             cols = slice(b * NQ, (b + 1) * NQ)
-            if b == 0:
-                nc.vector.quantize_mx(out=q_codes[:].bitcast(FP8X4), scales=q_scales[:], in_=q_grp[:])
             k_codes = ring3.tile([P, N], U32, align_bytes=64, name="k_codes")
             k_scales = ring3.tile([P, N], U8, align_bytes=64, name="k_scales")
             nc.vector.quantize_mx(out=k_codes[:].bitcast(FP8X4), scales=k_scales[:], in_=k_grp[b][:])
@@ -182,21 +191,30 @@ def tile_attend_x_mla_sigmoid_seg_kernel(tc, qT, cT, ts, kb, ch, offs, out):
                     stop=True,
                 )
 
+        v_grp = {}
+
+        def values_out(b, u):
+            if u == 0:
+                if b + 2 < B:
+                    v_grp[b] = stage.tile([P, D * LANES], BF16, align_bytes=64, tag=f"raw{b + 2}0", name=f"v_grp{b}")
+                else:
+                    v_grp[b] = ring3.tile([P, D * LANES], BF16, align_bytes=64, name="v_grp")
+            nc.scalar.copy(
+                v_grp[b][:].rearrange("s (m u e t) -> s u m e t", u=2, e=2, t=LANES)[:, u],
+                turned[b, u][:].bitcast(BF16).rearrange("s t (m e) -> s m e t", e=2),
+            )
+
         def values(b):
-            v_grp = ring3.tile([P, D * LANES], BF16, align_bytes=64, name="v_grp")
-            half = D * LANES // 2
-            for u in range(2):
-                nc.scalar.copy(
-                    v_grp[:, u * half : (u + 1) * half].rearrange("s (e m t) -> s e m t", e=2, t=LANES),
-                    turned[b, u][:].bitcast(BF16).rearrange("s t (m e) -> s e m t", e=2),
-                )
             v_codes[b] = ring3.tile([P, D], U32, align_bytes=64, name="v_codes")
             v_scales[b] = ring3.tile([P, D], U8, align_bytes=64, name="v_scales")
-            nc.vector.quantize_mx(out=v_codes[b][:].bitcast(FP8X4), scales=v_scales[b][:], in_=v_grp[:])
+            nc.vector.quantize_mx(out=v_codes[b][:].bitcast(FP8X4), scales=v_scales[b][:], in_=v_grp[b][:])
 
-        def weights(b):
+        def weigh(b):
             bias, scale = tokens[b][:, 0, :], tokens[b][:, 1, :]
-            p = ring2.tile([P, LANES, NQ], F32, name="p")
+            if b + 2 < B:
+                p = stage.tile([P, LANES, NQ], F32, align_bytes=64, tag=f"raw{b + 2}1", name=f"p{b}")
+            else:
+                p = ring2.tile([P, LANES, NQ], F32, name="p")
             for t in range(LANES):
                 nc.scalar.activation(
                     p[:, t, :],
@@ -205,17 +223,19 @@ def tile_attend_x_mla_sigmoid_seg_kernel(tc, qT, cT, ts, kb, ch, offs, out):
                     bias=bias[:, t : t + 1],
                     scale=scale[:, t : t + 1],
                 )
-            w_grp = ring2.tile([P, NQ, LANES], BF16, align_bytes=64, name="w_grp")
+            w_grp[b] = ring2.tile([P, NQ, LANES], BF16, align_bytes=64, name="w_grp")
             nc.vector.tensor_tensor(
-                w_grp[:],
-                p[:].rearrange("s t q -> s q t"),
-                scale.unsqueeze(1).to_broadcast([P, NQ, LANES]),
+                w_grp[b][:].rearrange("s (c i) t -> s c t i", i=4),
+                p[:].rearrange("s t (c i) -> s c t i", i=4),
+                scale.unsqueeze(1).unsqueeze(3).to_broadcast([P, NQ // 4, LANES, 4]),
                 MULT,
             )
+
+        def product(b):
             w_codes = ring2.tile([P, NQ], U32, align_bytes=64, name="w_codes")
             w_scales = ring2.tile([P, NQ], U8, align_bytes=64, name="w_scales")
             nc.vector.quantize_mx(
-                out=w_codes[:].bitcast(FP8X4), scales=w_scales[:], in_=w_grp[:].rearrange("s q t -> s (q t)")
+                out=w_codes[:].bitcast(FP8X4), scales=w_scales[:], in_=w_grp[b][:].rearrange("s q t -> s (q t)")
             )
             acc[b] = psum2.tile([P, D], F32, tag="acc", name=f"acc{b}")
             nc.tensor.matmul_mx(
@@ -231,47 +251,47 @@ def tile_attend_x_mla_sigmoid_seg_kernel(tc, qT, cT, ts, kb, ch, offs, out):
         def finish(b):
             y = ring2.tile([P, D], F32, name="y")
             nc.vector.scalar_tensor_tensor(
-                out=y[:].rearrange("q (m j) -> q m j", j=LANES),
-                in0=acc[b][:].rearrange("q (j m) -> q m j", j=LANES),
+                out=y[:],
+                in0=acc[b][:],
                 scalar=1.0 / 16.0,
-                in1=chans[:].rearrange("q (m j) -> q m j", j=LANES),
+                in1=chans[:],
                 op0=MULT,
                 op1=MULT,
             )
             nc.sync.dma_start(out[b], y[:])
 
-        gather_tokens(0, 1)
-        bank0 = psum2.tile([P, 512], F32, tag="acc", name="bank0")
-        turn_tokens(0, 1, bank0)
-        cast(0, 0, pieces=2)
-        cast(0, 1)
-        gather(0, 0)
-        turn(0, 0)
-        gather(0, 1)
-        turn(0, 1)
-        weave(0)
-        gather_tokens(1, B)
-        cast_queries()
-        score(0)
-        for b in range(1, B):
-            cast(b, 0)
-            cast(b, 1)
+        def front(b):
             gather(b, 0)
-            gather(b, 1)
-            weave(b)
-            if b >= 2:
-                weights(b - 2)
-            values(b - 1)
             turn(b, 0)
+            if b == 0:
+                gather_tokens(1, B)
+            gather(b, 1)
             turn(b, 1)
-            if b == 1:
-                bank1 = psum4.tile([P, 512], F32, tag="turned", name="bank1")
-                turn_tokens(1, B, bank1)
-            score(b)
-            if b >= 2:
-                finish(b - 2)
-        weights(B - 2)
-        values(B - 1)
-        finish(B - 2)
-        weights(B - 1)
-        finish(B - 1)
+            weave(b)
+
+        gather_tokens(0, 1)
+        cast(0, 0)
+        cast(0, 1)
+        cast(1, 0)
+        cast_queries()
+        cast(1, 1)
+        cast(2, 0)
+        front(0)
+        quantize_queries()
+        score(0)
+        front(1)
+        score(1)
+        for b in range(B):
+            values_out(b, 0)
+            values_out(b, 1)
+            if b + 2 < B:
+                cast(b + 2, 1)
+                front(b + 2)
+            weigh(b)
+            if b + 3 < B:
+                cast(b + 3, 0)
+            if b + 2 < B:
+                score(b + 2)
+            values(b)
+            product(b)
+            finish(b)

@@ -14,6 +14,8 @@ FLOPS = B * 2 * (2 * N * D * NQ)
 BYTES = 4 * (B * D * NQ + D * T + 2 * T + D + B * NQ * D) + 2 * P * (B * N // 16)
 
 CAST_ON_VECTOR = ()
+STAGE_BYTES = 2 * SEG * 4
+LATE = {2: ((3, 1), 8128), 3: ((0, 1), 0)}
 HALVES = ((0, 0), (0, 1),)
 
 F32 = mybir.dt.float32
@@ -48,12 +50,16 @@ def tile_attend_x_mla_sigmoid_seg_kernel(tc, qT, cT, ts, kb, ch, offs, out):
         nc.scalar.activation(warm_out[:], warm[:], SIGMOID)
 
         windows = {name: keep.tile([P, T], F32, name="window_" + name) for name in ("kb", "ts")}
+        def staged(place, offset, shape, dtype, name):
+            index = 2 * B if place == "q" else 2 * place[0] + place[1]
+            return stage.tile(shape, dtype, align_bytes=64, offset=index * STAGE_BYTES + offset, name=name)
+
         raw = {
-            (b, u): stage.tile([P, 2, SEG], F32, align_bytes=64, tag=f"raw{b}{u}", name=f"raw{b}{u}")
+            (b, u): staged((b, u), 0, [P, 2, SEG], F32, f"raw{b}{u}")
             for b in range(B)
             for u in range(2)
         }
-        q_raw = keep.tile([P, B, LANES, NQ], F32, name="q_raw")
+        q_raw = staged("q", 0, [P, B, LANES, NQ], F32, "q_raw")
         chans = keep.tile([P, D], F32, name="chans")
 
         for c0, c1 in ((0, SEG + 1), (SEG + 1, T)):
@@ -88,8 +94,8 @@ def tile_attend_x_mla_sigmoid_seg_kernel(tc, qT, cT, ts, kb, ch, offs, out):
         load_pool(0, 1)
         load_rows(SEG, T)
         load_pool(1, 0)
-        load_queries()
         load_pool(1, 1)
+        load_queries()
         for b in range(2, B):
             load_pool(b, 0)
             load_pool(b, 1)
@@ -103,27 +109,33 @@ def tile_attend_x_mla_sigmoid_seg_kernel(tc, qT, cT, ts, kb, ch, offs, out):
         picked, k_grp, tokens, scores, turned, acc = {}, {}, {}, {}, {}, {}
         v_codes, v_scales, w_grp = {}, {}, {}
 
-        def gather_tokens(b0, b1):
+        rows = {}
+
+        def gather_tokens(b0, b1, names):
             n = b1 - b0
-            if b0 == 0:
-                rows = keep.tile([P, 2, n * N], F32, name="rows_first")
-            else:
-                rows = stage.tile([P, 2, n * N], F32, align_bytes=64, tag="raw00", name="rows_later")
-            for i, name in enumerate(("kb", "ts")):
+            for name in names:
+                if b0 == 0:
+                    rows[name, b0] = keep.tile([P, n * N], F32, name=f"row_first_{name}")
+                else:
+                    rows[name, b0] = staged((0, ("kb", "ts").index(name)), 0, [P, n * N], F32, f"row_later_{name}")
                 nc.vector.tensor_copy(
-                    rows[:, i].bitcast(U32).rearrange("p (b t g r) -> p b g t r", b=n, t=LANES, r=RUN),
+                    rows[name, b0][:].bitcast(U32).rearrange("p (b t g r) -> p b g t r", b=n, t=LANES, r=RUN),
                     windows[name][:].bitcast(U32)[:, 0 : b1 * SEG].indirect(
                         lists[:, b0 * LIST_COLUMNS : b1 * LIST_COLUMNS]
                     ),
                 )
+
+        def turn_tokens(b0, b1):
+            n = b1 - b0
             bank = psum2.tile([P, 512], F32, tag="acc", name=f"bank{b0}")
-            blocks = rows[:].rearrange("p i (c s) -> p (i c) s", s=P)
-            for c in range(2 * n * LANES):
-                nc.tensor.transpose(bank[:, 2 * c : 2 * c + P], blocks[:, c, :], ident[:])
+            for i, name in enumerate(("kb", "ts")):
+                for c in range(n * LANES):
+                    c0 = 2 * (i * n * LANES + c)
+                    nc.tensor.transpose(bank[:, c0 : c0 + P], rows[name, b0][:, c * P : (c + 1) * P], ident[:])
             if b0 == 0:
                 columns = keep.tile([P, 2, n, LANES], F32, name="columns_first")
             else:
-                columns = stage.tile([P, 2, n, LANES], F32, align_bytes=64, tag="raw11", name="columns_later")
+                columns = staged((1, 1), 6144, [P, 2, n, LANES], F32, "columns_later")
             nc.vector.tensor_copy(
                 columns[:].rearrange("s i b t -> s (i b t)"),
                 bank[:, 0 : 4 * LANES * n].rearrange("s (c z) -> s c z", z=2)[:, :, 0],
@@ -145,7 +157,7 @@ def tile_attend_x_mla_sigmoid_seg_kernel(tc, qT, cT, ts, kb, ch, offs, out):
 
         def gather(b, u):
             if u == 0:
-                picked[b] = ring3.tile([P, 2 * N], U32, name="picked")
+                picked[b] = keep.tile([P, 2 * N], U32, name=f"picked{b}")
             window = pool[u][:].bitcast(U32)[:, 0 : (b + 1) * SEG]
             nc.vector.tensor_copy(
                 picked[b][:, u * N : (u + 1) * N].rearrange("p (t g r) -> p g t r", t=LANES, r=RUN),
@@ -154,7 +166,8 @@ def tile_attend_x_mla_sigmoid_seg_kernel(tc, qT, cT, ts, kb, ch, offs, out):
 
         def weave(b):
             k_grp[b] = ring3.tile([P, N * LANES], BF16, align_bytes=64, name="k_grp")
-            nc.vector.tensor_copy(
+            engine = nc.vector if b == B - 1 else nc.gpsimd
+            engine.tensor_copy(
                 k_grp[b][:].bitcast(I32).rearrange("p (c u) -> p c u", u=2),
                 picked[b][:].bitcast(I32).rearrange("p (u c) -> p c u", u=2),
             )
@@ -166,19 +179,34 @@ def tile_attend_x_mla_sigmoid_seg_kernel(tc, qT, cT, ts, kb, ch, offs, out):
                 nc.tensor.transpose(turned[b, u][:, t, :], words[:, u, t, :], ident[:])
 
         def cast_queries():
-            nc.scalar.copy(
-                q_grp[:].rearrange("p (b c i j) -> p b c j i", b=B, i=4, j=LANES),
-                q_raw[:].rearrange("p b j (c i) -> p b c j i", i=4),
+            nc.gpsimd.tensor_scalar(
+                q_grp[:].rearrange("p (b q j) -> p b q j", b=B, j=LANES),
+                q_raw[:].rearrange("p b j q -> p b q j"),
+                1.0,
+                0.0,
+                MULT,
+                ADD,
             )
 
         def quantize_queries():
             nc.vector.quantize_mx(out=q_codes[:].bitcast(FP8X4), scales=q_scales[:], in_=q_grp[:])
 
-        def score(b):
-            cols = slice(b * NQ, (b + 1) * NQ)
-            k_codes = ring3.tile([P, N], U32, align_bytes=64, name="k_codes")
+        keys = {}
+
+        def quantize_keys(b):
+            if b == 0:
+                k_codes = staged((1, 1), 4096, [P, N], U32, "k_codes0")
+            elif b + 1 < B:
+                k_codes = staged((b + 1, 0), 4096, [P, N], U32, f"k_codes{b}")
+            else:
+                k_codes = keep.tile([P, N], U32, align_bytes=64, name="k_codes_last")
             k_scales = ring3.tile([P, N], U8, align_bytes=64, name="k_scales")
             nc.vector.quantize_mx(out=k_codes[:].bitcast(FP8X4), scales=k_scales[:], in_=k_grp[b][:])
+            keys[b] = k_codes, k_scales
+
+        def score(b):
+            cols = slice(b * NQ, (b + 1) * NQ)
+            k_codes, k_scales = keys[b]
             scores[b] = psum2.tile([P, LANES, NQ], F32, name="scores")
             for t in range(LANES):
                 nc.tensor.matmul_mx(
@@ -196,9 +224,9 @@ def tile_attend_x_mla_sigmoid_seg_kernel(tc, qT, cT, ts, kb, ch, offs, out):
         def values_out(b, u):
             if u == 0:
                 if b + 2 < B:
-                    v_grp[b] = stage.tile([P, D * LANES], BF16, align_bytes=64, tag=f"raw{b + 2}0", name=f"v_grp{b}")
+                    v_grp[b] = staged((1 + 2 * b, 1), 0, [P, D * LANES], BF16, f"v_grp{b}")
                 else:
-                    v_grp[b] = ring3.tile([P, D * LANES], BF16, align_bytes=64, name="v_grp")
+                    v_grp[b] = staged(*LATE[b], [P, D * LANES], BF16, f"v_grp{b}")
             nc.scalar.copy(
                 v_grp[b][:].rearrange("s (m u e t) -> s u m e t", u=2, e=2, t=LANES)[:, u],
                 turned[b, u][:].bitcast(BF16).rearrange("s t (m e) -> s m e t", e=2),
@@ -212,7 +240,7 @@ def tile_attend_x_mla_sigmoid_seg_kernel(tc, qT, cT, ts, kb, ch, offs, out):
         def weigh(b):
             bias, scale = tokens[b][:, 0, :], tokens[b][:, 1, :]
             if b + 2 < B:
-                p = stage.tile([P, LANES, NQ], F32, align_bytes=64, tag=f"raw{b + 2}1", name=f"p{b}")
+                p = staged((3, b), 6144 - 1536 * b, [P, LANES, NQ], F32, f"p{b}")
             else:
                 p = ring2.tile([P, LANES, NQ], F32, name="p")
             for t in range(LANES):
@@ -232,7 +260,10 @@ def tile_attend_x_mla_sigmoid_seg_kernel(tc, qT, cT, ts, kb, ch, offs, out):
             )
 
         def product(b):
-            w_codes = ring2.tile([P, NQ], U32, align_bytes=64, name="w_codes")
+            if b == 0:
+                w_codes = staged((3, 1), 4096, [P, NQ], U32, f"w_codes{b}")
+            else:
+                w_codes = ring2.tile([P, NQ], U32, align_bytes=64, name="w_codes")
             w_scales = ring2.tile([P, NQ], U8, align_bytes=64, name="w_scales")
             nc.vector.quantize_mx(
                 out=w_codes[:].bitcast(FP8X4), scales=w_scales[:], in_=w_grp[b][:].rearrange("s q t -> s (q t)")
@@ -249,7 +280,10 @@ def tile_attend_x_mla_sigmoid_seg_kernel(tc, qT, cT, ts, kb, ch, offs, out):
             )
 
         def finish(b):
-            y = ring2.tile([P, D], F32, name="y")
+            if 1 <= b < B - 1:
+                y = staged(*LATE[b + 1], [P, D], F32, f"y{b}")
+            else:
+                y = ring2.tile([P, D], F32, name="y")
             nc.vector.scalar_tensor_tensor(
                 out=y[:],
                 in0=acc[b][:],
@@ -260,38 +294,65 @@ def tile_attend_x_mla_sigmoid_seg_kernel(tc, qT, cT, ts, kb, ch, offs, out):
             )
             nc.sync.dma_start(out[b], y[:])
 
-        def front(b):
-            gather(b, 0)
-            turn(b, 0)
-            if b == 0:
-                gather_tokens(1, B)
-            gather(b, 1)
-            turn(b, 1)
-            weave(b)
-
-        gather_tokens(0, 1)
+        gather_tokens(0, 1, ("kb", "ts"))
+        turn_tokens(0, 1)
         cast(0, 0)
         cast(0, 1)
         cast(1, 0)
-        cast_queries()
         cast(1, 1)
-        cast(2, 0)
-        front(0)
+        gather(0, 0)
+        turn(0, 0)
+        gather_tokens(1, B, ("kb",))
+        gather(0, 1)
+        turn(0, 1)
+        gather_tokens(1, B, ("ts",))
+        weave(0)
+        cast_queries()
+        gather(1, 0)
+        gather(1, 1)
+        turn(1, 0)
+        turn(1, 1)
+        quantize_keys(0)
+        turn_tokens(1, B)
+        weave(1)
+        values_out(0, 0)
+        values_out(0, 1)
+        values(0)
         quantize_queries()
         score(0)
-        front(1)
+        cast(2, 0)
+        gather(2, 0)
+        quantize_keys(1)
         score(1)
-        for b in range(B):
+        cast(2, 1)
+        gather(2, 1)
+        turn(2, 0)
+        turn(2, 1)
+        weave(2)
+        cast(3, 0)
+        gather(3, 0)
+        quantize_keys(2)
+        weigh(0)
+        score(2)
+        cast(3, 1)
+        gather(3, 1)
+        product(0)
+        weigh(1)
+        weave(3)
+        finish(0)
+        values_out(1, 0)
+        values_out(1, 1)
+        turn(3, 0)
+        turn(3, 1)
+        quantize_keys(3)
+        score(3)
+        values(1)
+        product(1)
+        for b in range(2, B):
             values_out(b, 0)
             values_out(b, 1)
-            if b + 2 < B:
-                cast(b + 2, 1)
-                front(b + 2)
-            weigh(b)
-            if b + 3 < B:
-                cast(b + 3, 0)
-            if b + 2 < B:
-                score(b + 2)
             values(b)
+            weigh(b)
+            finish(b - 1)
             product(b)
-            finish(b)
+        finish(B - 1)

@@ -15,8 +15,10 @@ BYTES = 4 * (B * D * NQ + D * T + 2 * T + D + B * NQ * D) + 2 * P * (B * N // 16
 
 CAST_ON_VECTOR = ()
 STAGE_BYTES = 2 * SEG * 4
-LATE = {2: ((3, 1), 8128), 3: ((0, 1), 0)}
-HALVES = ((0, 0), (0, 1),)
+LATE = {0: ((1, 1), 0), 1: ((3, 0), 4160), 2: ((3, 1), 8128), 3: ((0, 1), 0)}
+ROW = {("kb", 0): 0, ("ts", 0): 4, ("kb", 1): 8, ("ts", 1): 0}
+PITCH = 10
+HALVES = ((0, 0), (0, 1), (1, 0), (1, 1), (3, 0), (3, 1))
 
 F32 = mybir.dt.float32
 BF16 = mybir.dt.bfloat16
@@ -62,15 +64,19 @@ def tile_attend_x_mla_sigmoid_seg_kernel(tc, qT, cT, ts, kb, ch, offs, out):
         q_raw = staged("q", 0, [P, B, LANES, NQ], F32, "q_raw")
         chans = keep.tile([P, D], F32, name="chans")
 
-        for c0, c1 in ((0, SEG + 1), (SEG + 1, T)):
-            nc.vector.memset(windows["kb"][:, c0:c1], 0.0)
-            nc.gpsimd.memset(windows["ts"][:, c0:c1], 0.0)
+        split = 3 * SEG + 8
+        nc.vector.memset(windows["kb"][:, 0 : SEG + 1], 0.0)
+        nc.gpsimd.memset(windows["ts"][:, 0 : SEG + 1], 0.0)
         ident = keep.tile([P, P], F32, name="ident")
         make_identity(nc, ident[:])
+        nc.vector.memset(windows["kb"][:, SEG + 1 : split], 0.0)
+        nc.gpsimd.memset(windows["kb"][:, split:T], 0.0)
+        nc.gpsimd.memset(windows["ts"][:, SEG + 1 : T], 0.0)
 
-        def load_rows(c0, c1):
-            for name, src in (("kb", kb), ("ts", ts)):
-                nc.sync.dma_start(windows[name][0:1, c0:c1], src[0:1, c0:c1])
+        def load_row(name, c0, c1):
+            src = {"kb": kb, "ts": ts}[name]
+            row = ROW[name, c0 // SEG]
+            nc.sync.dma_start(windows[name][row : row + 1, c0:c1], src[0:1, c0:c1])
 
         cT_view = cT.rearrange("(p j) w -> p j w", j=LANES)
 
@@ -90,15 +96,18 @@ def tile_attend_x_mla_sigmoid_seg_kernel(tc, qT, cT, ts, kb, ch, offs, out):
             )
 
         load_pool(0, 0)
-        load_rows(0, SEG)
+        load_row("kb", 0, SEG)
+        load_row("ts", 0, SEG)
         load_pool(0, 1)
-        load_rows(SEG, T)
+        load_row("kb", SEG, T)
         load_pool(1, 0)
+        load_row("ts", SEG, T)
         load_pool(1, 1)
+        load_pool(2, 0)
+        load_pool(2, 1)
         load_queries()
-        for b in range(2, B):
-            load_pool(b, 0)
-            load_pool(b, 1)
+        load_pool(3, 0)
+        load_pool(3, 1)
         nc.sync.dma_start(chans[:], ch)
 
         q_grp = keep.tile([P, B * NQ * LANES], BF16, align_bytes=64, name="q_grp")
@@ -111,15 +120,17 @@ def tile_attend_x_mla_sigmoid_seg_kernel(tc, qT, cT, ts, kb, ch, offs, out):
 
         rows = {}
 
-        def gather_tokens(b0, b1, names):
+        def gather_tokens(b0, b1, names, place=None):
             n = b1 - b0
             for name in names:
-                if b0 == 0:
-                    rows[name, b0] = keep.tile([P, n * N], F32, name=f"row_first_{name}")
+                if place is None:
+                    row = keep.tile([P, n * N], F32, name=f"row_first_{name}")
                 else:
-                    rows[name, b0] = staged((0, ("kb", "ts").index(name)), 0, [P, n * N], F32, f"row_later_{name}")
+                    row = staged(place, 0, [P, n * N], F32, f"row_{name}{b0}")
+                for b in range(n):
+                    rows[name, b0 + b] = row[:, b * N : (b + 1) * N]
                 nc.vector.tensor_copy(
-                    rows[name, b0][:].bitcast(U32).rearrange("p (b t g r) -> p b g t r", b=n, t=LANES, r=RUN),
+                    row[:].bitcast(U32).rearrange("p (b t g r) -> p b g t r", b=n, t=LANES, r=RUN),
                     windows[name][:].bitcast(U32)[:, 0 : b1 * SEG].indirect(
                         lists[:, b0 * LIST_COLUMNS : b1 * LIST_COLUMNS]
                     ),
@@ -130,15 +141,12 @@ def tile_attend_x_mla_sigmoid_seg_kernel(tc, qT, cT, ts, kb, ch, offs, out):
             bank = psum2.tile([P, 512], F32, tag="acc", name=f"bank{b0}")
             for i, name in enumerate(("kb", "ts")):
                 for c in range(n * LANES):
-                    c0 = 2 * (i * n * LANES + c)
-                    nc.tensor.transpose(bank[:, c0 : c0 + P], rows[name, b0][:, c * P : (c + 1) * P], ident[:])
-            if b0 == 0:
-                columns = keep.tile([P, 2, n, LANES], F32, name="columns_first")
-            else:
-                columns = staged((1, 1), 6144, [P, 2, n, LANES], F32, "columns_later")
-            nc.vector.tensor_copy(
+                    c0 = PITCH * (i * n * LANES + c + 1) - 2 - ROW[name, min(c // LANES, 1)]
+                    nc.tensor.transpose(bank[:, c0 : c0 + P], rows[name, b0 + c // LANES][:, (c % LANES) * P : (c % LANES + 1) * P], ident[:])
+            columns = staged((3, 1), 4672, [P, 2, n, LANES], F32, "columns")
+            nc.scalar.copy(
                 columns[:].rearrange("s i b t -> s (i b t)"),
-                bank[:, 0 : 4 * LANES * n].rearrange("s (c z) -> s c z", z=2)[:, :, 0],
+                bank[:, 0 : PITCH * 2 * LANES * n].rearrange("s (c z) -> s c z", z=PITCH)[:, :, PITCH - 2],
             )
             for b in range(n):
                 tokens[b0 + b] = columns[:, :, b, :]
@@ -166,10 +174,10 @@ def tile_attend_x_mla_sigmoid_seg_kernel(tc, qT, cT, ts, kb, ch, offs, out):
 
         def weave(b):
             k_grp[b] = ring3.tile([P, N * LANES], BF16, align_bytes=64, name="k_grp")
-            engine = nc.vector if b == B - 1 else nc.gpsimd
-            engine.tensor_copy(
-                k_grp[b][:].bitcast(I32).rearrange("p (c u) -> p c u", u=2),
-                picked[b][:].bitcast(I32).rearrange("p (u c) -> p c u", u=2),
+            copy = nc.scalar.copy if b == B - 1 else nc.gpsimd.tensor_copy
+            copy(
+                k_grp[b][:].bitcast(U32).rearrange("p (c u) -> p c u", u=2),
+                picked[b][:].rearrange("p (u c) -> p c u", u=2),
             )
 
         def turn(b, u):
@@ -179,14 +187,10 @@ def tile_attend_x_mla_sigmoid_seg_kernel(tc, qT, cT, ts, kb, ch, offs, out):
                 nc.tensor.transpose(turned[b, u][:, t, :], words[:, u, t, :], ident[:])
 
         def cast_queries():
-            nc.gpsimd.tensor_scalar(
-                q_grp[:].rearrange("p (b q j) -> p b q j", b=B, j=LANES),
-                q_raw[:].rearrange("p b j q -> p b q j"),
-                1.0,
-                0.0,
-                MULT,
-                ADD,
-            )
+            grouped = q_grp[:].rearrange("p (b q j) -> p b q j", b=B, j=LANES)
+            planes = q_raw[:].rearrange("p b j q -> p b q j")
+            for b in range(0, B, 2):
+                nc.gpsimd.tensor_scalar(grouped[:, b : b + 2], planes[:, b : b + 2], 1.0, 0.0, MULT, ADD)
 
         def quantize_queries():
             nc.vector.quantize_mx(out=q_codes[:].bitcast(FP8X4), scales=q_scales[:], in_=q_grp[:])
@@ -196,18 +200,21 @@ def tile_attend_x_mla_sigmoid_seg_kernel(tc, qT, cT, ts, kb, ch, offs, out):
         def quantize_keys(b):
             if b == 0:
                 k_codes = staged((1, 1), 4096, [P, N], U32, "k_codes0")
-            elif b + 1 < B:
-                k_codes = staged((b + 1, 0), 4096, [P, N], U32, f"k_codes{b}")
+            elif b == 1:
+                k_codes = staged((2, 1), 4096, [P, N], U32, f"k_codes{b}")
             else:
-                k_codes = keep.tile([P, N], U32, align_bytes=64, name="k_codes_last")
-            k_scales = ring3.tile([P, N], U8, align_bytes=64, name="k_scales")
+                k_codes = keep.tile([P, N], U32, align_bytes=64, name=f"k_codes{b}")
+            if b == 2:
+                k_scales = staged((3, 1), 4160, [P, N], U8, "k_scales2")
+            else:
+                k_scales = ring3.tile([P, N], U8, align_bytes=64, name="k_scales")
             nc.vector.quantize_mx(out=k_codes[:].bitcast(FP8X4), scales=k_scales[:], in_=k_grp[b][:])
             keys[b] = k_codes, k_scales
 
         def score(b):
             cols = slice(b * NQ, (b + 1) * NQ)
             k_codes, k_scales = keys[b]
-            scores[b] = psum2.tile([P, LANES, NQ], F32, name="scores")
+            scores[b] = psum2.tile([P, LANES, NQ], F32, tag="scores", name="scores")
             for t in range(LANES):
                 nc.tensor.matmul_mx(
                     out=scores[b][:, t, :],
@@ -221,26 +228,33 @@ def tile_attend_x_mla_sigmoid_seg_kernel(tc, qT, cT, ts, kb, ch, offs, out):
 
         v_grp = {}
 
-        def values_out(b, u):
-            if u == 0:
+        def values_out(b, u, h=0, pieces=1):
+            if u == 0 and h == 0:
                 if b + 2 < B:
-                    v_grp[b] = staged((1 + 2 * b, 1), 0, [P, D * LANES], BF16, f"v_grp{b}")
+                    v_grp[b] = staged(*LATE[b], [P, D * LANES], BF16, f"v_grp{b}")
                 else:
                     v_grp[b] = staged(*LATE[b], [P, D * LANES], BF16, f"v_grp{b}")
+            rows_m = slice(h * P // pieces, (h + 1) * P // pieces)
             nc.scalar.copy(
-                v_grp[b][:].rearrange("s (m u e t) -> s u m e t", u=2, e=2, t=LANES)[:, u],
-                turned[b, u][:].bitcast(BF16).rearrange("s t (m e) -> s m e t", e=2),
+                v_grp[b][:].rearrange("s (m u e t) -> s u m e t", u=2, e=2, t=LANES)[:, u, rows_m],
+                turned[b, u][:].bitcast(BF16).rearrange("s t (m e) -> s m e t", e=2)[:, rows_m],
             )
 
-        def values(b):
-            v_codes[b] = ring3.tile([P, D], U32, align_bytes=64, name="v_codes")
-            v_scales[b] = ring3.tile([P, D], U8, align_bytes=64, name="v_scales")
-            nc.vector.quantize_mx(out=v_codes[b][:].bitcast(FP8X4), scales=v_scales[b][:], in_=v_grp[b][:])
+        def values(b, h=0, pieces=1):
+            if h == 0:
+                v_codes[b] = ring3.tile([P, D], U32, align_bytes=64, name="v_codes")
+                v_scales[b] = ring3.tile([P, D], U8, align_bytes=64, name="v_scales")
+            w = D // pieces
+            nc.vector.quantize_mx(
+                out=v_codes[b][:, h * w : (h + 1) * w].bitcast(FP8X4),
+                scales=v_scales[b][:, h * w : (h + 1) * w],
+                in_=v_grp[b][:, h * w * LANES : (h + 1) * w * LANES],
+            )
 
         def weigh(b):
             bias, scale = tokens[b][:, 0, :], tokens[b][:, 1, :]
             if b + 2 < B:
-                p = staged((3, b), 6144 - 1536 * b, [P, LANES, NQ], F32, f"p{b}")
+                p = staged((3, 1), 64 + 2048 * b, [P, LANES, NQ], F32, f"p{b}")
             else:
                 p = ring2.tile([P, LANES, NQ], F32, name="p")
             for t in range(LANES):
@@ -252,107 +266,126 @@ def tile_attend_x_mla_sigmoid_seg_kernel(tc, qT, cT, ts, kb, ch, offs, out):
                     scale=scale[:, t : t + 1],
                 )
             w_grp[b] = ring2.tile([P, NQ, LANES], BF16, align_bytes=64, name="w_grp")
-            nc.vector.tensor_tensor(
+            engine = nc.gpsimd if b < 1 else nc.vector
+            engine.tensor_tensor(
                 w_grp[b][:].rearrange("s (c i) t -> s c t i", i=4),
                 p[:].rearrange("s t (c i) -> s c t i", i=4),
                 scale.unsqueeze(1).unsqueeze(3).to_broadcast([P, NQ // 4, LANES, 4]),
                 MULT,
             )
 
+        weights, ys = {}, {}
+
         def product(b):
-            if b == 0:
-                w_codes = staged((3, 1), 4096, [P, NQ], U32, f"w_codes{b}")
-            else:
-                w_codes = ring2.tile([P, NQ], U32, align_bytes=64, name="w_codes")
+            w_codes = ring2.tile([P, NQ], U32, align_bytes=64, name="w_codes")
             w_scales = ring2.tile([P, NQ], U8, align_bytes=64, name="w_scales")
             nc.vector.quantize_mx(
                 out=w_codes[:].bitcast(FP8X4), scales=w_scales[:], in_=w_grp[b][:].rearrange("s q t -> s (q t)")
             )
-            acc[b] = psum2.tile([P, D], F32, tag="acc", name=f"acc{b}")
-            nc.tensor.matmul_mx(
-                out=acc[b][:],
-                lhsT=w_codes[:].bitcast(FP8X4),
-                lhsT_scale=w_scales[:],
-                rhs=v_codes[b][:].bitcast(FP8X4),
-                rhs_scale=v_scales[b][:],
-                start=True,
-                stop=True,
-            )
+            weights[b] = w_codes, w_scales
+            acc[b] = []
 
-        def finish(b):
-            if 1 <= b < B - 1:
-                y = staged(*LATE[b + 1], [P, D], F32, f"y{b}")
-            else:
-                y = ring2.tile([P, D], F32, name="y")
-            nc.vector.scalar_tensor_tensor(
-                out=y[:],
-                in0=acc[b][:],
-                scalar=1.0 / 16.0,
-                in1=chans[:],
-                op0=MULT,
-                op1=MULT,
-            )
-            nc.sync.dma_start(out[b], y[:])
+        def multiply(b, i=0, pieces=1):
+            w_codes, w_scales = weights[b]
+            w = D // pieces
+            if True:
+                bank = psum2.tile([P, w], F32, tag="acc", name=f"acc{b}{i}") if i == 0 else psum2.tile([P, w], F32, tag="scores", name=f"acc{b}{i}")
+                nc.tensor.matmul_mx(
+                    out=bank[:],
+                    lhsT=w_codes[:].bitcast(FP8X4),
+                    lhsT_scale=w_scales[:],
+                    rhs=v_codes[b][:, i * w : (i + 1) * w].bitcast(FP8X4),
+                    rhs_scale=v_scales[b][:, i * w : (i + 1) * w],
+                    start=True,
+                    stop=True,
+                )
+                acc[b].append(bank)
+
+        def finish(b, i=0, pieces=1):
+            if i == 0:
+                if b == 1:
+                    ys[b] = staged(*LATE[b + 1], [P, D], F32, f"y{b}")
+                else:
+                    ys[b] = ring2.tile([P, D], F32, name="y")
+            y, bank = ys[b], acc[b][i]
+            w = D // pieces
+            if True:
+                cols = slice(i * w, (i + 1) * w)
+                nc.vector.scalar_tensor_tensor(
+                    out=y[:, cols], in0=bank[:], scalar=1.0 / 16.0, in1=chans[:, cols], op0=MULT, op1=MULT
+                )
+                nc.sync.dma_start(out[b][:, cols], y[:, cols])
 
         gather_tokens(0, 1, ("kb", "ts"))
-        turn_tokens(0, 1)
         cast(0, 0)
         cast(0, 1)
         cast(1, 0)
         cast(1, 1)
         gather(0, 0)
         turn(0, 0)
-        gather_tokens(1, B, ("kb",))
+        gather_tokens(1, B, ("kb",), (0, 0))
         gather(0, 1)
         turn(0, 1)
-        gather_tokens(1, B, ("ts",))
         weave(0)
-        cast_queries()
         gather(1, 0)
+        gather_tokens(1, B - 1, ("ts",), (1, 0))
         gather(1, 1)
         turn(1, 0)
         turn(1, 1)
         quantize_keys(0)
-        turn_tokens(1, B)
         weave(1)
         values_out(0, 0)
-        values_out(0, 1)
-        values(0)
-        quantize_queries()
-        score(0)
         cast(2, 0)
         gather(2, 0)
-        quantize_keys(1)
-        score(1)
         cast(2, 1)
+        values_out(0, 1)
+        values(0)
         gather(2, 1)
         turn(2, 0)
         turn(2, 1)
+        gather_tokens(B - 1, B, ("ts",), (2, 1))
+        cast_queries()
         weave(2)
+        quantize_queries()
+        score(0)
+        quantize_keys(1)
+        score(1)
         cast(3, 0)
         gather(3, 0)
+        cast(3, 1)
+        turn_tokens(0, B)
+        gather(3, 1)
         quantize_keys(2)
         weigh(0)
         score(2)
-        cast(3, 1)
-        gather(3, 1)
-        product(0)
         weigh(1)
         weave(3)
-        finish(0)
+        quantize_keys(3)
+        product(0)
+        multiply(0)
         values_out(1, 0)
         values_out(1, 1)
         turn(3, 0)
         turn(3, 1)
-        quantize_keys(3)
         score(3)
+        finish(0)
         values(1)
         product(1)
-        for b in range(2, B):
-            values_out(b, 0)
-            values_out(b, 1)
-            values(b)
-            weigh(b)
-            finish(b - 1)
-            product(b)
-        finish(B - 1)
+        multiply(1)
+        values_out(2, 0)
+        values_out(2, 1)
+        values(2)
+        weigh(2)
+        finish(1)
+        product(2)
+        multiply(2)
+        weigh(3)
+        finish(2)
+        product(3)
+        for h in range(2):
+            values_out(3, 0, h, 2)
+            values_out(3, 1, h, 2)
+            values(3, h, 2)
+            multiply(3, h, 2)
+        for h in range(2):
+            finish(3, h, 2)

@@ -15,10 +15,10 @@ BYTES = 4 * (B * D * NQ + D * T + 2 * T + D + B * NQ * D) + 2 * P * (B * N // 16
 
 CAST_ON_VECTOR = ()
 STAGE_BYTES = 2 * SEG * 4
-LATE = {0: ((1, 1), 0), 1: ((3, 0), 4160), 2: ((3, 1), 8128), 3: ((0, 1), 0)}
+LATE = {0: ((1, 1), 0), 1: ((2, 1), 4096), 2: ((3, 1), 0), 3: ((1, 0), 0)}
 ROW = {("kb", 0): 0, ("ts", 0): 4, ("kb", 1): 8, ("ts", 1): 0}
 PITCH = 10
-HALVES = ((0, 0), (0, 1), (1, 0), (1, 1), (3, 0), (3, 1))
+HALVES = ((0, 0), (0, 1), (3, 1))
 
 F32 = mybir.dt.float32
 BF16 = mybir.dt.bfloat16
@@ -53,7 +53,7 @@ def tile_attend_x_mla_sigmoid_seg_kernel(tc, qT, cT, ts, kb, ch, offs, out):
 
         windows = {name: keep.tile([P, T], F32, name="window_" + name) for name in ("kb", "ts")}
         def staged(place, offset, shape, dtype, name):
-            index = 2 * B if place == "q" else 2 * place[0] + place[1]
+            index = {"q": 2 * B, "g": 2 * B + 1}[place] if place in ("q", "g") else 2 * place[0] + place[1]
             return stage.tile(shape, dtype, align_bytes=64, offset=index * STAGE_BYTES + offset, name=name)
 
         raw = {
@@ -103,14 +103,14 @@ def tile_attend_x_mla_sigmoid_seg_kernel(tc, qT, cT, ts, kb, ch, offs, out):
         load_pool(1, 0)
         load_row("ts", SEG, T)
         load_pool(1, 1)
+        load_queries()
         load_pool(2, 0)
         load_pool(2, 1)
-        load_queries()
         load_pool(3, 0)
         load_pool(3, 1)
         nc.sync.dma_start(chans[:], ch)
 
-        q_grp = keep.tile([P, B * NQ * LANES], BF16, align_bytes=64, name="q_grp")
+        q_grp = staged("g", 0, [P, B * NQ * LANES], BF16, "q_grp")
         q_codes = keep.tile([P, B * NQ], U32, align_bytes=64, name="q_codes")
         q_scales = keep.tile([P, B * NQ], U8, align_bytes=64, name="q_scales")
 
@@ -126,7 +126,7 @@ def tile_attend_x_mla_sigmoid_seg_kernel(tc, qT, cT, ts, kb, ch, offs, out):
                 if place is None:
                     row = keep.tile([P, n * N], F32, name=f"row_first_{name}")
                 else:
-                    row = staged(place, 0, [P, n * N], F32, f"row_{name}{b0}")
+                    row = staged(*place, [P, n * N], F32, f"row_{name}{b0}")
                 for b in range(n):
                     rows[name, b0 + b] = row[:, b * N : (b + 1) * N]
                 nc.vector.tensor_copy(
@@ -141,9 +141,9 @@ def tile_attend_x_mla_sigmoid_seg_kernel(tc, qT, cT, ts, kb, ch, offs, out):
             bank = psum2.tile([P, 512], F32, tag="acc", name=f"bank{b0}")
             for i, name in enumerate(("kb", "ts")):
                 for c in range(n * LANES):
-                    c0 = PITCH * (i * n * LANES + c + 1) - 2 - ROW[name, min(c // LANES, 1)]
+                    c0 = PITCH * (i * n * LANES + c + 1) - 2 - ROW[name, min(b0 + c // LANES, 1)]
                     nc.tensor.transpose(bank[:, c0 : c0 + P], rows[name, b0 + c // LANES][:, (c % LANES) * P : (c % LANES + 1) * P], ident[:])
-            columns = staged((3, 1), 4672, [P, 2, n, LANES], F32, "columns")
+            columns = staged(*{0: ((2, 1), 2112), 2: ((3, 1), 4096)}[b0], [P, 2, n, LANES], F32, f"columns{b0}")
             nc.scalar.copy(
                 columns[:].rearrange("s i b t -> s (i b t)"),
                 bank[:, 0 : PITCH * 2 * LANES * n].rearrange("s (c z) -> s c z", z=PITCH)[:, :, PITCH - 2],
@@ -173,11 +173,14 @@ def tile_attend_x_mla_sigmoid_seg_kernel(tc, qT, cT, ts, kb, ch, offs, out):
             )
 
         def weave(b):
-            k_grp[b] = ring3.tile([P, N * LANES], BF16, align_bytes=64, name="k_grp")
-            copy = nc.scalar.copy if b == B - 1 else nc.gpsimd.tensor_copy
-            copy(
-                k_grp[b][:].bitcast(U32).rearrange("p (c u) -> p c u", u=2),
-                picked[b][:].rearrange("p (u c) -> p c u", u=2),
+            if b == 1:
+                k_grp[b] = staged("g", 0, [P, N * LANES], BF16, "k_grp1")
+            else:
+                k_grp[b] = ring3.tile([P, N * LANES], BF16, align_bytes=64, name="k_grp")
+            engine = nc.vector if b == B - 1 else nc.gpsimd
+            engine.tensor_copy(
+                k_grp[b][:].bitcast(I32).rearrange("p (c u) -> p c u", u=2),
+                picked[b][:].bitcast(I32).rearrange("p (u c) -> p c u", u=2),
             )
 
         def turn(b, u):
@@ -200,12 +203,10 @@ def tile_attend_x_mla_sigmoid_seg_kernel(tc, qT, cT, ts, kb, ch, offs, out):
         def quantize_keys(b):
             if b == 0:
                 k_codes = staged((1, 1), 4096, [P, N], U32, "k_codes0")
-            elif b == 1:
-                k_codes = staged((2, 1), 4096, [P, N], U32, f"k_codes{b}")
             else:
                 k_codes = keep.tile([P, N], U32, align_bytes=64, name=f"k_codes{b}")
-            if b == 2:
-                k_scales = staged((3, 1), 4160, [P, N], U8, "k_scales2")
+            if b == 1:
+                k_scales = staged((2, 0), 0, [P, N], U8, "k_scales1")
             else:
                 k_scales = ring3.tile([P, N], U8, align_bytes=64, name="k_scales")
             nc.vector.quantize_mx(out=k_codes[:].bitcast(FP8X4), scales=k_scales[:], in_=k_grp[b][:])
@@ -253,8 +254,8 @@ def tile_attend_x_mla_sigmoid_seg_kernel(tc, qT, cT, ts, kb, ch, offs, out):
 
         def weigh(b):
             bias, scale = tokens[b][:, 0, :], tokens[b][:, 1, :]
-            if b + 2 < B:
-                p = staged((3, 1), 64 + 2048 * b, [P, LANES, NQ], F32, f"p{b}")
+            if b == 1:
+                p = staged((3, 0), 0, [P, LANES, NQ], F32, f"p{b}")
             else:
                 p = ring2.tile([P, LANES, NQ], F32, name="p")
             for t in range(LANES):
@@ -266,7 +267,7 @@ def tile_attend_x_mla_sigmoid_seg_kernel(tc, qT, cT, ts, kb, ch, offs, out):
                     scale=scale[:, t : t + 1],
                 )
             w_grp[b] = ring2.tile([P, NQ, LANES], BF16, align_bytes=64, name="w_grp")
-            engine = nc.gpsimd if b < 1 else nc.vector
+            engine = nc.vector
             engine.tensor_tensor(
                 w_grp[b][:].rearrange("s (c i) t -> s c t i", i=4),
                 p[:].rearrange("s t (c i) -> s c t i", i=4),
@@ -278,7 +279,10 @@ def tile_attend_x_mla_sigmoid_seg_kernel(tc, qT, cT, ts, kb, ch, offs, out):
 
         def product(b):
             w_codes = ring2.tile([P, NQ], U32, align_bytes=64, name="w_codes")
-            w_scales = ring2.tile([P, NQ], U8, align_bytes=64, name="w_scales")
+            if b == 1:
+                w_scales = staged((3, 1), 4608, [P, NQ], U8, "w_scales1")
+            else:
+                w_scales = ring2.tile([P, NQ], U8, align_bytes=64, name="w_scales")
             nc.vector.quantize_mx(
                 out=w_codes[:].bitcast(FP8X4), scales=w_scales[:], in_=w_grp[b][:].rearrange("s q t -> s (q t)")
             )
@@ -303,7 +307,9 @@ def tile_attend_x_mla_sigmoid_seg_kernel(tc, qT, cT, ts, kb, ch, offs, out):
 
         def finish(b, i=0, pieces=1):
             if i == 0:
-                if b == 1:
+                if b == 0:
+                    ys[b] = staged((3, 0), 2048, [P, D], F32, f"y{b}")
+                elif b == 1:
                     ys[b] = staged(*LATE[b + 1], [P, D], F32, f"y{b}")
                 else:
                     ys[b] = ring2.tile([P, D], F32, name="y")
@@ -323,55 +329,57 @@ def tile_attend_x_mla_sigmoid_seg_kernel(tc, qT, cT, ts, kb, ch, offs, out):
         cast(1, 1)
         gather(0, 0)
         turn(0, 0)
-        gather_tokens(1, B, ("kb",), (0, 0))
+        gather_tokens(1, B - 1, ("kb",), ((0, 0), 0))
         gather(0, 1)
         turn(0, 1)
         weave(0)
+        gather_tokens(1, B - 1, ("ts",), ((0, 1), 0))
+        cast_queries()
         gather(1, 0)
-        gather_tokens(1, B - 1, ("ts",), (1, 0))
         gather(1, 1)
         turn(1, 0)
         turn(1, 1)
         quantize_keys(0)
-        weave(1)
         values_out(0, 0)
-        cast(2, 0)
-        gather(2, 0)
-        cast(2, 1)
         values_out(0, 1)
         values(0)
+        quantize_queries()
+        score(0)
+        weave(1)
+        cast(2, 0)
+        gather(2, 0)
+        quantize_keys(1)
+        score(1)
+        cast(2, 1)
         gather(2, 1)
         turn(2, 0)
         turn(2, 1)
-        gather_tokens(B - 1, B, ("ts",), (2, 1))
-        cast_queries()
         weave(2)
-        quantize_queries()
-        score(0)
-        quantize_keys(1)
-        score(1)
-        cast(3, 0)
-        gather(3, 0)
-        cast(3, 1)
-        turn_tokens(0, B)
-        gather(3, 1)
-        quantize_keys(2)
-        weigh(0)
-        score(2)
-        weigh(1)
-        weave(3)
-        quantize_keys(3)
-        product(0)
-        multiply(0)
+        gather_tokens(B - 1, B, ("kb",), ((2, 1), 64))
+        gather_tokens(B - 1, B, ("ts",), ((2, 0), 6208))
         values_out(1, 0)
         values_out(1, 1)
-        turn(3, 0)
-        turn(3, 1)
-        score(3)
-        finish(0)
+        turn_tokens(0, 2)
+        turn_tokens(2, B)
+        quantize_keys(2)
         values(1)
+        weigh(0)
+        score(2)
+        product(0)
+        multiply(0)
+        cast(3, 0)
+        gather(3, 0)
+        turn(3, 0)
+        finish(0)
+        weigh(1)
+        cast(3, 1)
+        gather(3, 1)
+        turn(3, 1)
         product(1)
         multiply(1)
+        weave(3)
+        quantize_keys(3)
+        score(3)
         values_out(2, 0)
         values_out(2, 1)
         values(2)

@@ -8,17 +8,44 @@ P = 128
 SEG = T // B
 LANES = 4
 RUN = 8
+LINE = 4
 LIST_COLUMNS = N // 16
+LAST = B - 1
+ON_GPSIMD = 2
 
 FLOPS = B * 2 * (2 * N * D * NQ)
 BYTES = 4 * (B * D * NQ + D * T + 2 * T + D + B * NQ * D) + 2 * P * (B * N // 16)
 
-CAST_ON_VECTOR = ()
-STAGE_BYTES = 2 * SEG * 4
-LATE = {0: ((1, 1), 0), 1: ((2, 1), 4096), 2: ((3, 1), 0), 3: ((1, 0), 0)}
+HALVED = ((0, 0), (0, 1), (1, 0), (1, 1), (2, 0), (2, 1), (3, 1))
+
+KB_SPLIT = 2 * SEG + 264
+
 ROW = {("kb", 0): 0, ("ts", 0): 4, ("kb", 1): 8, ("ts", 1): 0}
 PITCH = 10
-HALVES = ((0, 0), (0, 1), (3, 1))
+
+AREA = 2 * SEG * 4
+HALF_AREA = AREA // 2
+REUSE = {
+    "row_kb1": ((0, 0), 0),
+    "row_ts1": ((0, 1), 0),
+    "row_kb3": ((2, 1), 64),
+    "row_ts3": ((2, 0), 6208),
+    "v_grp0": ((1, 0), HALF_AREA),
+    "v_grp1": ((2, 1), HALF_AREA),
+    "v_grp2": ((3, 1), 0),
+    "v_grp3": ((1, 0), 0),
+    "columns0": ((2, 1), 2112),
+    "columns2": ((3, 1), HALF_AREA),
+    "p1": ((3, 0), 0),
+    "k_codes0": ((1, 1), HALF_AREA),
+    "k_scales1": ((2, 1), 2240),
+    "w_scales1": ((3, 1), 4608),
+    "y0": ((3, 0), 2048),
+    "y1": ((3, 1), 0),
+    "k_grp1": ("g", 0),
+    "w_grp0": ("q", 0),
+    "w_grp1": ("q", 0),
+}
 
 F32 = mybir.dt.float32
 BF16 = mybir.dt.bfloat16
@@ -43,6 +70,16 @@ def tile_attend_x_mla_sigmoid_seg_kernel(tc, qT, cT, ts, kb, ch, offs, out):
         psum2 = ctx.enter_context(tc.psum_pool(name="psum2", bufs=2))
         psum4 = ctx.enter_context(tc.psum_pool(name="psum4", bufs=4))
 
+        def staged(area, offset, shape, dtype, name):
+            index = {"q": 2 * B, "g": 2 * B + 1}[area] if area in ("q", "g") else 2 * area[0] + area[1]
+            return stage.tile(shape, dtype, align_bytes=64, offset=index * AREA + offset, name=name)
+
+        def placed(kind, b, shape, dtype, home, align=64):
+            name = f"{kind}{b}"
+            if name in REUSE:
+                return staged(*REUSE[name], shape, dtype, name)
+            return home.tile(shape, dtype, align_bytes=align, name=name if home is keep else kind)
+
         lists = keep.tile([P, B * N // 16], U16, name="lists")
         nc.sync.dma_start(lists[:], offs)
 
@@ -52,47 +89,37 @@ def tile_attend_x_mla_sigmoid_seg_kernel(tc, qT, cT, ts, kb, ch, offs, out):
         nc.scalar.activation(warm_out[:], warm[:], SIGMOID)
 
         windows = {name: keep.tile([P, T], F32, name="window_" + name) for name in ("kb", "ts")}
-        def staged(place, offset, shape, dtype, name):
-            index = {"q": 2 * B, "g": 2 * B + 1}[place] if place in ("q", "g") else 2 * place[0] + place[1]
-            return stage.tile(shape, dtype, align_bytes=64, offset=index * STAGE_BYTES + offset, name=name)
-
-        raw = {
-            (b, u): staged((b, u), 0, [P, 2, SEG], F32, f"raw{b}{u}")
-            for b in range(B)
-            for u in range(2)
-        }
-        q_raw = staged("q", 0, [P, B, LANES, NQ], F32, "q_raw")
+        raw = {(b, u): staged((b, u), 0, [P, 2, SEG], F32, f"raw{b}{u}") for b in range(B) for u in range(2)}
+        q_raw = [staged("q", HALF_AREA * h, [P, 2, LANES, NQ], F32, f"q_raw{h}") for h in range(2)]
         chans = keep.tile([P, D], F32, name="chans")
 
-        split = 3 * SEG + 8
         nc.vector.memset(windows["kb"][:, 0 : SEG + 1], 0.0)
         nc.gpsimd.memset(windows["ts"][:, 0 : SEG + 1], 0.0)
+        nc.vector.memset(windows["kb"][:, SEG + 1 : KB_SPLIT], 0.0)
+        nc.gpsimd.memset(windows["kb"][:, KB_SPLIT:T], 0.0)
+        nc.gpsimd.memset(windows["ts"][:, SEG + 1 : T], 0.0)
         ident = keep.tile([P, P], F32, name="ident")
         make_identity(nc, ident[:])
-        nc.vector.memset(windows["kb"][:, SEG + 1 : split], 0.0)
-        nc.gpsimd.memset(windows["kb"][:, split:T], 0.0)
-        nc.gpsimd.memset(windows["ts"][:, SEG + 1 : T], 0.0)
-
-        def load_row(name, c0, c1):
-            src = {"kb": kb, "ts": ts}[name]
-            row = ROW[name, c0 // SEG]
-            nc.sync.dma_start(windows[name][row : row + 1, c0:c1], src[0:1, c0:c1])
 
         cT_view = cT.rearrange("(p j) w -> p j w", j=LANES)
 
-        def load_pool(b, u):
-            pieces = 2 if (b, u) in HALVES else 1
-            w = SEG // pieces
-            for i in range(pieces):
-                nc.sync.dma_start(
-                    raw[b, u][:, :, i * w : (i + 1) * w],
-                    cT_view[:, 2 * u : 2 * u + 2, b * SEG + i * w : b * SEG + (i + 1) * w],
-                )
+        def token_ranges(b, u):
+            width = SEG // 2 if (b, u) in HALVED else SEG
+            return [(c0, c0 + width) for c0 in range(0, SEG, width)]
 
-        def load_queries():
+        def load_row(name, c0, c1):
+            row = ROW[name, c0 // SEG]
+            source = {"kb": kb, "ts": ts}[name]
+            nc.sync.dma_start(windows[name][row : row + 1, c0:c1], source[0:1, c0:c1])
+
+        def load_pool(b, u):
+            for c0, c1 in token_ranges(b, u):
+                nc.sync.dma_start(raw[b, u][:, :, c0:c1], cT_view[:, 2 * u : 2 * u + 2, b * SEG + c0 : b * SEG + c1])
+
+        def load_queries(h):
             nc.sync.dma_start(
-                q_raw[:].rearrange("p b j q -> p b (j q)"),
-                qT.rearrange("b (p j) q -> p b (j q)", j=LANES),
+                q_raw[h][:].rearrange("p b j q -> p b (j q)"),
+                qT.rearrange("b (p j) q -> p b (j q)", j=LANES)[:, 2 * h : 2 * h + 2],
             )
 
         load_pool(0, 0)
@@ -103,47 +130,43 @@ def tile_attend_x_mla_sigmoid_seg_kernel(tc, qT, cT, ts, kb, ch, offs, out):
         load_pool(1, 0)
         load_row("ts", SEG, T)
         load_pool(1, 1)
-        load_queries()
-        load_pool(2, 0)
-        load_pool(2, 1)
-        load_pool(3, 0)
-        load_pool(3, 1)
+        for h in range(2):
+            load_queries(h)
+            load_pool(2 + h, 0)
+            load_pool(2 + h, 1)
         nc.sync.dma_start(chans[:], ch)
 
-        q_grp = staged("g", 0, [P, B * NQ * LANES], BF16, "q_grp")
+        q_grp = [staged("g", HALF_AREA * h, [P, 2 * NQ * LANES], BF16, f"q_grp{h}") for h in range(2)]
         q_codes = keep.tile([P, B * NQ], U32, align_bytes=64, name="q_codes")
         q_scales = keep.tile([P, B * NQ], U8, align_bytes=64, name="q_scales")
 
         pool = [keep.tile([P, 2 * T], BF16, name=f"pool{u}") for u in range(2)]
-        picked, k_grp, tokens, scores, turned, acc = {}, {}, {}, {}, {}, {}
-        v_codes, v_scales, w_grp = {}, {}, {}
+        rows, tokens, picked, turned = {}, {}, {}, {}
+        k_grp, keys, scores = {}, {}, {}
+        v_grp, values, w_grp, weights, acc, ys = {}, {}, {}, {}, {}, {}
 
-        rows = {}
-
-        def gather_tokens(b0, b1, names, place=None):
+        def gather_tokens(name, b0, b1):
             n = b1 - b0
-            for name in names:
-                if place is None:
-                    row = keep.tile([P, n * N], F32, name=f"row_first_{name}")
-                else:
-                    row = staged(*place, [P, n * N], F32, f"row_{name}{b0}")
-                for b in range(n):
-                    rows[name, b0 + b] = row[:, b * N : (b + 1) * N]
-                nc.vector.tensor_copy(
-                    row[:].bitcast(U32).rearrange("p (b t g r) -> p b g t r", b=n, t=LANES, r=RUN),
-                    windows[name][:].bitcast(U32)[:, 0 : b1 * SEG].indirect(
-                        lists[:, b0 * LIST_COLUMNS : b1 * LIST_COLUMNS]
-                    ),
-                )
+            row = placed(f"row_{name}", b0, [P, n * N], F32, keep, align=None)
+            for b in range(n):
+                rows[name, b0 + b] = row[:, b * N : (b + 1) * N]
+            nc.vector.tensor_copy(
+                row[:].bitcast(U32).rearrange("p (b t g r) -> p b g t r", b=n, t=LANES, r=RUN),
+                windows[name][:].bitcast(U32)[:, 0 : b1 * SEG].indirect(
+                    lists[:, b0 * LIST_COLUMNS : b1 * LIST_COLUMNS]
+                ),
+            )
 
         def turn_tokens(b0, b1):
             n = b1 - b0
             bank = psum2.tile([P, 512], F32, tag="acc", name=f"bank{b0}")
             for i, name in enumerate(("kb", "ts")):
-                for c in range(n * LANES):
-                    c0 = PITCH * (i * n * LANES + c + 1) - 2 - ROW[name, min(b0 + c // LANES, 1)]
-                    nc.tensor.transpose(bank[:, c0 : c0 + P], rows[name, b0 + c // LANES][:, (c % LANES) * P : (c % LANES + 1) * P], ident[:])
-            columns = staged(*{0: ((2, 1), 2112), 2: ((3, 1), 4096)}[b0], [P, 2, n, LANES], F32, f"columns{b0}")
+                for b in range(b0, b1):
+                    for t in range(LANES):
+                        c = (i * n + b - b0) * LANES + t
+                        c0 = PITCH * (c + 1) - 2 - ROW[name, min(b, 1)]
+                        nc.tensor.transpose(bank[:, c0 : c0 + P], rows[name, b][:, t * P : (t + 1) * P], ident[:])
+            columns = placed("columns", b0, [P, 2, n, LANES], F32, keep)
             nc.scalar.copy(
                 columns[:].rearrange("s i b t -> s (i b t)"),
                 bank[:, 0 : PITCH * 2 * LANES * n].rearrange("s (c z) -> s c z", z=PITCH)[:, :, PITCH - 2],
@@ -152,16 +175,12 @@ def tile_attend_x_mla_sigmoid_seg_kernel(tc, qT, cT, ts, kb, ch, offs, out):
                 tokens[b0 + b] = columns[:, :, b, :]
 
         def cast(b, u):
-            pieces = 2 if (b, u) in HALVES else 1
-            w = SEG // pieces
-            for i in range(pieces):
-                c0 = 2 * (b * SEG + i * w)
-                pair_out = pool[u][:, c0 : c0 + 2 * w].rearrange("p (w e) -> p w e", e=2)
-                pair_in = raw[b, u][:, :, i * w : (i + 1) * w].rearrange("p e w -> p w e")
-                if (b, u) in CAST_ON_VECTOR:
-                    nc.vector.tensor_copy(pair_out, pair_in)
-                else:
-                    nc.scalar.activation(pair_out, pair_in, COPY)
+            for c0, c1 in token_ranges(b, u):
+                nc.scalar.activation(
+                    pool[u][:, 2 * (b * SEG + c0) : 2 * (b * SEG + c1)].rearrange("p (w e) -> p w e", e=2),
+                    raw[b, u][:, :, c0:c1].rearrange("p e w -> p w e"),
+                    COPY,
+                )
 
         def gather(b, u):
             if u == 0:
@@ -173,11 +192,8 @@ def tile_attend_x_mla_sigmoid_seg_kernel(tc, qT, cT, ts, kb, ch, offs, out):
             )
 
         def weave(b):
-            if b == 1:
-                k_grp[b] = staged("g", 0, [P, N * LANES], BF16, "k_grp1")
-            else:
-                k_grp[b] = ring3.tile([P, N * LANES], BF16, align_bytes=64, name="k_grp")
-            engine = nc.vector if b == B - 1 else nc.gpsimd
+            k_grp[b] = placed("k_grp", b, [P, N * LANES], BF16, ring3)
+            engine = nc.vector if b == LAST else nc.gpsimd
             engine.tensor_copy(
                 k_grp[b][:].bitcast(I32).rearrange("p (c u) -> p c u", u=2),
                 picked[b][:].bitcast(I32).rearrange("p (u c) -> p c u", u=2),
@@ -189,26 +205,18 @@ def tile_attend_x_mla_sigmoid_seg_kernel(tc, qT, cT, ts, kb, ch, offs, out):
             for t in range(LANES):
                 nc.tensor.transpose(turned[b, u][:, t, :], words[:, u, t, :], ident[:])
 
-        def cast_queries():
-            grouped = q_grp[:].rearrange("p (b q j) -> p b q j", b=B, j=LANES)
-            planes = q_raw[:].rearrange("p b j q -> p b q j")
-            for b in range(0, B, 2):
-                nc.gpsimd.tensor_scalar(grouped[:, b : b + 2], planes[:, b : b + 2], 1.0, 0.0, MULT, ADD)
+        def cast_queries(h):
+            grouped = q_grp[h][:].rearrange("p (b q j) -> p b q j", b=2, j=LANES)
+            planes = q_raw[h][:].rearrange("p b j q -> p b q j")
+            nc.gpsimd.tensor_scalar(grouped, planes, 1.0, 0.0, MULT, ADD)
 
-        def quantize_queries():
-            nc.vector.quantize_mx(out=q_codes[:].bitcast(FP8X4), scales=q_scales[:], in_=q_grp[:])
-
-        keys = {}
+        def quantize_queries(h):
+            cols = slice(2 * h * NQ, 2 * (h + 1) * NQ)
+            nc.vector.quantize_mx(out=q_codes[:, cols].bitcast(FP8X4), scales=q_scales[:, cols], in_=q_grp[h][:])
 
         def quantize_keys(b):
-            if b == 0:
-                k_codes = staged((1, 1), 4096, [P, N], U32, "k_codes0")
-            else:
-                k_codes = keep.tile([P, N], U32, align_bytes=64, name=f"k_codes{b}")
-            if b == 1:
-                k_scales = staged((2, 0), 0, [P, N], U8, "k_scales1")
-            else:
-                k_scales = ring3.tile([P, N], U8, align_bytes=64, name="k_scales")
+            k_codes = placed("k_codes", b, [P, N], U32, keep)
+            k_scales = placed("k_scales", b, [P, N], U8, ring3)
             nc.vector.quantize_mx(out=k_codes[:].bitcast(FP8X4), scales=k_scales[:], in_=k_grp[b][:])
             keys[b] = k_codes, k_scales
 
@@ -227,37 +235,56 @@ def tile_attend_x_mla_sigmoid_seg_kernel(tc, qT, cT, ts, kb, ch, offs, out):
                     stop=True,
                 )
 
-        v_grp = {}
 
-        def values_out(b, u, h=0, pieces=1):
+        def copy_values(b, u, h=0, parts=1):
             if u == 0 and h == 0:
-                if b + 2 < B:
-                    v_grp[b] = staged(*LATE[b], [P, D * LANES], BF16, f"v_grp{b}")
-                else:
-                    v_grp[b] = staged(*LATE[b], [P, D * LANES], BF16, f"v_grp{b}")
-            rows_m = slice(h * P // pieces, (h + 1) * P // pieces)
+                v_grp[b] = placed("v_grp", b, [P, D * LANES], BF16, keep)
+            ms = slice(h * P // parts, (h + 1) * P // parts)
             nc.scalar.copy(
-                v_grp[b][:].rearrange("s (m u e t) -> s u m e t", u=2, e=2, t=LANES)[:, u, rows_m],
-                turned[b, u][:].bitcast(BF16).rearrange("s t (m e) -> s m e t", e=2)[:, rows_m],
+                v_grp[b][:].rearrange("s (m u e t) -> s u m e t", u=2, e=2, t=LANES)[:, u, ms],
+                turned[b, u][:].bitcast(BF16).rearrange("s t (m e) -> s m e t", e=2)[:, ms],
             )
 
-        def values(b, h=0, pieces=1):
+        def quantize_values(b, h=0, parts=1):
             if h == 0:
-                v_codes[b] = ring3.tile([P, D], U32, align_bytes=64, name="v_codes")
-                v_scales[b] = ring3.tile([P, D], U8, align_bytes=64, name="v_scales")
-            w = D // pieces
+                v_codes = ring3.tile([P, D], U32, align_bytes=64, name="v_codes")
+                v_scales = ring3.tile([P, D], U8, align_bytes=64, name="v_scales")
+                values[b] = v_codes, v_scales
+            v_codes, v_scales = values[b]
+            d0, d1 = h * D // parts, (h + 1) * D // parts
             nc.vector.quantize_mx(
-                out=v_codes[b][:, h * w : (h + 1) * w].bitcast(FP8X4),
-                scales=v_scales[b][:, h * w : (h + 1) * w],
-                in_=v_grp[b][:, h * w * LANES : (h + 1) * w * LANES],
+                out=v_codes[:, d0:d1].bitcast(FP8X4),
+                scales=v_scales[:, d0:d1],
+                in_=v_grp[b][:, d0 * LANES : d1 * LANES],
             )
+
+        def multiply(b, h=0, parts=1):
+            w_codes, w_scales = weights[b]
+            v_codes, v_scales = values[b]
+            d0, d1 = h * D // parts, (h + 1) * D // parts
+            acc[b, h] = psum2.tile([P, d1 - d0], F32, tag=("acc", "scores")[h], name=f"acc{b}{h}")
+            nc.tensor.matmul_mx(
+                out=acc[b, h][:],
+                lhsT=w_codes[:].bitcast(FP8X4),
+                lhsT_scale=w_scales[:],
+                rhs=v_codes[:, d0:d1].bitcast(FP8X4),
+                rhs_scale=v_scales[:, d0:d1],
+                start=True,
+                stop=True,
+            )
+
+        def finish(b, h=0, parts=1):
+            if h == 0:
+                ys[b] = placed("y", b, [P, D], F32, ring2, align=None)
+            cols = slice(h * D // parts, (h + 1) * D // parts)
+            nc.vector.scalar_tensor_tensor(
+                out=ys[b][:, cols], in0=acc[b, h][:], scalar=1.0 / 16.0, in1=chans[:, cols], op0=MULT, op1=MULT
+            )
+            nc.sync.dma_start(out[b][:, cols], ys[b][:, cols])
 
         def weigh(b):
             bias, scale = tokens[b][:, 0, :], tokens[b][:, 1, :]
-            if b == 1:
-                p = staged((3, 0), 0, [P, LANES, NQ], F32, f"p{b}")
-            else:
-                p = ring2.tile([P, LANES, NQ], F32, name="p")
+            p = placed("p", b, [P, LANES, NQ], F32, ring2, align=None)
             for t in range(LANES):
                 nc.scalar.activation(
                     p[:, t, :],
@@ -266,134 +293,100 @@ def tile_attend_x_mla_sigmoid_seg_kernel(tc, qT, cT, ts, kb, ch, offs, out):
                     bias=bias[:, t : t + 1],
                     scale=scale[:, t : t + 1],
                 )
-            w_grp[b] = ring2.tile([P, NQ, LANES], BF16, align_bytes=64, name="w_grp")
-            engine = nc.vector
+            w_grp[b] = placed("w_grp", b, [P, NQ, LANES], BF16, ring2)
+            engine = nc.gpsimd if b < ON_GPSIMD else nc.vector
             engine.tensor_tensor(
-                w_grp[b][:].rearrange("s (c i) t -> s c t i", i=4),
-                p[:].rearrange("s t (c i) -> s c t i", i=4),
-                scale.unsqueeze(1).unsqueeze(3).to_broadcast([P, NQ // 4, LANES, 4]),
+                w_grp[b][:].rearrange("s (c i) t -> s c t i", i=LINE),
+                p[:].rearrange("s t (c i) -> s c t i", i=LINE),
+                scale.unsqueeze(1).unsqueeze(3).to_broadcast([P, NQ // LINE, LANES, LINE]),
                 MULT,
             )
 
-        weights, ys = {}, {}
-
-        def product(b):
+        def quantize_weights(b):
             w_codes = ring2.tile([P, NQ], U32, align_bytes=64, name="w_codes")
-            if b == 1:
-                w_scales = staged((3, 1), 4608, [P, NQ], U8, "w_scales1")
-            else:
-                w_scales = ring2.tile([P, NQ], U8, align_bytes=64, name="w_scales")
+            w_scales = placed("w_scales", b, [P, NQ], U8, ring2)
             nc.vector.quantize_mx(
                 out=w_codes[:].bitcast(FP8X4), scales=w_scales[:], in_=w_grp[b][:].rearrange("s q t -> s (q t)")
             )
             weights[b] = w_codes, w_scales
-            acc[b] = []
 
-        def multiply(b, i=0, pieces=1):
-            w_codes, w_scales = weights[b]
-            w = D // pieces
-            if True:
-                bank = psum2.tile([P, w], F32, tag="acc", name=f"acc{b}{i}") if i == 0 else psum2.tile([P, w], F32, tag="scores", name=f"acc{b}{i}")
-                nc.tensor.matmul_mx(
-                    out=bank[:],
-                    lhsT=w_codes[:].bitcast(FP8X4),
-                    lhsT_scale=w_scales[:],
-                    rhs=v_codes[b][:, i * w : (i + 1) * w].bitcast(FP8X4),
-                    rhs_scale=v_scales[b][:, i * w : (i + 1) * w],
-                    start=True,
-                    stop=True,
-                )
-                acc[b].append(bank)
-
-        def finish(b, i=0, pieces=1):
-            if i == 0:
-                if b == 0:
-                    ys[b] = staged((3, 0), 2048, [P, D], F32, f"y{b}")
-                elif b == 1:
-                    ys[b] = staged(*LATE[b + 1], [P, D], F32, f"y{b}")
-                else:
-                    ys[b] = ring2.tile([P, D], F32, name="y")
-            y, bank = ys[b], acc[b][i]
-            w = D // pieces
-            if True:
-                cols = slice(i * w, (i + 1) * w)
-                nc.vector.scalar_tensor_tensor(
-                    out=y[:, cols], in0=bank[:], scalar=1.0 / 16.0, in1=chans[:, cols], op0=MULT, op1=MULT
-                )
-                nc.sync.dma_start(out[b][:, cols], y[:, cols])
-
-        gather_tokens(0, 1, ("kb", "ts"))
+        gather_tokens("kb", 0, 1)
+        gather_tokens("ts", 0, 1)
         cast(0, 0)
         cast(0, 1)
         cast(1, 0)
-        cast(1, 1)
         gather(0, 0)
         turn(0, 0)
-        gather_tokens(1, B - 1, ("kb",), ((0, 0), 0))
+        copy_values(0, 0)
+        cast(1, 1)
+        gather_tokens("kb", 1, LAST)
         gather(0, 1)
         turn(0, 1)
         weave(0)
-        gather_tokens(1, B - 1, ("ts",), ((0, 1), 0))
-        cast_queries()
+        gather_tokens("ts", 1, LAST)
+        cast_queries(0)
         gather(1, 0)
         gather(1, 1)
         turn(1, 0)
         turn(1, 1)
         quantize_keys(0)
-        values_out(0, 0)
-        values_out(0, 1)
-        values(0)
-        quantize_queries()
+        copy_values(0, 1)
+        quantize_values(0)
+        quantize_queries(0)
         score(0)
         weave(1)
-        cast(2, 0)
-        gather(2, 0)
+        cast_queries(1)
+
+        for u in range(2):
+            cast(2, u)
+            gather(2, u)
         quantize_keys(1)
         score(1)
-        cast(2, 1)
-        gather(2, 1)
         turn(2, 0)
         turn(2, 1)
         weave(2)
-        gather_tokens(B - 1, B, ("kb",), ((2, 1), 64))
-        gather_tokens(B - 1, B, ("ts",), ((2, 0), 6208))
-        values_out(1, 0)
-        values_out(1, 1)
+        gather_tokens("kb", LAST, B)
+        gather_tokens("ts", LAST, B)
         turn_tokens(0, 2)
         turn_tokens(2, B)
-        quantize_keys(2)
-        values(1)
         weigh(0)
+        copy_values(1, 0)
+        copy_values(1, 1)
+        quantize_queries(1)
+        quantize_keys(2)
+        quantize_values(1)
         score(2)
-        product(0)
+        quantize_weights(0)
         multiply(0)
-        cast(3, 0)
-        gather(3, 0)
-        turn(3, 0)
+
+        cast(LAST, 0)
+        gather(LAST, 0)
+        turn(LAST, 0)
         finish(0)
         weigh(1)
-        cast(3, 1)
-        gather(3, 1)
-        turn(3, 1)
-        product(1)
+        cast(LAST, 1)
+        gather(LAST, 1)
+        turn(LAST, 1)
+        quantize_weights(1)
         multiply(1)
-        weave(3)
-        quantize_keys(3)
-        score(3)
-        values_out(2, 0)
-        values_out(2, 1)
-        values(2)
+        weave(LAST)
+        quantize_keys(LAST)
+        score(LAST)
+
+        copy_values(2, 0)
+        copy_values(2, 1)
+        quantize_values(2)
         weigh(2)
         finish(1)
-        product(2)
+        quantize_weights(2)
         multiply(2)
-        weigh(3)
+        weigh(LAST)
         finish(2)
-        product(3)
+        quantize_weights(LAST)
         for h in range(2):
-            values_out(3, 0, h, 2)
-            values_out(3, 1, h, 2)
-            values(3, h, 2)
-            multiply(3, h, 2)
+            copy_values(LAST, 0, h, 2)
+            copy_values(LAST, 1, h, 2)
+            quantize_values(LAST, h, 2)
+            multiply(LAST, h, 2)
         for h in range(2):
-            finish(3, h, 2)
+            finish(LAST, h, 2)

@@ -28,23 +28,29 @@ HALF_AREA = AREA // 2
 REUSE = {
     "row_kb1": ((0, 0), 0),
     "row_ts1": ((0, 1), 0),
-    "row_kb3": ((2, 1), 64),
+    "row_kb3": ((2, 0), 4096),
     "row_ts3": ((2, 0), 6208),
-    "v_grp0": ((1, 0), HALF_AREA),
-    "v_grp1": ((2, 1), HALF_AREA),
-    "v_grp2": ((3, 1), 0),
-    "v_grp3": ((1, 0), 0),
+    "v_grp0": ((0, 0), HALF_AREA),
+    "words0": ((0, 1), HALF_AREA),
+    "k_grp0": ((0, 1), HALF_AREA),
+    "words1": ((1, 0), 0),
+    "v_grp1": ((2, 0), 0),
+    "v_grp2": ((3, 1), 64),
+    "v_grp3": ((3, 1), 6912),
     "columns0": ((2, 1), 2112),
-    "columns2": ((3, 1), HALF_AREA),
-    "p1": ((3, 0), 0),
+    "columns2": ((3, 1), 4160),
+    "p1": ((3, 1), 4352),
+    "v_scales1": ((3, 1), 6400),
+    "p3": ((2, 1), HALF_AREA),
+    "y2": ((2, 1), HALF_AREA),
     "k_codes0": ((1, 1), HALF_AREA),
     "k_scales1": ((2, 1), 2240),
-    "w_scales1": ((3, 1), 4608),
-    "y0": ((3, 0), 2048),
-    "y1": ((3, 1), 0),
+    "w_scales1": ((3, 1), 4224),
+    "y0": ((3, 0), 6208),
+    "y1": ((3, 1), 64),
     "k_grp1": ("g", 0),
-    "w_grp0": ("q", 0),
-    "w_grp1": ("q", 0),
+    "w_grp0": ("q", 3072),
+    "w_grp1": ("q", 3072),
 }
 
 F32 = mybir.dt.float32
@@ -93,11 +99,11 @@ def tile_attend_x_mla_sigmoid_seg_kernel(tc, qT, cT, ts, kb, ch, offs, out):
         q_raw = [staged("q", HALF_AREA * h, [P, 2, LANES, NQ], F32, f"q_raw{h}") for h in range(2)]
         chans = keep.tile([P, D], F32, name="chans")
 
-        nc.vector.memset(windows["kb"][:, 0 : SEG + 1], 0.0)
-        nc.gpsimd.memset(windows["ts"][:, 0 : SEG + 1], 0.0)
-        nc.vector.memset(windows["kb"][:, SEG + 1 : KB_SPLIT], 0.0)
-        nc.gpsimd.memset(windows["kb"][:, KB_SPLIT:T], 0.0)
-        nc.gpsimd.memset(windows["ts"][:, SEG + 1 : T], 0.0)
+        nc.gpsimd.memset(windows["kb"][:, 0:SEG], 0.0)
+        nc.vector.memset(windows["ts"][:, 0 : SEG + 1], 0.0)
+        nc.gpsimd.memset(windows["kb"][:, SEG:T], 0.0)
+        nc.vector.memset(windows["ts"][:, SEG + 1 : KB_SPLIT], 0.0)
+        nc.gpsimd.memset(windows["ts"][:, KB_SPLIT:T], 0.0)
         ident = keep.tile([P, P], F32, name="ident")
         make_identity(nc, ident[:])
 
@@ -112,8 +118,8 @@ def tile_attend_x_mla_sigmoid_seg_kernel(tc, qT, cT, ts, kb, ch, offs, out):
             source = {"kb": kb, "ts": ts}[name]
             nc.sync.dma_start(windows[name][row : row + 1, c0:c1], source[0:1, c0:c1])
 
-        def load_pool(b, u):
-            for c0, c1 in token_ranges(b, u):
+        def load_pool(b, u, parts=slice(0, 2)):
+            for c0, c1 in token_ranges(b, u)[parts]:
                 nc.sync.dma_start(raw[b, u][:, :, c0:c1], cT_view[:, 2 * u : 2 * u + 2, b * SEG + c0 : b * SEG + c1])
 
         def load_queries(h):
@@ -122,8 +128,9 @@ def tile_attend_x_mla_sigmoid_seg_kernel(tc, qT, cT, ts, kb, ch, offs, out):
                 qT.rearrange("b (p j) q -> p b (j q)", j=LANES)[:, 2 * h : 2 * h + 2],
             )
 
-        load_pool(0, 0)
+        load_pool(0, 0, slice(0, 1))
         load_row("kb", 0, SEG)
+        load_pool(0, 0, slice(1, 2))
         load_row("ts", 0, SEG)
         load_pool(0, 1)
         load_row("kb", SEG, T)
@@ -174,8 +181,8 @@ def tile_attend_x_mla_sigmoid_seg_kernel(tc, qT, cT, ts, kb, ch, offs, out):
             for b in range(n):
                 tokens[b0 + b] = columns[:, :, b, :]
 
-        def cast(b, u):
-            for c0, c1 in token_ranges(b, u):
+        def cast(b, u, parts=slice(0, 2)):
+            for c0, c1 in token_ranges(b, u)[parts]:
                 nc.scalar.activation(
                     pool[u][:, 2 * (b * SEG + c0) : 2 * (b * SEG + c1)].rearrange("p (w e) -> p w e", e=2),
                     raw[b, u][:, :, c0:c1].rearrange("p e w -> p w e"),
@@ -245,10 +252,24 @@ def tile_attend_x_mla_sigmoid_seg_kernel(tc, qT, cT, ts, kb, ch, offs, out):
                 turned[b, u][:].bitcast(BF16).rearrange("s t (m e) -> s m e t", e=2)[:, ms],
             )
 
+        def copy_words(b, u):
+            if u == 0:
+                v_grp[b] = placed("v_grp", b, [P, D * LANES], BF16, keep)
+            words = placed("words", u, [P, LANES, P], F32, keep)
+            nc.scalar.copy(words[:], turned[b, u][:])
+            nc.gpsimd.tensor_scalar(
+                v_grp[b][:].rearrange("s (m u e t) -> s u m e t", u=2, e=2, t=LANES)[:, u],
+                words[:].bitcast(BF16).rearrange("s t (m e) -> s m e t", e=2),
+                1.0,
+                0.0,
+                MULT,
+                ADD,
+            )
+
         def quantize_values(b, h=0, parts=1):
             if h == 0:
                 v_codes = ring3.tile([P, D], U32, align_bytes=64, name="v_codes")
-                v_scales = ring3.tile([P, D], U8, align_bytes=64, name="v_scales")
+                v_scales = placed("v_scales", b, [P, D], U8, ring3)
                 values[b] = v_codes, v_scales
             v_codes, v_scales = values[b]
             d0, d1 = h * D // parts, (h + 1) * D // parts
@@ -282,9 +303,12 @@ def tile_attend_x_mla_sigmoid_seg_kernel(tc, qT, cT, ts, kb, ch, offs, out):
             )
             nc.sync.dma_start(out[b][:, cols], ys[b][:, cols])
 
-        def weigh(b):
+        ps = {}
+
+        def sigmoid(b):
             bias, scale = tokens[b][:, 0, :], tokens[b][:, 1, :]
             p = placed("p", b, [P, LANES, NQ], F32, ring2, align=None)
+            ps[b] = p
             for t in range(LANES):
                 nc.scalar.activation(
                     p[:, t, :],
@@ -293,6 +317,9 @@ def tile_attend_x_mla_sigmoid_seg_kernel(tc, qT, cT, ts, kb, ch, offs, out):
                     bias=bias[:, t : t + 1],
                     scale=scale[:, t : t + 1],
                 )
+
+        def weigh(b):
+            p, scale = ps[b], tokens[b][:, 1, :]
             w_grp[b] = placed("w_grp", b, [P, NQ, LANES], BF16, ring2)
             engine = nc.gpsimd if b < ON_GPSIMD else nc.vector
             engine.tensor_tensor(
@@ -314,15 +341,18 @@ def tile_attend_x_mla_sigmoid_seg_kernel(tc, qT, cT, ts, kb, ch, offs, out):
         gather_tokens("ts", 0, 1)
         cast(0, 0)
         cast(0, 1)
-        cast(1, 0)
+        cast(1, 0, slice(0, 1))
         gather(0, 0)
         turn(0, 0)
-        copy_values(0, 0)
-        cast(1, 1)
+        copy_words(0, 0)
+        cast(1, 0, slice(1, 2))
+        cast(1, 1, slice(0, 1))
         gather_tokens("kb", 1, LAST)
         gather(0, 1)
         turn(0, 1)
         weave(0)
+        copy_words(0, 1)
+        cast(1, 1, slice(1, 2))
         gather_tokens("ts", 1, LAST)
         cast_queries(0)
         gather(1, 0)
@@ -330,16 +360,17 @@ def tile_attend_x_mla_sigmoid_seg_kernel(tc, qT, cT, ts, kb, ch, offs, out):
         turn(1, 0)
         turn(1, 1)
         quantize_keys(0)
-        copy_values(0, 1)
         quantize_values(0)
         quantize_queries(0)
         score(0)
         weave(1)
         cast_queries(1)
 
-        for u in range(2):
-            cast(2, u)
-            gather(2, u)
+        cast(2, 0)
+        gather(2, 0)
+        copy_values(1, 0)
+        cast(2, 1)
+        gather(2, 1)
         quantize_keys(1)
         score(1)
         turn(2, 0)
@@ -349,44 +380,47 @@ def tile_attend_x_mla_sigmoid_seg_kernel(tc, qT, cT, ts, kb, ch, offs, out):
         gather_tokens("ts", LAST, B)
         turn_tokens(0, 2)
         turn_tokens(2, B)
+        sigmoid(0)
         weigh(0)
-        copy_values(1, 0)
         copy_values(1, 1)
         quantize_queries(1)
         quantize_keys(2)
-        quantize_values(1)
         score(2)
         quantize_weights(0)
         multiply(0)
-
-        cast(LAST, 0)
-        gather(LAST, 0)
-        turn(LAST, 0)
-        finish(0)
+        cast(3, 0)
+        gather(3, 0)
+        turn(3, 0)
+        cast(3, 1)
+        gather(3, 1)
+        turn(3, 1)
+        sigmoid(1)
         weigh(1)
-        cast(LAST, 1)
-        gather(LAST, 1)
-        turn(LAST, 1)
+        finish(0)
+        weave(3)
+        quantize_values(1)
+        quantize_keys(3)
+        score(3)
         quantize_weights(1)
         multiply(1)
-        weave(LAST)
-        quantize_keys(LAST)
-        score(LAST)
-
         copy_values(2, 0)
+        sigmoid(2)
+        weigh(2)
         copy_values(2, 1)
         quantize_values(2)
-        weigh(2)
-        finish(1)
         quantize_weights(2)
+        finish(1)
         multiply(2)
-        weigh(LAST)
+        copy_values(3, 0)
+        sigmoid(3)
+        weigh(3)
+        copy_values(3, 1, 0, 2)
+        quantize_values(3, 0, 2)
+        quantize_weights(3)
+        multiply(3, 0, 2)
+        copy_values(3, 1, 1, 2)
+        quantize_values(3, 1, 2)
+        multiply(3, 1, 2)
         finish(2)
-        quantize_weights(LAST)
-        for h in range(2):
-            copy_values(LAST, 0, h, 2)
-            copy_values(LAST, 1, h, 2)
-            quantize_values(LAST, h, 2)
-            multiply(LAST, h, 2)
-        for h in range(2):
-            finish(LAST, h, 2)
+        finish(3, 0, 2)
+        finish(3, 1, 2)

@@ -49,9 +49,19 @@ REUSE = {
     "y0": ((3, 0), 6208),
     "y1": ((3, 1), 64),
     "k_grp1": ("g", 0),
-    "w_grp0": ("q", 3072),
-    "w_grp1": ("q", 3072),
+    "k_grp2": ("g", 0),
+    "q_scales1": ((2, 1), 2752),
+    "w_scales0": ((3, 0), 0),
+    "w_grp0": ("g", 0),
+    "w_grp1": ("g", 0),
 }
+
+BANK = {
+    "turned00": 0, "turned01": 1, "turned10": 2, "turned11": 3, "bank0": 4, "scores0": 6, "turned20": 0,
+    "turned21": 1, "bank2": 2, "scores1": 7, "scores2": 6, "turned30": 5, "acc00": 4, "turned31": 3,
+    "scores3": 7, "acc10": 2, "acc20": 4, "acc30": 2, "acc31": 6,
+}
+QUERY_GROUPS = ((0, 1), (1, B))
 
 F32 = mybir.dt.float32
 BF16 = mybir.dt.bfloat16
@@ -73,8 +83,10 @@ def tile_attend_x_mla_sigmoid_seg_kernel(tc, qT, cT, ts, kb, ch, offs, out):
         stage = ctx.enter_context(tc.tile_pool(name="stage", bufs=1))
         ring3 = ctx.enter_context(tc.tile_pool(name="ring3", bufs=3))
         ring2 = ctx.enter_context(tc.tile_pool(name="ring2", bufs=2))
-        psum2 = ctx.enter_context(tc.psum_pool(name="psum2", bufs=2))
-        psum4 = ctx.enter_context(tc.psum_pool(name="psum4", bufs=4))
+        psum = ctx.enter_context(tc.psum_pool(name="psum", bufs=1))
+
+        def in_bank(name, shape):
+            return psum.tile(shape, F32, offset=2048 * BANK[name], name=name)
 
         def staged(area, offset, shape, dtype, name):
             index = {"q": 2 * B, "g": 2 * B + 1}[area] if area in ("q", "g") else 2 * area[0] + area[1]
@@ -96,7 +108,9 @@ def tile_attend_x_mla_sigmoid_seg_kernel(tc, qT, cT, ts, kb, ch, offs, out):
 
         windows = {name: keep.tile([P, T], F32, name="window_" + name) for name in ("kb", "ts")}
         raw = {(b, u): staged((b, u), 0, [P, 2, SEG], F32, f"raw{b}{u}") for b in range(B) for u in range(2)}
-        q_raw = [staged("q", HALF_AREA * h, [P, 2, LANES, NQ], F32, f"q_raw{h}") for h in range(2)]
+        q_raw = [
+            staged("q", b0 * LANES * NQ * 4, [P, b1 - b0, LANES, NQ], F32, f"q_raw{b0}") for b0, b1 in QUERY_GROUPS
+        ]
         chans = keep.tile([P, D], F32, name="chans")
 
         nc.gpsimd.memset(windows["kb"][:, 0:SEG], 0.0)
@@ -125,7 +139,7 @@ def tile_attend_x_mla_sigmoid_seg_kernel(tc, qT, cT, ts, kb, ch, offs, out):
         def load_queries(h):
             nc.sync.dma_start(
                 q_raw[h][:].rearrange("p b j q -> p b (j q)"),
-                qT.rearrange("b (p j) q -> p b (j q)", j=LANES)[:, 2 * h : 2 * h + 2],
+                qT.rearrange("b (p j) q -> p b (j q)", j=LANES)[:, slice(*QUERY_GROUPS[h])],
             )
 
         load_pool(0, 0, slice(0, 1))
@@ -143,9 +157,11 @@ def tile_attend_x_mla_sigmoid_seg_kernel(tc, qT, cT, ts, kb, ch, offs, out):
             load_pool(2 + h, 1)
         nc.sync.dma_start(chans[:], ch)
 
-        q_grp = [staged("g", HALF_AREA * h, [P, 2 * NQ * LANES], BF16, f"q_grp{h}") for h in range(2)]
-        q_codes = keep.tile([P, B * NQ], U32, align_bytes=64, name="q_codes")
-        q_scales = keep.tile([P, B * NQ], U8, align_bytes=64, name="q_scales")
+        q_grp = [
+            staged("g", HALF_AREA * h, [P, (b1 - b0) * NQ * LANES], BF16, f"q_grp{h}")
+            for h, (b0, b1) in enumerate(QUERY_GROUPS)
+        ]
+        queries = {}
 
         pool = [keep.tile([P, 2 * T], BF16, name=f"pool{u}") for u in range(2)]
         rows, tokens, picked, turned = {}, {}, {}, {}
@@ -166,20 +182,20 @@ def tile_attend_x_mla_sigmoid_seg_kernel(tc, qT, cT, ts, kb, ch, offs, out):
 
         def turn_tokens(b0, b1):
             n = b1 - b0
-            bank = psum2.tile([P, 512], F32, tag="acc", name=f"bank{b0}")
-            for i, name in enumerate(("kb", "ts")):
-                for b in range(b0, b1):
+            bank = in_bank(f"bank{b0}", [P, 512])
+            for b in range(b0, b1):
+                for i, name in enumerate(("kb", "ts")):
                     for t in range(LANES):
-                        c = (i * n + b - b0) * LANES + t
+                        c = (2 * (b - b0) + i) * LANES + t
                         c0 = PITCH * (c + 1) - 2 - ROW[name, min(b, 1)]
                         nc.tensor.transpose(bank[:, c0 : c0 + P], rows[name, b][:, t * P : (t + 1) * P], ident[:])
-            columns = placed("columns", b0, [P, 2, n, LANES], F32, keep)
+            columns = placed("columns", b0, [P, n, 2, LANES], F32, keep)
             nc.scalar.copy(
-                columns[:].rearrange("s i b t -> s (i b t)"),
+                columns[:].rearrange("s b i t -> s (b i t)"),
                 bank[:, 0 : PITCH * 2 * LANES * n].rearrange("s (c z) -> s c z", z=PITCH)[:, :, PITCH - 2],
             )
             for b in range(n):
-                tokens[b0 + b] = columns[:, :, b, :]
+                tokens[b0 + b] = columns[:, b]
 
         def cast(b, u, parts=slice(0, 2)):
             for c0, c1 in token_ranges(b, u)[parts]:
@@ -208,18 +224,29 @@ def tile_attend_x_mla_sigmoid_seg_kernel(tc, qT, cT, ts, kb, ch, offs, out):
 
         def turn(b, u):
             words = picked[b][:].bitcast(F32).rearrange("p (u t s) -> p u t s", t=LANES, u=2)
-            turned[b, u] = psum4.tile([P, LANES, P], F32, tag="turned", name=f"turned{b}{u}")
+            turned[b, u] = in_bank(f"turned{b}{u}", [P, LANES, P])
             for t in range(LANES):
                 nc.tensor.transpose(turned[b, u][:, t, :], words[:, u, t, :], ident[:])
 
         def cast_queries(h):
-            grouped = q_grp[h][:].rearrange("p (b q j) -> p b q j", b=2, j=LANES)
+            grouped = q_grp[h][:].rearrange("p (b q j) -> p b q j", q=NQ, j=LANES)
             planes = q_raw[h][:].rearrange("p b j q -> p b q j")
             nc.gpsimd.tensor_scalar(grouped, planes, 1.0, 0.0, MULT, ADD)
 
         def quantize_queries(h):
-            cols = slice(2 * h * NQ, 2 * (h + 1) * NQ)
-            nc.vector.quantize_mx(out=q_codes[:, cols].bitcast(FP8X4), scales=q_scales[:, cols], in_=q_grp[h][:])
+            b0, b1 = QUERY_GROUPS[h]
+            q_codes = placed("q_codes", h, [P, (b1 - b0) * NQ], U32, keep)
+            q_scales = placed("q_scales", h, [P, (b1 - b0) * NQ], U8, keep)
+            for c0, c1 in ((0, NQ), (NQ, (b1 - b0) * NQ)):
+                if c1 > c0:
+                    nc.vector.quantize_mx(
+                        out=q_codes[:, c0:c1].bitcast(FP8X4),
+                        scales=q_scales[:, c0:c1],
+                        in_=q_grp[h][:, c0 * LANES : c1 * LANES],
+                    )
+            for b in range(b0, b1):
+                cols = slice((b - b0) * NQ, (b - b0 + 1) * NQ)
+                queries[b] = q_codes[:, cols], q_scales[:, cols]
 
         def quantize_keys(b):
             k_codes = placed("k_codes", b, [P, N], U32, keep)
@@ -228,16 +255,16 @@ def tile_attend_x_mla_sigmoid_seg_kernel(tc, qT, cT, ts, kb, ch, offs, out):
             keys[b] = k_codes, k_scales
 
         def score(b):
-            cols = slice(b * NQ, (b + 1) * NQ)
+            q_codes, q_scales = queries[b]
             k_codes, k_scales = keys[b]
-            scores[b] = psum2.tile([P, LANES, NQ], F32, tag="scores", name="scores")
+            scores[b] = in_bank(f"scores{b}", [P, LANES, NQ])
             for t in range(LANES):
                 nc.tensor.matmul_mx(
                     out=scores[b][:, t, :],
                     lhsT=k_codes[:, t * P : (t + 1) * P].bitcast(FP8X4),
                     lhsT_scale=k_scales[:, t * P : (t + 1) * P],
-                    rhs=q_codes[:, cols].bitcast(FP8X4),
-                    rhs_scale=q_scales[:, cols],
+                    rhs=q_codes.bitcast(FP8X4),
+                    rhs_scale=q_scales,
                     start=True,
                     stop=True,
                 )
@@ -283,7 +310,7 @@ def tile_attend_x_mla_sigmoid_seg_kernel(tc, qT, cT, ts, kb, ch, offs, out):
             w_codes, w_scales = weights[b]
             v_codes, v_scales = values[b]
             d0, d1 = h * D // parts, (h + 1) * D // parts
-            acc[b, h] = psum2.tile([P, d1 - d0], F32, tag=("acc", "scores")[h], name=f"acc{b}{h}")
+            acc[b, h] = in_bank(f"acc{b}{h}", [P, d1 - d0])
             nc.tensor.matmul_mx(
                 out=acc[b, h][:],
                 lhsT=w_codes[:].bitcast(FP8X4),
@@ -372,7 +399,6 @@ def tile_attend_x_mla_sigmoid_seg_kernel(tc, qT, cT, ts, kb, ch, offs, out):
         cast(2, 1)
         gather(2, 1)
         quantize_keys(1)
-        score(1)
         turn(2, 0)
         turn(2, 1)
         weave(2)
@@ -381,16 +407,17 @@ def tile_attend_x_mla_sigmoid_seg_kernel(tc, qT, cT, ts, kb, ch, offs, out):
         turn_tokens(0, 2)
         turn_tokens(2, B)
         sigmoid(0)
-        weigh(0)
         copy_values(1, 1)
         quantize_queries(1)
+        score(1)
         quantize_keys(2)
         score(2)
-        quantize_weights(0)
-        multiply(0)
+        weigh(0)
         cast(3, 0)
         gather(3, 0)
         turn(3, 0)
+        quantize_weights(0)
+        multiply(0)
         cast(3, 1)
         gather(3, 1)
         turn(3, 1)

@@ -101,11 +101,6 @@ def tile_attend_x_mla_sigmoid_seg_kernel(tc, qT, cT, ts, kb, ch, offs, out):
         lists = keep.tile([P, B * N // 16], U16, name="lists")
         nc.sync.dma_start(lists[:], offs)
 
-        warm = keep.tile([P, 1], F32, name="warm")
-        nc.gpsimd.memset(warm[:], 0.0)
-        warm_out = keep.tile([P, 1], F32, name="warm_out")
-        nc.scalar.activation(warm_out[:], warm[:], SIGMOID)
-
         windows = {name: keep.tile([P, T], F32, name="window_" + name) for name in ("kb", "ts")}
         raw = {(b, u): staged((b, u), 0, [P, 2, SEG], F32, f"raw{b}{u}") for b in range(B) for u in range(2)}
         q_raw = [

@@ -7,66 +7,16 @@ B, N, T, D, NQ = 4, 512, 4096, 512, 128
 P = 128
 SEG = T // B
 LANES = 4
-RUN = 8
 LINE = 4
 LIST_COLUMNS = N // 16
 LAST = B - 1
-ON_GPSIMD = 2
 
 FLOPS = B * 2 * (2 * N * D * NQ)
 BYTES = 4 * (B * D * NQ + D * T + 2 * T + D + B * NQ * D) + 2 * P * (B * N // 16)
 
-HALVED = ((0, 0), (0, 1), (1, 0), (1, 1), (2, 0), (2, 1), (3, 1))
-
-KB_SPLIT = 2 * SEG + 264
-
-ROW = {("kb", 0): 0, ("ts", 0): 4, ("kb", 1): 8, ("ts", 1): 0}
-PITCH = 10
-
-AREA = 2 * SEG * 4
-HALF_AREA = AREA // 2
-REUSE = {
-    "row_kb1": ((0, 0), 0),
-    "row_ts1": ((0, 1), 0),
-    "row_kb3": ((2, 0), 4096),
-    "row_ts3": ((2, 0), 6208),
-    "v_grp0": ((0, 0), HALF_AREA),
-    "words0": ((0, 1), HALF_AREA),
-    "k_grp0": ((0, 1), HALF_AREA),
-    "words1": ((1, 0), 0),
-    "v_grp1": ((2, 0), 0),
-    "v_grp2": ((3, 1), 64),
-    "v_grp3": ((3, 1), 6912),
-    "columns0": ((2, 1), 2112),
-    "columns2": ((3, 1), 4160),
-    "p1": ((3, 1), 4352),
-    "v_scales1": ((3, 1), 6400),
-    "p3": ((2, 1), HALF_AREA),
-    "y2": ((2, 1), HALF_AREA),
-    "k_codes0": ((1, 1), HALF_AREA),
-    "k_scales1": ((2, 1), 2240),
-    "w_scales1": ((3, 1), 4224),
-    "y0": ((3, 0), 6208),
-    "y1": ((3, 1), 64),
-    "k_grp1": ("g", 0),
-    "k_grp2": ("g", 0),
-    "q_scales1": ((2, 1), 2752),
-    "w_scales0": ((3, 0), 0),
-    "w_grp0": ("g", 0),
-    "w_grp1": ("g", 0),
-}
-
-BANK = {
-    "turned00": 0, "turned01": 1, "turned10": 2, "turned11": 3, "bank0": 4, "scores0": 6, "turned20": 0,
-    "turned21": 1, "bank2": 2, "scores1": 7, "scores2": 6, "turned30": 5, "acc00": 4, "turned31": 3,
-    "scores3": 7, "acc10": 2, "acc20": 4, "acc30": 2, "acc31": 6,
-}
-QUERY_GROUPS = ((0, 1), (1, B))
-
 F32 = mybir.dt.float32
 BF16 = mybir.dt.bfloat16
 U32 = mybir.dt.uint32
-I32 = mybir.dt.int32
 U16 = mybir.dt.uint16
 U8 = mybir.dt.uint8
 FP8X4 = mybir.dt.float8_e4m3fn_x4
@@ -75,61 +25,85 @@ MULT = mybir.AluOpType.mult
 COPY = mybir.ActivationFunctionType.Copy
 SIGMOID = mybir.ActivationFunctionType.Sigmoid
 
+TS_SPLIT = 3 * SEG - 127
+ROW = {"kb": (0, 0, 8, 8), "ts": (4, 8, 8, 0)}
+PITCH = 10
+QUERY_GROUPS = ((0, B),)
+SLOT = SEG * 4
+
+WINDOW_SLOT = ((0, 1, 2, 3), (4, 6, 8, 10), (0, 12, 15, 18), (6, 21, 25, 0))
+WINDOW_AT = {(b, j): WINDOW_SLOT[b][j] * SLOT for b in range(B) for j in range(LANES)}
+REUSE = {
+    "q_scales0": ((1, 0), 0),
+    "v_scales0": ((1, 0), 512),
+    "v_grp0": (29, 0),
+    "k_grp1": (29, 0),
+    "p0": ((1, 3), 2048),
+    "v_scales1": ((2, 2), 0),
+    "w_grp0": (30, 0),
+    "k_grp2": (30, 0),
+    "v_grp2": ((2, 3), 0),
+    "p1": ((3, 0), 0),
+    "k_scales2": ((3, 2), 0),
+    "w_grp1": ((3, 3), 0),
+    "v_scales2": ((3, 3), 1024),
+    "p2": ((3, 3), 2048),
+    "v_grp3": ((3, 3), 4096),
+}
+BANK = {"turned00": 0, "turned01": 1, "turned10": 2, "turned11": 3, "turned20": 0, "turned21": 1, "turned30": 2, "turned31": 3, "bank0": 1, "bank2": 2, "scores00": 6, "scores10": 7, "scores20": 6, "scores30": 7, "acc00": 5, "acc10": 4, "acc20": 5, "acc30": 4, "acc31": 6}
+
 
 def tile_attend_x_mla_sigmoid_seg_kernel(tc, qT, cT, ts, kb, ch, offs, out):
     nc = tc.nc
     with ExitStack() as ctx:
         keep = ctx.enter_context(tc.tile_pool(name="keep", bufs=1))
         stage = ctx.enter_context(tc.tile_pool(name="stage", bufs=1))
-        ring3 = ctx.enter_context(tc.tile_pool(name="ring3", bufs=3))
-        ring2 = ctx.enter_context(tc.tile_pool(name="ring2", bufs=2))
+        ring = ctx.enter_context(tc.tile_pool(name="ring", bufs=2))
         psum = ctx.enter_context(tc.psum_pool(name="psum", bufs=1))
 
         def in_bank(name, shape):
             return psum.tile(shape, F32, offset=2048 * BANK[name], name=name)
 
-        def staged(area, offset, shape, dtype, name):
-            index = {"q": 2 * B, "g": 2 * B + 1}[area] if area in ("q", "g") else 2 * area[0] + area[1]
-            return stage.tile(shape, dtype, align_bytes=64, offset=index * AREA + offset, name=name)
-
-        def placed(kind, b, shape, dtype, home, align=64):
+        def placed(kind, b, shape, dtype, home):
             name = f"{kind}{b}"
             if name in REUSE:
-                return staged(*REUSE[name], shape, dtype, name)
-            return home.tile(shape, dtype, align_bytes=align, name=name if home is keep else kind)
+                piece, offset = REUSE[name]
+                return stage.tile(shape, dtype, align_bytes=64, offset=(WINDOW_AT[piece] if piece in WINDOW_AT else piece * SLOT) + offset, name=name)
+            return home.tile(shape, dtype, align_bytes=64, name=name if home is keep else kind)
 
         lists = keep.tile([P, B * N // 16], U16, name="lists")
         nc.sync.dma_start(lists[:], offs)
 
         windows = {name: keep.tile([P, T], F32, name="window_" + name) for name in ("kb", "ts")}
-        raw = {(b, u): staged((b, u), 0, [P, 2, SEG], F32, f"raw{b}{u}") for b in range(B) for u in range(2)}
-        q_raw = [
-            staged("q", b0 * LANES * NQ * 4, [P, b1 - b0, LANES, NQ], F32, f"q_raw{b0}") for b0, b1 in QUERY_GROUPS
-        ]
+        planes = {
+            (b, j): stage.tile([P, (b + 1) * SEG], F32, align_bytes=64, offset=WINDOW_AT[b, j], name=f"plane{b}{j}")
+            for b in range(B)
+            for j in range(LANES)
+        }
+        q_raw = [placed("q_raw", b0, [P, b1 - b0, LANES, NQ], F32, keep) for b0, b1 in QUERY_GROUPS]
         chans = keep.tile([P, D], F32, name="chans")
-
-        nc.gpsimd.memset(windows["kb"][:, 0:SEG], 0.0)
-        nc.vector.memset(windows["ts"][:, 0 : SEG + 1], 0.0)
-        nc.gpsimd.memset(windows["kb"][:, SEG:T], 0.0)
-        nc.vector.memset(windows["ts"][:, SEG + 1 : KB_SPLIT], 0.0)
-        nc.gpsimd.memset(windows["ts"][:, KB_SPLIT:T], 0.0)
         ident = keep.tile([P, P], F32, name="ident")
+
+        warm = keep.tile([P, 2], F32, name="warm")
+        nc.vector.memset(warm[:, 0:1], 0.0)
+        nc.scalar.activation(warm[:, 1:2], warm[:, 0:1], SIGMOID)
+        nc.vector.memset(windows["ts"][:, 0 : SEG + 1], 0.0)
+        nc.gpsimd.memset(windows["kb"][:, 0 : 2 * SEG], 0.0)
+        nc.vector.memset(windows["ts"][:, SEG + 1 : 3 * SEG], 0.0)
+        nc.gpsimd.memset(windows["kb"][:, 2 * SEG : T], 0.0)
+        nc.gpsimd.memset(windows["ts"][:, 3 * SEG : T], 0.0)
         make_identity(nc, ident[:])
 
         cT_view = cT.rearrange("(p j) w -> p j w", j=LANES)
 
-        def token_ranges(b, u):
-            width = SEG // 2 if (b, u) in HALVED else SEG
-            return [(c0, c0 + width) for c0 in range(0, SEG, width)]
-
         def load_row(name, c0, c1):
-            row = ROW[name, c0 // SEG]
+            row = ROW[name][c0 // SEG]
             source = {"kb": kb, "ts": ts}[name]
             nc.sync.dma_start(windows[name][row : row + 1, c0:c1], source[0:1, c0:c1])
 
-        def load_pool(b, u, parts=slice(0, 2)):
-            for c0, c1 in token_ranges(b, u)[parts]:
-                nc.sync.dma_start(raw[b, u][:, :, c0:c1], cT_view[:, 2 * u : 2 * u + 2, b * SEG + c0 : b * SEG + c1])
+        def load_pool(b, j):
+            cols = slice(b * SEG, (b + 1) * SEG)
+            nc.sync.dma_start(planes[b, j][:, cols], cT_view[:, j, cols])
 
         def load_queries(h):
             nc.sync.dma_start(
@@ -137,169 +111,148 @@ def tile_attend_x_mla_sigmoid_seg_kernel(tc, qT, cT, ts, kb, ch, offs, out):
                 qT.rearrange("b (p j) q -> p b (j q)", j=LANES)[:, slice(*QUERY_GROUPS[h])],
             )
 
-        load_pool(0, 0, slice(0, 1))
-        load_row("kb", 0, SEG)
-        load_pool(0, 0, slice(1, 2))
-        load_row("ts", 0, SEG)
-        load_pool(0, 1)
-        load_row("kb", SEG, T)
-        load_pool(1, 0)
-        load_row("ts", SEG, T)
-        load_pool(1, 1)
-        for h in range(2):
-            load_queries(h)
-            load_pool(2 + h, 0)
-            load_pool(2 + h, 1)
-        nc.sync.dma_start(chans[:], ch)
+        def load_chans():
+            nc.sync.dma_start(chans[:], ch)
 
-        q_grp = [
-            staged("g", HALF_AREA * h, [P, (b1 - b0) * NQ * LANES], BF16, f"q_grp{h}")
-            for h, (b0, b1) in enumerate(QUERY_GROUPS)
-        ]
-        queries = {}
-
-        pool = [keep.tile([P, 2 * T], BF16, name=f"pool{u}") for u in range(2)]
-        rows, tokens, picked, turned = {}, {}, {}, {}
+        queries, rows, tokens, picked, turned, q_grp = {}, {}, {}, {}, {}, {}
         k_grp, keys, scores = {}, {}, {}
-        v_grp, values, w_grp, weights, acc, ys = {}, {}, {}, {}, {}, {}
+        v_grp, values, w_grp, weights, acc, ys, ps = {}, {}, {}, {}, {}, {}, {}
 
-        def gather_tokens(name, b0, b1):
-            n = b1 - b0
-            row = placed(f"row_{name}", b0, [P, n * N], F32, keep, align=None)
-            for b in range(n):
-                rows[name, b0 + b] = row[:, b * N : (b + 1) * N]
+        def offsets(b, h=0, parts=1):
+            width = LIST_COLUMNS // parts
+            return lists[:, b * LIST_COLUMNS + h * width : b * LIST_COLUMNS + (h + 1) * width]
+
+        def gather_tokens(name, b):
+            rows[name, b] = placed("row_" + name, b, [P, N], F32, keep)
             nc.vector.tensor_copy(
-                row[:].bitcast(U32).rearrange("p (b t g r) -> p b g t r", b=n, t=LANES, r=RUN),
-                windows[name][:].bitcast(U32)[:, 0 : b1 * SEG].indirect(
-                    lists[:, b0 * LIST_COLUMNS : b1 * LIST_COLUMNS]
-                ),
+                rows[name, b][:].bitcast(U32).rearrange("p (t s) -> p s t", t=LANES),
+                windows[name][:].bitcast(U32)[:, 0 : (b + 1) * SEG].indirect(offsets(b)),
             )
 
-        def turn_tokens(b0, b1):
+        def turn_tokens(b0, b1, engine):
             n = b1 - b0
             bank = in_bank(f"bank{b0}", [P, 512])
             for b in range(b0, b1):
                 for i, name in enumerate(("kb", "ts")):
                     for t in range(LANES):
                         c = (2 * (b - b0) + i) * LANES + t
-                        c0 = PITCH * (c + 1) - 2 - ROW[name, min(b, 1)]
+                        c0 = PITCH * (c + 1) - 2 - ROW[name][b]
                         nc.tensor.transpose(bank[:, c0 : c0 + P], rows[name, b][:, t * P : (t + 1) * P], ident[:])
             columns = placed("columns", b0, [P, n, 2, LANES], F32, keep)
-            nc.scalar.copy(
+            copy(
+                engine,
                 columns[:].rearrange("s b i t -> s (b i t)"),
                 bank[:, 0 : PITCH * 2 * LANES * n].rearrange("s (c z) -> s c z", z=PITCH)[:, :, PITCH - 2],
             )
             for b in range(n):
                 tokens[b0 + b] = columns[:, b]
 
-        def cast(b, u, parts=slice(0, 2)):
-            for c0, c1 in token_ranges(b, u)[parts]:
-                nc.scalar.activation(
-                    pool[u][:, 2 * (b * SEG + c0) : 2 * (b * SEG + c1)].rearrange("p (w e) -> p w e", e=2),
-                    raw[b, u][:, :, c0:c1].rearrange("p e w -> p w e"),
-                    COPY,
+        def copy(engine, to, source):
+            if engine is nc.scalar:
+                nc.scalar.copy(to, source)
+            else:
+                engine.tensor_copy(to, source)
+
+        def gather(b, j, engine, h=0, parts=1):
+            if b not in picked:
+                picked[b] = placed("picked", b, [P, LANES * N], BF16, ring)
+            width = N // parts
+            plane = picked[b][:, j * N + h * width : j * N + (h + 1) * width]
+            source = planes[b, j][:].indirect(offsets(b, h, parts))
+            if engine is nc.scalar:
+                nc.scalar.activation(plane, source, COPY)
+            else:
+                nc.vector.tensor_copy(plane, source)
+
+        def weave(b, engine, h=0, parts=1):
+            if b not in k_grp:
+                k_grp[b] = placed("k_grp", b, [P, N * LANES], BF16, ring)
+            lanes = slice(h * LANES // parts, (h + 1) * LANES // parts)
+            if engine is nc.gpsimd:
+                nc.gpsimd.tensor_scalar(
+                    k_grp[b][:].rearrange("p (t s j) -> p t s j", t=LANES, j=LANES)[:, lanes],
+                    picked[b][:].rearrange("p (j s t) -> p t s j", t=LANES, j=LANES)[:, lanes],
+                    1.0,
+                    0.0,
+                    MULT,
+                    ADD,
+                )
+            else:
+                copy(
+                    engine,
+                    k_grp[b][:].rearrange("p (t c s j) -> p c t s j", t=LANES, s=2, j=LANES)[:, :, lanes],
+                    picked[b][:].rearrange("p (j c s t) -> p c t s j", t=LANES, s=2, j=LANES)[:, :, lanes],
                 )
 
-        def gather(b, u):
-            if u == 0:
-                picked[b] = keep.tile([P, 2 * N], U32, name=f"picked{b}")
-            window = pool[u][:].bitcast(U32)[:, 0 : (b + 1) * SEG]
-            nc.vector.tensor_copy(
-                picked[b][:, u * N : (u + 1) * N].rearrange("p (t g r) -> p g t r", t=LANES, r=RUN),
-                window.indirect(lists[:, b * LIST_COLUMNS : (b + 1) * LIST_COLUMNS]),
+        def turn(b, j):
+            words = picked[b][:].bitcast(F32)
+            if j % 2 == 0:
+                turned[b, j // 2] = in_bank(f"turned{b}{j // 2}", [P, LANES, P])
+            w0 = j * N // 2
+            for h in range(2):
+                nc.tensor.transpose(
+                    turned[b, j // 2][:, 2 * (j % 2) + h, :], words[:, w0 + h : w0 + N // 2 : 2], ident[:]
+                )
+
+        def copy_values(b, u, engine):
+            if b not in v_grp:
+                v_grp[b] = placed("v_grp", b, [P, D * LANES], BF16, ring)
+            copy(
+                engine,
+                v_grp[b][:].bitcast(F32).rearrange("s (m u c) -> s u m c", u=2, c=LANES)[:, u],
+                turned[b, u][:].rearrange("s c m -> s m c"),
             )
 
-        def weave(b):
-            k_grp[b] = placed("k_grp", b, [P, N * LANES], BF16, ring3)
-            engine = nc.vector if b == LAST else nc.gpsimd
-            engine.tensor_copy(
-                k_grp[b][:].bitcast(I32).rearrange("p (c u) -> p c u", u=2),
-                picked[b][:].bitcast(I32).rearrange("p (u c) -> p c u", u=2),
-            )
-
-        def turn(b, u):
-            words = picked[b][:].bitcast(F32).rearrange("p (u t s) -> p u t s", t=LANES, u=2)
-            turned[b, u] = in_bank(f"turned{b}{u}", [P, LANES, P])
-            for t in range(LANES):
-                nc.tensor.transpose(turned[b, u][:, t, :], words[:, u, t, :], ident[:])
-
-        def cast_queries(h):
+        def cast_queries(h, engine):
+            b0, b1 = QUERY_GROUPS[h]
+            q_grp[h] = placed("q_grp", h, [P, (b1 - b0) * NQ * LANES], BF16, keep)
             grouped = q_grp[h][:].rearrange("p (b q j) -> p b q j", q=NQ, j=LANES)
-            planes = q_raw[h][:].rearrange("p b j q -> p b q j")
-            nc.gpsimd.tensor_scalar(grouped, planes, 1.0, 0.0, MULT, ADD)
+            source = q_raw[h][:].rearrange("p b j q -> p b q j")
+            if engine is nc.gpsimd:
+                nc.gpsimd.tensor_scalar(grouped, source, 1.0, 0.0, MULT, ADD)
+            else:
+                copy(engine, grouped, source)
 
         def quantize_queries(h):
             b0, b1 = QUERY_GROUPS[h]
             q_codes = placed("q_codes", h, [P, (b1 - b0) * NQ], U32, keep)
             q_scales = placed("q_scales", h, [P, (b1 - b0) * NQ], U8, keep)
-            for c0, c1 in ((0, NQ), (NQ, (b1 - b0) * NQ)):
-                if c1 > c0:
-                    nc.vector.quantize_mx(
-                        out=q_codes[:, c0:c1].bitcast(FP8X4),
-                        scales=q_scales[:, c0:c1],
-                        in_=q_grp[h][:, c0 * LANES : c1 * LANES],
-                    )
+            nc.vector.quantize_mx(out=q_codes[:].bitcast(FP8X4), scales=q_scales[:], in_=q_grp[h][:])
             for b in range(b0, b1):
                 cols = slice((b - b0) * NQ, (b - b0 + 1) * NQ)
                 queries[b] = q_codes[:, cols], q_scales[:, cols]
 
-        def quantize_keys(b):
-            k_codes = placed("k_codes", b, [P, N], U32, keep)
-            k_scales = placed("k_scales", b, [P, N], U8, ring3)
-            nc.vector.quantize_mx(out=k_codes[:].bitcast(FP8X4), scales=k_scales[:], in_=k_grp[b][:])
-            keys[b] = k_codes, k_scales
+        def quantize_keys(b, h=0, parts=1):
+            if b not in keys:
+                keys[b] = placed("k_codes", b, [P, N], U32, ring), placed("k_scales", b, [P, N], U8, ring)
+            k_codes, k_scales = keys[b]
+            c0, c1 = h * N // parts, (h + 1) * N // parts
+            nc.vector.quantize_mx(
+                out=k_codes[:, c0:c1].bitcast(FP8X4), scales=k_scales[:, c0:c1], in_=k_grp[b][:, c0 * LANES : c1 * LANES]
+            )
 
-        def score(b):
+        def score(b, h=0, parts=1):
             q_codes, q_scales = queries[b]
             k_codes, k_scales = keys[b]
-            scores[b] = in_bank(f"scores{b}", [P, LANES, NQ])
-            for t in range(LANES):
+            n = LANES // parts
+            scores[b, h] = in_bank(f"scores{b}{h}", [P, n, NQ])
+            for i in range(n):
+                cols = slice((h * n + i) * P, (h * n + i + 1) * P)
                 nc.tensor.matmul_mx(
-                    out=scores[b][:, t, :],
-                    lhsT=k_codes[:, t * P : (t + 1) * P].bitcast(FP8X4),
-                    lhsT_scale=k_scales[:, t * P : (t + 1) * P],
+                    out=scores[b, h][:, i, :],
+                    lhsT=k_codes[:, cols].bitcast(FP8X4),
+                    lhsT_scale=k_scales[:, cols],
                     rhs=q_codes.bitcast(FP8X4),
                     rhs_scale=q_scales,
                     start=True,
                     stop=True,
                 )
 
-
-        def copy_values(b, u, h=0, parts=1):
-            if u == 0 and h == 0:
-                v_grp[b] = placed("v_grp", b, [P, D * LANES], BF16, keep)
-            ms = slice(h * P // parts, (h + 1) * P // parts)
-            nc.scalar.copy(
-                v_grp[b][:].rearrange("s (m u e t) -> s u m e t", u=2, e=2, t=LANES)[:, u, ms],
-                turned[b, u][:].bitcast(BF16).rearrange("s t (m e) -> s m e t", e=2)[:, ms],
-            )
-
-        def copy_words(b, u):
-            if u == 0:
-                v_grp[b] = placed("v_grp", b, [P, D * LANES], BF16, keep)
-            words = placed("words", u, [P, LANES, P], F32, keep)
-            nc.scalar.copy(words[:], turned[b, u][:])
-            nc.gpsimd.tensor_scalar(
-                v_grp[b][:].rearrange("s (m u e t) -> s u m e t", u=2, e=2, t=LANES)[:, u],
-                words[:].bitcast(BF16).rearrange("s t (m e) -> s m e t", e=2),
-                1.0,
-                0.0,
-                MULT,
-                ADD,
-            )
-
-        def quantize_values(b, h=0, parts=1):
-            if h == 0:
-                v_codes = ring3.tile([P, D], U32, align_bytes=64, name="v_codes")
-                v_scales = placed("v_scales", b, [P, D], U8, ring3)
-                values[b] = v_codes, v_scales
-            v_codes, v_scales = values[b]
-            d0, d1 = h * D // parts, (h + 1) * D // parts
-            nc.vector.quantize_mx(
-                out=v_codes[:, d0:d1].bitcast(FP8X4),
-                scales=v_scales[:, d0:d1],
-                in_=v_grp[b][:, d0 * LANES : d1 * LANES],
-            )
+        def quantize_values(b):
+            v_codes = placed("v_codes", b, [P, D], U32, ring)
+            v_scales = placed("v_scales", b, [P, D], U8, ring)
+            values[b] = v_codes, v_scales
+            nc.vector.quantize_mx(out=v_codes[:].bitcast(FP8X4), scales=v_scales[:], in_=v_grp[b][:])
 
         def multiply(b, h=0, parts=1):
             w_codes, w_scales = weights[b]
@@ -317,33 +270,28 @@ def tile_attend_x_mla_sigmoid_seg_kernel(tc, qT, cT, ts, kb, ch, offs, out):
             )
 
         def finish(b, h=0, parts=1):
-            if h == 0:
-                ys[b] = placed("y", b, [P, D], F32, ring2, align=None)
+            if b not in ys:
+                ys[b] = placed("y", b, [P, D], F32, ring)
             cols = slice(h * D // parts, (h + 1) * D // parts)
             nc.vector.scalar_tensor_tensor(
                 out=ys[b][:, cols], in0=acc[b, h][:], scalar=1.0 / 16.0, in1=chans[:, cols], op0=MULT, op1=MULT
             )
             nc.sync.dma_start(out[b][:, cols], ys[b][:, cols])
 
-        ps = {}
-
-        def sigmoid(b):
+        def sigmoid(b, h=0, parts=1):
             bias, scale = tokens[b][:, 0, :], tokens[b][:, 1, :]
-            p = placed("p", b, [P, LANES, NQ], F32, ring2, align=None)
-            ps[b] = p
-            for t in range(LANES):
+            if b not in ps:
+                ps[b] = placed("p", b, [P, LANES, NQ], F32, ring)
+            n = LANES // parts
+            for i in range(n):
+                t = h * n + i
                 nc.scalar.activation(
-                    p[:, t, :],
-                    scores[b][:, t, :],
-                    SIGMOID,
-                    bias=bias[:, t : t + 1],
-                    scale=scale[:, t : t + 1],
+                    ps[b][:, t, :], scores[b, h][:, i, :], SIGMOID, bias=bias[:, t : t + 1], scale=scale[:, t : t + 1]
                 )
 
-        def weigh(b):
+        def weigh(b, engine):
             p, scale = ps[b], tokens[b][:, 1, :]
-            w_grp[b] = placed("w_grp", b, [P, NQ, LANES], BF16, ring2)
-            engine = nc.gpsimd if b < ON_GPSIMD else nc.vector
+            w_grp[b] = placed("w_grp", b, [P, NQ, LANES], BF16, ring)
             engine.tensor_tensor(
                 w_grp[b][:].rearrange("s (c i) t -> s c t i", i=LINE),
                 p[:].rearrange("s t (c i) -> s c t i", i=LINE),
@@ -352,97 +300,103 @@ def tile_attend_x_mla_sigmoid_seg_kernel(tc, qT, cT, ts, kb, ch, offs, out):
             )
 
         def quantize_weights(b):
-            w_codes = ring2.tile([P, NQ], U32, align_bytes=64, name="w_codes")
-            w_scales = placed("w_scales", b, [P, NQ], U8, ring2)
+            w_codes = placed("w_codes", b, [P, NQ], U32, ring)
+            w_scales = placed("w_scales", b, [P, NQ], U8, ring)
             nc.vector.quantize_mx(
                 out=w_codes[:].bitcast(FP8X4), scales=w_scales[:], in_=w_grp[b][:].rearrange("s q t -> s (q t)")
             )
             weights[b] = w_codes, w_scales
 
-        gather_tokens("kb", 0, 1)
-        gather_tokens("ts", 0, 1)
-        cast(0, 0)
-        cast(0, 1)
-        cast(1, 0, slice(0, 1))
-        gather(0, 0)
-        turn(0, 0)
-        copy_words(0, 0)
-        cast(1, 0, slice(1, 2))
-        cast(1, 1, slice(0, 1))
-        gather_tokens("kb", 1, LAST)
-        gather(0, 1)
-        turn(0, 1)
-        weave(0)
-        copy_words(0, 1)
-        cast(1, 1, slice(1, 2))
-        gather_tokens("ts", 1, LAST)
-        cast_queries(0)
-        gather(1, 0)
-        gather(1, 1)
+        vector, scalar, gpsimd = nc.vector, nc.scalar, nc.gpsimd
+        load_pool(0, 0)
+        load_row("ts", 0, SEG)
+        load_pool(0, 1)
+        load_row("kb", 0, 2 * SEG)
+        load_queries(0)
+        load_row("ts", SEG, 3 * SEG)
+        load_pool(0, 2)
+        load_row("kb", 2 * SEG, T)
+        load_pool(0, 3)
+        load_row("ts", 3 * SEG, T)
+        for j in range(LANES):
+            load_pool(1, j)
+
+        for name, b in (("ts", 0), ("kb", 0), ("kb", 1), ("ts", 1), ("ts", 2), ("kb", 2), ("kb", 3), ("ts", 3)):
+            gather_tokens(name, b)
+        cast_queries(0, gpsimd)
+        for j in range(LANES):
+            gather(0, j, scalar)
+            turn(0, j)
+            if j == 1:
+                copy_values(0, 0, scalar)
+        for j in range(LANES):
+            load_pool(2, j)
+        load_chans()
+        weave(0, gpsimd)
+        gather(1, 0, scalar)
         turn(1, 0)
-        turn(1, 1)
+        copy_values(0, 1, scalar)
+        turn_tokens(0, 2, vector)
         quantize_keys(0)
-        quantize_values(0)
         quantize_queries(0)
         score(0)
-        weave(1)
-        cast_queries(1)
-
-        cast(2, 0)
-        gather(2, 0)
-        copy_values(1, 0)
-        cast(2, 1)
-        gather(2, 1)
-        quantize_keys(1)
-        turn(2, 0)
-        turn(2, 1)
-        weave(2)
-        gather_tokens("kb", LAST, B)
-        gather_tokens("ts", LAST, B)
-        turn_tokens(0, 2)
-        turn_tokens(2, B)
+        quantize_values(0)
+        for j in range(1, LANES):
+            gather(1, j, scalar)
+            turn(1, j)
+        for j in range(LANES - 1):
+            load_pool(3, j)
+        weave(1, gpsimd)
+        copy_values(1, 0, vector)
         sigmoid(0)
-        copy_values(1, 1)
-        quantize_queries(1)
+        turn_tokens(2, B, vector)
+        copy_values(1, 1, vector)
+        weigh(0, gpsimd)
+        gather(2, 0, scalar)
+        load_pool(3, 3)
+        turn(2, 0)
+        for j in range(1, LANES):
+            gather(2, j, vector if j == 1 else scalar)
+            turn(2, j)
+        quantize_keys(1)
         score(1)
-        quantize_keys(2)
-        score(2)
-        weigh(0)
-        cast(3, 0)
-        gather(3, 0)
-        turn(3, 0)
+        quantize_values(1)
         quantize_weights(0)
         multiply(0)
-        cast(3, 1)
-        gather(3, 1)
-        turn(3, 1)
-        sigmoid(1)
-        weigh(1)
+        weave(2, gpsimd)
+        gather(3, 0, scalar)
+        copy_values(2, 0, vector)
+        copy_values(2, 1, vector)
         finish(0)
-        weave(3)
-        quantize_values(1)
+        sigmoid(1)
+        gather(3, 1, scalar)
+        gather(3, 2, vector)
+        gather(3, 3, scalar)
+        for j in range(LANES):
+            turn(3, j)
+        quantize_keys(2)
+        score(2)
+        weave(3, vector, 0, 2)
+        weave(3, scalar, 1, 2)
+        weigh(1, vector)
         quantize_keys(3)
         score(3)
+        sigmoid(2)
         quantize_weights(1)
         multiply(1)
-        copy_values(2, 0)
-        sigmoid(2)
-        weigh(2)
-        copy_values(2, 1)
         quantize_values(2)
-        quantize_weights(2)
-        finish(1)
-        multiply(2)
-        copy_values(3, 0)
+        copy_values(3, 0, scalar)
+        weigh(2, vector)
         sigmoid(3)
-        weigh(3)
-        copy_values(3, 1, 0, 2)
-        quantize_values(3, 0, 2)
+        finish(1)
+        quantize_weights(2)
+        multiply(2)
+        copy_values(3, 1, scalar)
+        weigh(3, vector)
+        finish(2)
+        quantize_values(3)
         quantize_weights(3)
         multiply(3, 0, 2)
-        copy_values(3, 1, 1, 2)
-        quantize_values(3, 1, 2)
         multiply(3, 1, 2)
-        finish(2)
         finish(3, 0, 2)
         finish(3, 1, 2)

@@ -25,32 +25,34 @@ MULT = mybir.AluOpType.mult
 COPY = mybir.ActivationFunctionType.Copy
 SIGMOID = mybir.ActivationFunctionType.Sigmoid
 
-TS_SPLIT = 3 * SEG - 127
-ROW = {"kb": (0, 0, 8, 8), "ts": (4, 8, 8, 0)}
+TS_SPLIT = 3 * SEG - 120
+ROW = {"kb": (0, 4, 8, 8), "ts": (4, 4, 0, 0)}
 PITCH = 10
 QUERY_GROUPS = ((0, B),)
 SLOT = SEG * 4
 
-WINDOW_SLOT = ((0, 1, 2, 3), (4, 6, 8, 10), (0, 12, 15, 18), (6, 21, 25, 0))
+WINDOW_SLOT = ((2, 3, 0, 1), (5, 9, 11, 7), (2, 13, 16, 19), (9, 22, 26, 2))
 WINDOW_AT = {(b, j): WINDOW_SLOT[b][j] * SLOT for b in range(B) for j in range(LANES)}
 REUSE = {
-    "q_scales0": ((1, 0), 0),
-    "v_scales0": ((1, 0), 512),
-    "v_grp0": (29, 0),
-    "k_grp1": (29, 0),
-    "p0": ((1, 3), 2048),
+    "columns0": ((0, 2), 0),
+    "v_grp0": (30, 0),
+    "k_grp1": (30, 0),
+    "q_scales0": ((1, 0), 4096),
+    "v_scales0": ((1, 0), 4608),
+    "p0": ((1, 3), 0),
     "v_scales1": ((2, 2), 0),
-    "w_grp0": (30, 0),
-    "k_grp2": (30, 0),
+    "w_grp0": ((2, 1), 0),
+    "k_grp2": ((2, 1), 0),
     "v_grp2": ((2, 3), 0),
+    "columns2": ((2, 3), 4096),
     "p1": ((3, 0), 0),
     "k_scales2": ((3, 2), 0),
-    "w_grp1": ((3, 3), 0),
-    "v_scales2": ((3, 3), 1024),
+    "w_grp1": ((3, 2), 1024),
+    "v_scales2": ((3, 2), 512),
     "p2": ((3, 3), 2048),
     "v_grp3": ((3, 3), 4096),
 }
-BANK = {"turned00": 0, "turned01": 1, "turned10": 2, "turned11": 3, "turned20": 0, "turned21": 1, "turned30": 2, "turned31": 3, "bank0": 1, "bank2": 2, "scores00": 6, "scores10": 7, "scores20": 6, "scores30": 7, "acc00": 5, "acc10": 4, "acc20": 5, "acc30": 4, "acc31": 6}
+BANK = {"turned00": 0, "turned01": 1, "turned10": 2, "turned11": 3, "turned20": 0, "turned21": 1, "turned30": 2, "turned31": 3, "bank0": 4, "bank2": 3, "scores00": 6, "scores10": 7, "scores20": 6, "scores30": 7, "scores31": 0, "acc00": 5, "acc10": 4, "acc20": 5, "acc30": 4, "acc31": 6}
 
 
 def tile_attend_x_mla_sigmoid_seg_kernel(tc, qT, cT, ts, kb, ch, offs, out):
@@ -87,12 +89,13 @@ def tile_attend_x_mla_sigmoid_seg_kernel(tc, qT, cT, ts, kb, ch, offs, out):
         warm = keep.tile([P, 2], F32, name="warm")
         nc.vector.memset(warm[:, 0:1], 0.0)
         nc.scalar.activation(warm[:, 1:2], warm[:, 0:1], SIGMOID)
-        nc.vector.memset(windows["ts"][:, 0 : SEG + 1], 0.0)
-        nc.gpsimd.memset(windows["kb"][:, 0 : 2 * SEG], 0.0)
-        nc.vector.memset(windows["ts"][:, SEG + 1 : 3 * SEG], 0.0)
-        nc.gpsimd.memset(windows["kb"][:, 2 * SEG : T], 0.0)
-        nc.gpsimd.memset(windows["ts"][:, 3 * SEG : T], 0.0)
+        nc.gpsimd.memset(windows["kb"][:, 0:SEG], 0.0)
+        nc.vector.memset(windows["ts"][:, 0 : 2 * SEG + 1], 0.0)
+        nc.gpsimd.memset(windows["kb"][:, SEG : 2 * SEG], 0.0)
         make_identity(nc, ident[:])
+        nc.vector.memset(windows["ts"][:, 2 * SEG + 1 : TS_SPLIT], 0.0)
+        nc.gpsimd.memset(windows["kb"][:, 2 * SEG : T], 0.0)
+        nc.gpsimd.memset(windows["ts"][:, TS_SPLIT:T], 0.0)
 
         cT_view = cT.rearrange("(p j) w -> p j w", j=LANES)
 
@@ -115,19 +118,24 @@ def tile_attend_x_mla_sigmoid_seg_kernel(tc, qT, cT, ts, kb, ch, offs, out):
             nc.sync.dma_start(chans[:], ch)
 
         queries, rows, tokens, picked, turned, q_grp = {}, {}, {}, {}, {}, {}
-        k_grp, keys, scores = {}, {}, {}
+        k_grp, keys, scores, lanes = {}, {}, {}, {}
         v_grp, values, w_grp, weights, acc, ys, ps = {}, {}, {}, {}, {}, {}, {}
 
         def offsets(b, h=0, parts=1):
             width = LIST_COLUMNS // parts
             return lists[:, b * LIST_COLUMNS + h * width : b * LIST_COLUMNS + (h + 1) * width]
 
-        def gather_tokens(name, b):
+        def gather_tokens(name, b, engine):
             rows[name, b] = placed("row_" + name, b, [P, N], F32, keep)
-            nc.vector.tensor_copy(
-                rows[name, b][:].bitcast(U32).rearrange("p (t s) -> p s t", t=LANES),
-                windows[name][:].bitcast(U32)[:, 0 : (b + 1) * SEG].indirect(offsets(b)),
-            )
+            if engine is nc.scalar:
+                nc.scalar.activation(rows[name, b][:], windows[name][:, 0 : (b + 1) * SEG].indirect(offsets(b)), COPY)
+                lanes[name, b] = [rows[name, b][:, t:N:LANES] for t in range(LANES)]
+            else:
+                nc.vector.tensor_copy(
+                    rows[name, b][:].bitcast(U32).rearrange("p (t s) -> p s t", t=LANES),
+                    windows[name][:].bitcast(U32)[:, 0 : (b + 1) * SEG].indirect(offsets(b)),
+                )
+                lanes[name, b] = [rows[name, b][:, t * P : (t + 1) * P] for t in range(LANES)]
 
         def turn_tokens(b0, b1, engine):
             n = b1 - b0
@@ -137,7 +145,7 @@ def tile_attend_x_mla_sigmoid_seg_kernel(tc, qT, cT, ts, kb, ch, offs, out):
                     for t in range(LANES):
                         c = (2 * (b - b0) + i) * LANES + t
                         c0 = PITCH * (c + 1) - 2 - ROW[name][b]
-                        nc.tensor.transpose(bank[:, c0 : c0 + P], rows[name, b][:, t * P : (t + 1) * P], ident[:])
+                        nc.tensor.transpose(bank[:, c0 : c0 + P], lanes[name, b][t], ident[:])
             columns = placed("columns", b0, [P, n, 2, LANES], F32, keep)
             copy(
                 engine,
@@ -167,11 +175,11 @@ def tile_attend_x_mla_sigmoid_seg_kernel(tc, qT, cT, ts, kb, ch, offs, out):
         def weave(b, engine, h=0, parts=1):
             if b not in k_grp:
                 k_grp[b] = placed("k_grp", b, [P, N * LANES], BF16, ring)
-            lanes = slice(h * LANES // parts, (h + 1) * LANES // parts)
+            part = slice(h * LANES // parts, (h + 1) * LANES // parts)
             if engine is nc.gpsimd:
                 nc.gpsimd.tensor_scalar(
-                    k_grp[b][:].rearrange("p (t s j) -> p t s j", t=LANES, j=LANES)[:, lanes],
-                    picked[b][:].rearrange("p (j s t) -> p t s j", t=LANES, j=LANES)[:, lanes],
+                    k_grp[b][:].rearrange("p (t s j) -> p s t j", t=LANES, j=LANES)[:, :, part],
+                    picked[b][:].rearrange("p (j s t) -> p s t j", t=LANES, j=LANES)[:, :, part],
                     1.0,
                     0.0,
                     MULT,
@@ -180,8 +188,8 @@ def tile_attend_x_mla_sigmoid_seg_kernel(tc, qT, cT, ts, kb, ch, offs, out):
             else:
                 copy(
                     engine,
-                    k_grp[b][:].rearrange("p (t c s j) -> p c t s j", t=LANES, s=2, j=LANES)[:, :, lanes],
-                    picked[b][:].rearrange("p (j c s t) -> p c t s j", t=LANES, s=2, j=LANES)[:, :, lanes],
+                    k_grp[b][:].rearrange("p (t c s j) -> p c t s j", t=LANES, s=2, j=LANES)[:, :, part],
+                    picked[b][:].rearrange("p (j c s t) -> p c t s j", t=LANES, s=2, j=LANES)[:, :, part],
                 )
 
         def turn(b, j):
@@ -196,7 +204,7 @@ def tile_attend_x_mla_sigmoid_seg_kernel(tc, qT, cT, ts, kb, ch, offs, out):
 
         def copy_values(b, u, engine):
             if b not in v_grp:
-                v_grp[b] = placed("v_grp", b, [P, D * LANES], BF16, ring)
+                v_grp[b] = placed("v_grp", b, [P, D * LANES], BF16, keep)
             copy(
                 engine,
                 v_grp[b][:].bitcast(F32).rearrange("s (m u c) -> s u m c", u=2, c=LANES)[:, u],
@@ -309,36 +317,37 @@ def tile_attend_x_mla_sigmoid_seg_kernel(tc, qT, cT, ts, kb, ch, offs, out):
 
         vector, scalar, gpsimd = nc.vector, nc.scalar, nc.gpsimd
         load_pool(0, 0)
-        load_row("ts", 0, SEG)
+        load_row("kb", 0, SEG)
         load_pool(0, 1)
-        load_row("kb", 0, 2 * SEG)
+        load_row("ts", 0, 2 * SEG)
+        load_row("kb", SEG, 2 * SEG)
         load_queries(0)
-        load_row("ts", SEG, 3 * SEG)
-        load_pool(0, 2)
         load_row("kb", 2 * SEG, T)
+        load_pool(0, 2)
+        load_row("ts", 2 * SEG, T)
         load_pool(0, 3)
-        load_row("ts", 3 * SEG, T)
         for j in range(LANES):
             load_pool(1, j)
 
-        for name, b in (("ts", 0), ("kb", 0), ("kb", 1), ("ts", 1), ("ts", 2), ("kb", 2), ("kb", 3), ("ts", 3)):
-            gather_tokens(name, b)
+        for name, b in (("kb", 0), ("ts", 0), ("kb", 1), ("kb", 2), ("kb", 3), ("ts", 2), ("ts", 3)):
+            gather_tokens(name, b, vector)
         cast_queries(0, gpsimd)
         for j in range(LANES):
             gather(0, j, scalar)
             turn(0, j)
             if j == 1:
                 copy_values(0, 0, scalar)
+                gather_tokens("ts", 1, scalar)
+                turn_tokens(0, 2, vector)
         for j in range(LANES):
             load_pool(2, j)
         load_chans()
         weave(0, gpsimd)
+        copy_values(0, 1, vector)
         gather(1, 0, scalar)
         turn(1, 0)
-        copy_values(0, 1, scalar)
-        turn_tokens(0, 2, vector)
-        quantize_keys(0)
         quantize_queries(0)
+        quantize_keys(0)
         score(0)
         quantize_values(0)
         for j in range(1, LANES):
@@ -349,9 +358,7 @@ def tile_attend_x_mla_sigmoid_seg_kernel(tc, qT, cT, ts, kb, ch, offs, out):
         weave(1, gpsimd)
         copy_values(1, 0, vector)
         sigmoid(0)
-        turn_tokens(2, B, vector)
         copy_values(1, 1, vector)
-        weigh(0, gpsimd)
         gather(2, 0, scalar)
         load_pool(3, 3)
         turn(2, 0)
@@ -360,6 +367,7 @@ def tile_attend_x_mla_sigmoid_seg_kernel(tc, qT, cT, ts, kb, ch, offs, out):
             turn(2, j)
         quantize_keys(1)
         score(1)
+        weigh(0, vector)
         quantize_values(1)
         quantize_weights(0)
         multiply(0)
@@ -367,6 +375,7 @@ def tile_attend_x_mla_sigmoid_seg_kernel(tc, qT, cT, ts, kb, ch, offs, out):
         gather(3, 0, scalar)
         copy_values(2, 0, vector)
         copy_values(2, 1, vector)
+        turn_tokens(2, B, vector)
         finish(0)
         sigmoid(1)
         gather(3, 1, scalar)
@@ -376,26 +385,29 @@ def tile_attend_x_mla_sigmoid_seg_kernel(tc, qT, cT, ts, kb, ch, offs, out):
             turn(3, j)
         quantize_keys(2)
         score(2)
-        weave(3, vector, 0, 2)
-        weave(3, scalar, 1, 2)
         weigh(1, vector)
-        quantize_keys(3)
-        score(3)
-        sigmoid(2)
+        quantize_values(2)
         quantize_weights(1)
         multiply(1)
-        quantize_values(2)
+        weave(3, vector, 0, 2)
+        weave(3, scalar, 1, 2)
+        finish(1)
+        quantize_keys(3, 0, 2)
+        score(3, 0, 2)
+        sigmoid(2)
+        quantize_keys(3, 1, 2)
+        score(3, 1, 2)
         copy_values(3, 0, scalar)
         weigh(2, vector)
-        sigmoid(3)
-        finish(1)
+        sigmoid(3, 0, 2)
+        sigmoid(3, 1, 2)
         quantize_weights(2)
         multiply(2)
         copy_values(3, 1, scalar)
         weigh(3, vector)
         finish(2)
-        quantize_values(3)
         quantize_weights(3)
+        quantize_values(3)
         multiply(3, 0, 2)
         multiply(3, 1, 2)
         finish(3, 0, 2)

@@ -31,24 +31,27 @@ PITCH = 10
 QUERY_GROUPS = ((0, B),)
 SLOT = SEG * 4
 
-WINDOW_SLOT = ((2, 3, 0, 1), (5, 9, 11, 7), (2, 13, 16, 19), (9, 22, 26, 2))
+WINDOW_SLOT = ((0, 1, 2, 3), (4, 8, 10, 6), (12, 15, 18, 21), (8, 24, 28, 0))
 WINDOW_AT = {(b, j): WINDOW_SLOT[b][j] * SLOT for b in range(B) for j in range(LANES)}
 REUSE = {
-    "columns0": ((0, 2), 0),
-    "v_grp0": (30, 0),
-    "k_grp1": (30, 0),
-    "q_scales0": ((1, 0), 4096),
-    "v_scales0": ((1, 0), 4608),
+    "v_grp0": (32, 0),
+    "k_grp1": (32, 0),
+    "columns0": ((1, 0), 0),
+    "q_scales0": ((1, 0), 512),
+    "v_scales0": ((1, 0), 1024),
     "p0": ((1, 3), 0),
+    "v_grp1": ((2, 0), 0),
     "v_scales1": ((2, 2), 0),
-    "w_grp0": ((2, 1), 0),
-    "k_grp2": ((2, 1), 0),
+    "w_grp0": ((2, 2), 1024),
+    "k_grp2": ((2, 2), 1024),
     "v_grp2": ((2, 3), 0),
     "columns2": ((2, 3), 4096),
+    "k_grp3": ((2, 3), 8192),
     "p1": ((3, 0), 0),
-    "k_scales2": ((3, 2), 0),
-    "w_grp1": ((3, 2), 1024),
-    "v_scales2": ((3, 2), 512),
+    "k_scales2": ((3, 1), 0),
+    "w_grp1": ((3, 1), 1024),
+    "v_scales2": ((3, 1), 512),
+    "y1": ((3, 2), 0),
     "p2": ((3, 3), 2048),
     "v_grp3": ((3, 3), 4096),
 }
@@ -174,7 +177,7 @@ def tile_attend_x_mla_sigmoid_seg_kernel(tc, qT, cT, ts, kb, ch, offs, out):
 
         def weave(b, engine, h=0, parts=1):
             if b not in k_grp:
-                k_grp[b] = placed("k_grp", b, [P, N * LANES], BF16, ring)
+                k_grp[b] = placed("k_grp", b, [P, N * LANES], BF16, keep)
             part = slice(h * LANES // parts, (h + 1) * LANES // parts)
             if engine is nc.gpsimd:
                 nc.gpsimd.tensor_scalar(
@@ -289,7 +292,7 @@ def tile_attend_x_mla_sigmoid_seg_kernel(tc, qT, cT, ts, kb, ch, offs, out):
         def sigmoid(b, h=0, parts=1):
             bias, scale = tokens[b][:, 0, :], tokens[b][:, 1, :]
             if b not in ps:
-                ps[b] = placed("p", b, [P, LANES, NQ], F32, ring)
+                ps[b] = placed("p", b, [P, LANES, NQ], F32, keep)
             n = LANES // parts
             for i in range(n):
                 t = h * n + i
@@ -353,17 +356,18 @@ def tile_attend_x_mla_sigmoid_seg_kernel(tc, qT, cT, ts, kb, ch, offs, out):
         for j in range(1, LANES):
             gather(1, j, scalar)
             turn(1, j)
-        for j in range(LANES - 1):
+        for j in range(LANES):
             load_pool(3, j)
         weave(1, gpsimd)
-        copy_values(1, 0, vector)
         sigmoid(0)
-        copy_values(1, 1, vector)
-        gather(2, 0, scalar)
-        load_pool(3, 3)
+        gather(2, 0, vector)
         turn(2, 0)
-        for j in range(1, LANES):
-            gather(2, j, vector if j == 1 else scalar)
+        copy_values(1, 0, vector)
+        copy_values(1, 1, vector)
+        gather(2, 1, vector)
+        turn(2, 1)
+        for j in range(2, LANES):
+            gather(2, j, scalar)
             turn(2, j)
         quantize_keys(1)
         score(1)
@@ -379,7 +383,7 @@ def tile_attend_x_mla_sigmoid_seg_kernel(tc, qT, cT, ts, kb, ch, offs, out):
         finish(0)
         sigmoid(1)
         gather(3, 1, scalar)
-        gather(3, 2, vector)
+        gather(3, 2, scalar)
         gather(3, 3, scalar)
         for j in range(LANES):
             turn(3, j)
@@ -389,25 +393,25 @@ def tile_attend_x_mla_sigmoid_seg_kernel(tc, qT, cT, ts, kb, ch, offs, out):
         quantize_values(2)
         quantize_weights(1)
         multiply(1)
-        weave(3, vector, 0, 2)
+        weave(3, gpsimd, 0, 2)
         weave(3, scalar, 1, 2)
         finish(1)
+        copy_values(3, 0, vector)
+        copy_values(3, 1, scalar)
         quantize_keys(3, 0, 2)
         score(3, 0, 2)
         sigmoid(2)
         quantize_keys(3, 1, 2)
         score(3, 1, 2)
-        copy_values(3, 0, scalar)
+        quantize_values(3)
         weigh(2, vector)
         sigmoid(3, 0, 2)
         sigmoid(3, 1, 2)
         quantize_weights(2)
         multiply(2)
-        copy_values(3, 1, scalar)
         weigh(3, vector)
-        finish(2)
         quantize_weights(3)
-        quantize_values(3)
+        finish(2)
         multiply(3, 0, 2)
         multiply(3, 1, 2)
         finish(3, 0, 2)

@@ -117,8 +117,8 @@ def tile_attend_x_mla_sigmoid_seg_kernel(tc, qT, cT, ts, kb, ch, offs, out):
                 qT.rearrange("b (p j) q -> p b (j q)", j=LANES)[:, slice(*QUERY_GROUPS[h])],
             )
 
-        def load_chans():
-            nc.sync.dma_start(chans[:], ch)
+        def load_chans(c0=0, c1=D):
+            nc.sync.dma_start(chans[:, c0:c1], ch[:, c0:c1])
 
         queries, rows, tokens, picked, turned, q_grp = {}, {}, {}, {}, {}, {}
         k_grp, keys, scores, lanes = {}, {}, {}, {}
@@ -179,21 +179,11 @@ def tile_attend_x_mla_sigmoid_seg_kernel(tc, qT, cT, ts, kb, ch, offs, out):
             if b not in k_grp:
                 k_grp[b] = placed("k_grp", b, [P, N * LANES], BF16, keep)
             part = slice(h * LANES // parts, (h + 1) * LANES // parts)
-            if engine is nc.gpsimd:
-                nc.gpsimd.tensor_scalar(
-                    k_grp[b][:].rearrange("p (t s j) -> p s t j", t=LANES, j=LANES)[:, :, part],
-                    picked[b][:].rearrange("p (j s t) -> p s t j", t=LANES, j=LANES)[:, :, part],
-                    1.0,
-                    0.0,
-                    MULT,
-                    ADD,
-                )
-            else:
-                copy(
-                    engine,
-                    k_grp[b][:].rearrange("p (t c s j) -> p c t s j", t=LANES, s=2, j=LANES)[:, :, part],
-                    picked[b][:].rearrange("p (j c s t) -> p c t s j", t=LANES, s=2, j=LANES)[:, :, part],
-                )
+            copy(
+                engine,
+                k_grp[b][:].rearrange("p (t c s j) -> p c t s j", t=LANES, s=2, j=LANES)[:, :, part],
+                picked[b][:].rearrange("p (j c s t) -> p c t s j", t=LANES, s=2, j=LANES)[:, :, part],
+            )
 
         def turn(b, j):
             words = picked[b][:].bitcast(F32)

@@ -31,15 +31,15 @@ PITCH = 10
 QUERY_GROUPS = ((0, B),)
 SLOT = SEG * 4
 
-WINDOW_SLOT = ((0, 1, 2, 3), (4, 8, 10, 6), (12, 15, 18, 21), (8, 24, 28, 0))
+WINDOW_SLOT = ((0, 1, 2, 3), (4, 8, 10, 6), (12, 15, 18, 21), (8, 24, 28, 32))
 WINDOW_AT = {(b, j): WINDOW_SLOT[b][j] * SLOT for b in range(B) for j in range(LANES)}
 REUSE = {
-    "v_grp0": (32, 0),
-    "k_grp1": (32, 0),
+    "v_grp0": ((0, 3), 0),
+    "k_grp1": ((0, 3), 0),
     "columns0": ((1, 0), 0),
     "q_scales0": ((1, 0), 512),
     "v_scales0": ((1, 0), 1024),
-    "p0": ((1, 3), 0),
+    "p0": ((2, 1), 0),
     "v_grp1": ((2, 0), 0),
     "v_scales1": ((2, 2), 0),
     "w_grp0": ((2, 2), 1024),
@@ -52,6 +52,7 @@ REUSE = {
     "w_grp1": ((3, 1), 1024),
     "v_scales2": ((3, 1), 512),
     "y1": ((3, 2), 0),
+    "p3": ((3, 2), 4096),
     "p2": ((3, 3), 2048),
     "v_grp3": ((3, 3), 4096),
 }
@@ -175,10 +176,10 @@ def tile_attend_x_mla_sigmoid_seg_kernel(tc, qT, cT, ts, kb, ch, offs, out):
             else:
                 nc.vector.tensor_copy(plane, source)
 
-        def weave(b, engine, h=0, parts=1):
+        def weave(b, engine, t0=0, t1=LANES):
             if b not in k_grp:
                 k_grp[b] = placed("k_grp", b, [P, N * LANES], BF16, keep)
-            part = slice(h * LANES // parts, (h + 1) * LANES // parts)
+            part = slice(t0, t1)
             copy(
                 engine,
                 k_grp[b][:].rearrange("p (t c s j) -> p c t s j", t=LANES, s=2, j=LANES)[:, :, part],
@@ -329,13 +330,13 @@ def tile_attend_x_mla_sigmoid_seg_kernel(tc, qT, cT, ts, kb, ch, offs, out):
             gather(0, j, scalar)
             turn(0, j)
             if j == 1:
-                copy_values(0, 0, scalar)
                 gather_tokens("ts", 1, scalar)
                 turn_tokens(0, 2, vector)
         for j in range(LANES):
             load_pool(2, j)
         load_chans()
         weave(0, gpsimd)
+        copy_values(0, 0, vector)
         copy_values(0, 1, vector)
         gather(1, 0, scalar)
         turn(1, 0)
@@ -349,13 +350,13 @@ def tile_attend_x_mla_sigmoid_seg_kernel(tc, qT, cT, ts, kb, ch, offs, out):
         for j in range(LANES):
             load_pool(3, j)
         weave(1, gpsimd)
-        sigmoid(0)
         gather(2, 0, vector)
         turn(2, 0)
         copy_values(1, 0, vector)
         copy_values(1, 1, vector)
-        gather(2, 1, vector)
+        gather(2, 1, scalar)
         turn(2, 1)
+        sigmoid(0)
         for j in range(2, LANES):
             gather(2, j, scalar)
             turn(2, j)
@@ -384,7 +385,7 @@ def tile_attend_x_mla_sigmoid_seg_kernel(tc, qT, cT, ts, kb, ch, offs, out):
         quantize_weights(1)
         multiply(1)
         weave(3, gpsimd, 0, 2)
-        weave(3, scalar, 1, 2)
+        weave(3, scalar, 2, 4)
         finish(1)
         copy_values(3, 0, vector)
         copy_values(3, 1, scalar)

from contextlib import ExitStack

import concourse.mybir as mybir
from concourse.masks import make_identity

B, N, T, D, NQ = 4, 512, 4096, 512, 128
P = 128
SEG = T // B
LANES = 4
LINE = 4
LIST_COLUMNS = N // 16
LAST = B - 1

FLOPS = B * 2 * (2 * N * D * NQ)
BYTES = 4 * (B * D * NQ + D * T + 2 * T + D + B * NQ * D) + 2 * P * (B * N // 16)

F32 = mybir.dt.float32
BF16 = mybir.dt.bfloat16
U32 = mybir.dt.uint32
U16 = mybir.dt.uint16
U8 = mybir.dt.uint8
FP8X4 = mybir.dt.float8_e4m3fn_x4
ADD = mybir.AluOpType.add
MULT = mybir.AluOpType.mult
COPY = mybir.ActivationFunctionType.Copy
SIGMOID = mybir.ActivationFunctionType.Sigmoid

TS_SPLIT = 3 * SEG - 120
ROW = {"kb": (0, 4, 8, 8), "ts": (4, 4, 0, 0)}
PITCH = 10
QUERY_GROUPS = ((0, B),)
SLOT = SEG * 4

WINDOW_SLOT = ((0, 1, 2, 3), (4, 8, 10, 6), (12, 15, 18, 21), (8, 24, 28, 32))
WINDOW_AT = {(b, j): WINDOW_SLOT[b][j] * SLOT for b in range(B) for j in range(LANES)}
REUSE = {
    "v_grp0": ((0, 3), 0),
    "k_grp1": ((0, 3), 0),
    "columns0": ((1, 0), 0),
    "q_scales0": ((1, 0), 512),
    "v_scales0": ((1, 0), 1024),
    "p0": ((2, 1), 0),
    "v_grp1": ((2, 0), 0),
    "v_scales1": ((2, 2), 0),
    "w_grp0": ((2, 2), 1024),
    "k_grp2": ((2, 2), 1024),
    "v_grp2": ((2, 3), 0),
    "columns2": ((2, 3), 4096),
    "k_grp3": ((2, 3), 8192),
    "p1": ((3, 0), 0),
    "k_scales2": ((3, 1), 0),
    "w_grp1": ((3, 1), 1024),
    "v_scales2": ((3, 1), 512),
    "y1": ((3, 2), 0),
    "p3": ((3, 2), 4096),
    "p2": ((3, 3), 2048),
    "v_grp3": ((3, 3), 4096),
}
BANK = {"turned00": 0, "turned01": 1, "turned10": 2, "turned11": 3, "turned20": 0, "turned21": 1, "turned30": 2, "turned31": 3, "bank0": 4, "bank2": 3, "scores00": 6, "scores10": 7, "scores20": 6, "scores30": 7, "scores31": 0, "acc00": 5, "acc10": 4, "acc20": 5, "acc30": 4, "acc31": 6}


def tile_attend_x_mla_sigmoid_seg_kernel(tc, qT, cT, ts, kb, ch, offs, out):
    nc = tc.nc
    with ExitStack() as ctx:
        keep = ctx.enter_context(tc.tile_pool(name="keep", bufs=1))
        stage = ctx.enter_context(tc.tile_pool(name="stage", bufs=1))
        ring = ctx.enter_context(tc.tile_pool(name="ring", bufs=2))
        psum = ctx.enter_context(tc.psum_pool(name="psum", bufs=1))

        def in_bank(name, shape):
            return psum.tile(shape, F32, offset=2048 * BANK[name], name=name)

        def placed(kind, b, shape, dtype, home):
            name = f"{kind}{b}"
            if name in REUSE:
                piece, offset = REUSE[name]
                return stage.tile(shape, dtype, align_bytes=64, offset=(WINDOW_AT[piece] if piece in WINDOW_AT else piece * SLOT) + offset, name=name)
            return home.tile(shape, dtype, align_bytes=64, name=name if home is keep else kind)

        lists = keep.tile([P, B * N // 16], U16, name="lists")
        nc.sync.dma_start(lists[:], offs)

        windows = {name: keep.tile([P, T], F32, name="window_" + name) for name in ("kb", "ts")}
        planes = {
            (b, j): stage.tile([P, (b + 1) * SEG], F32, align_bytes=64, offset=WINDOW_AT[b, j], name=f"plane{b}{j}")
            for b in range(B)
            for j in range(LANES)
        }
        q_raw = [placed("q_raw", b0, [P, b1 - b0, LANES, NQ], F32, keep) for b0, b1 in QUERY_GROUPS]
        chans = keep.tile([P, D], F32, name="chans")
        ident = keep.tile([P, P], F32, name="ident")

        warm = keep.tile([P, 2], F32, name="warm")
        nc.vector.memset(warm[:, 0:1], 0.0)
        nc.scalar.activation(warm[:, 1:2], warm[:, 0:1], SIGMOID)
        nc.gpsimd.memset(windows["kb"][:, 0:SEG], 0.0)
        nc.vector.memset(windows["ts"][:, 0 : 2 * SEG + 1], 0.0)
        nc.gpsimd.memset(windows["kb"][:, SEG : 2 * SEG], 0.0)
        make_identity(nc, ident[:])
        nc.vector.memset(windows["ts"][:, 2 * SEG + 1 : TS_SPLIT], 0.0)
        nc.gpsimd.memset(windows["kb"][:, 2 * SEG : T], 0.0)
        nc.gpsimd.memset(windows["ts"][:, TS_SPLIT:T], 0.0)

        cT_view = cT.rearrange("(p j) w -> p j w", j=LANES)

        def load_row(name, c0, c1):
            row = ROW[name][c0 // SEG]
            source = {"kb": kb, "ts": ts}[name]
            nc.sync.dma_start(windows[name][row : row + 1, c0:c1], source[0:1, c0:c1])

        def load_pool(b, j):
            cols = slice(b * SEG, (b + 1) * SEG)
            nc.sync.dma_start(planes[b, j][:, cols], cT_view[:, j, cols])

        def load_queries(h):
            nc.sync.dma_start(
                q_raw[h][:].rearrange("p b j q -> p b (j q)"),
                qT.rearrange("b (p j) q -> p b (j q)", j=LANES)[:, slice(*QUERY_GROUPS[h])],
            )

        def load_chans(c0=0, c1=D):
            nc.sync.dma_start(chans[:, c0:c1], ch[:, c0:c1])

        queries, rows, tokens, picked, turned, q_grp = {}, {}, {}, {}, {}, {}
        k_grp, keys, scores, lanes = {}, {}, {}, {}
        v_grp, values, w_grp, weights, acc, ys, ps = {}, {}, {}, {}, {}, {}, {}

        def offsets(b, h=0, parts=1):
            width = LIST_COLUMNS // parts
            return lists[:, b * LIST_COLUMNS + h * width : b * LIST_COLUMNS + (h + 1) * width]

        def gather_tokens(name, b, engine):
            rows[name, b] = placed("row_" + name, b, [P, N], F32, keep)
            if engine is nc.scalar:
                nc.scalar.activation(rows[name, b][:], windows[name][:, 0 : (b + 1) * SEG].indirect(offsets(b)), COPY)
                lanes[name, b] = [rows[name, b][:, t:N:LANES] for t in range(LANES)]
            else:
                nc.vector.tensor_copy(
                    rows[name, b][:].bitcast(U32).rearrange("p (t s) -> p s t", t=LANES),
                    windows[name][:].bitcast(U32)[:, 0 : (b + 1) * SEG].indirect(offsets(b)),
                )
                lanes[name, b] = [rows[name, b][:, t * P : (t + 1) * P] for t in range(LANES)]

        def turn_tokens(b0, b1, engine):
            n = b1 - b0
            bank = in_bank(f"bank{b0}", [P, 512])
            for b in range(b0, b1):
                for i, name in enumerate(("kb", "ts")):
                    for t in range(LANES):
                        c = (2 * (b - b0) + i) * LANES + t
                        c0 = PITCH * (c + 1) - 2 - ROW[name][b]
                        nc.tensor.transpose(bank[:, c0 : c0 + P], lanes[name, b][t], ident[:])
            columns = placed("columns", b0, [P, n, 2, LANES], F32, keep)
            copy(
                engine,
                columns[:].rearrange("s b i t -> s (b i t)"),
                bank[:, 0 : PITCH * 2 * LANES * n].rearrange("s (c z) -> s c z", z=PITCH)[:, :, PITCH - 2],
            )
            for b in range(n):
                tokens[b0 + b] = columns[:, b]

        def copy(engine, to, source):
            if engine is nc.scalar:
                nc.scalar.copy(to, source)
            else:
                engine.tensor_copy(to, source)

        def gather(b, j, engine, h=0, parts=1):
            if b not in picked:
                picked[b] = placed("picked", b, [P, LANES * N], BF16, ring)
            width = N // parts
            plane = picked[b][:, j * N + h * width : j * N + (h + 1) * width]
            source = planes[b, j][:].indirect(offsets(b, h, parts))
            if engine is nc.scalar:
                nc.scalar.activation(plane, source, COPY)
            else:
                nc.vector.tensor_copy(plane, source)

        def weave(b, engine, t0=0, t1=LANES):
            if b not in k_grp:
                k_grp[b] = placed("k_grp", b, [P, N * LANES], BF16, keep)
            part = slice(t0, t1)
            copy(
                engine,
                k_grp[b][:].rearrange("p (t c s j) -> p c t s j", t=LANES, s=2, j=LANES)[:, :, part],
                picked[b][:].rearrange("p (j c s t) -> p c t s j", t=LANES, s=2, j=LANES)[:, :, part],
            )

        def turn(b, j):
            words = picked[b][:].bitcast(F32)
            if j % 2 == 0:
                turned[b, j // 2] = in_bank(f"turned{b}{j // 2}", [P, LANES, P])
            w0 = j * N // 2
            for h in range(2):
                nc.tensor.transpose(
                    turned[b, j // 2][:, 2 * (j % 2) + h, :], words[:, w0 + h : w0 + N // 2 : 2], ident[:]
                )

        def copy_values(b, u, engine):
            if b not in v_grp:
                v_grp[b] = placed("v_grp", b, [P, D * LANES], BF16, keep)
            copy(
                engine,
                v_grp[b][:].bitcast(F32).rearrange("s (m u c) -> s u m c", u=2, c=LANES)[:, u],
                turned[b, u][:].rearrange("s c m -> s m c"),
            )

        def cast_queries(h, engine):
            b0, b1 = QUERY_GROUPS[h]
            q_grp[h] = placed("q_grp", h, [P, (b1 - b0) * NQ * LANES], BF16, keep)
            grouped = q_grp[h][:].rearrange("p (b q j) -> p b q j", q=NQ, j=LANES)
            source = q_raw[h][:].rearrange("p b j q -> p b q j")
            if engine is nc.gpsimd:
                nc.gpsimd.tensor_scalar(grouped, source, 1.0, 0.0, MULT, ADD)
            else:
                copy(engine, grouped, source)

        def quantize_queries(h):
            b0, b1 = QUERY_GROUPS[h]
            q_codes = placed("q_codes", h, [P, (b1 - b0) * NQ], U32, keep)
            q_scales = placed("q_scales", h, [P, (b1 - b0) * NQ], U8, keep)
            nc.vector.quantize_mx(out=q_codes[:].bitcast(FP8X4), scales=q_scales[:], in_=q_grp[h][:])
            for b in range(b0, b1):
                cols = slice((b - b0) * NQ, (b - b0 + 1) * NQ)
                queries[b] = q_codes[:, cols], q_scales[:, cols]

        def quantize_keys(b, h=0, parts=1):
            if b not in keys:
                keys[b] = placed("k_codes", b, [P, N], U32, ring), placed("k_scales", b, [P, N], U8, ring)
            k_codes, k_scales = keys[b]
            c0, c1 = h * N // parts, (h + 1) * N // parts
            nc.vector.quantize_mx(
                out=k_codes[:, c0:c1].bitcast(FP8X4), scales=k_scales[:, c0:c1], in_=k_grp[b][:, c0 * LANES : c1 * LANES]
            )

        def score(b, h=0, parts=1):
            q_codes, q_scales = queries[b]
            k_codes, k_scales = keys[b]
            n = LANES // parts
            scores[b, h] = in_bank(f"scores{b}{h}", [P, n, NQ])
            for i in range(n):
                cols = slice((h * n + i) * P, (h * n + i + 1) * P)
                nc.tensor.matmul_mx(
                    out=scores[b, h][:, i, :],
                    lhsT=k_codes[:, cols].bitcast(FP8X4),
                    lhsT_scale=k_scales[:, cols],
                    rhs=q_codes.bitcast(FP8X4),
                    rhs_scale=q_scales,
                    start=True,
                    stop=True,
                )

        def quantize_values(b):
            v_codes = placed("v_codes", b, [P, D], U32, ring)
            v_scales = placed("v_scales", b, [P, D], U8, ring)
            values[b] = v_codes, v_scales
            nc.vector.quantize_mx(out=v_codes[:].bitcast(FP8X4), scales=v_scales[:], in_=v_grp[b][:])

        def multiply(b, h=0, parts=1):
            w_codes, w_scales = weights[b]
            v_codes, v_scales = values[b]
            d0, d1 = h * D // parts, (h + 1) * D // parts
            acc[b, h] = in_bank(f"acc{b}{h}", [P, d1 - d0])
            nc.tensor.matmul_mx(
                out=acc[b, h][:],
                lhsT=w_codes[:].bitcast(FP8X4),
                lhsT_scale=w_scales[:],
                rhs=v_codes[:, d0:d1].bitcast(FP8X4),
                rhs_scale=v_scales[:, d0:d1],
                start=True,
                stop=True,
            )

        def finish(b, h=0, parts=1):
            if b not in ys:
                ys[b] = placed("y", b, [P, D], F32, ring)
            cols = slice(h * D // parts, (h + 1) * D // parts)
            nc.vector.scalar_tensor_tensor(
                out=ys[b][:, cols], in0=acc[b, h][:], scalar=1.0 / 16.0, in1=chans[:, cols], op0=MULT, op1=MULT
            )
            nc.sync.dma_start(out[b][:, cols], ys[b][:, cols])

        def sigmoid(b, h=0, parts=1):
            bias, scale = tokens[b][:, 0, :], tokens[b][:, 1, :]
            if b not in ps:
                ps[b] = placed("p", b, [P, LANES, NQ], F32, keep)
            n = LANES // parts
            for i in range(n):
                t = h * n + i
                nc.scalar.activation(
                    ps[b][:, t, :], scores[b, h][:, i, :], SIGMOID, bias=bias[:, t : t + 1], scale=scale[:, t : t + 1]
                )

        def weigh(b, engine):
            p, scale = ps[b], tokens[b][:, 1, :]
            w_grp[b] = placed("w_grp", b, [P, NQ, LANES], BF16, ring)
            engine.tensor_tensor(
                w_grp[b][:].rearrange("s (c i) t -> s c t i", i=LINE),
                p[:].rearrange("s t (c i) -> s c t i", i=LINE),
                scale.unsqueeze(1).unsqueeze(3).to_broadcast([P, NQ // LINE, LANES, LINE]),
                MULT,
            )

        def quantize_weights(b):
            w_codes = placed("w_codes", b, [P, NQ], U32, ring)
            w_scales = placed("w_scales", b, [P, NQ], U8, ring)
            nc.vector.quantize_mx(
                out=w_codes[:].bitcast(FP8X4), scales=w_scales[:], in_=w_grp[b][:].rearrange("s q t -> s (q t)")
            )
            weights[b] = w_codes, w_scales

        vector, scalar, gpsimd = nc.vector, nc.scalar, nc.gpsimd
        load_pool(0, 0)
        load_row("kb", 0, SEG)
        load_pool(0, 1)
        load_row("ts", 0, 2 * SEG)
        load_row("kb", SEG, 2 * SEG)
        load_queries(0)
        load_row("kb", 2 * SEG, T)
        load_pool(0, 2)
        load_row("ts", 2 * SEG, T)
        load_pool(0, 3)
        for j in range(LANES):
            load_pool(1, j)

        for name, b in (("kb", 0), ("ts", 0), ("kb", 1), ("kb", 2), ("kb", 3), ("ts", 2), ("ts", 3)):
            gather_tokens(name, b, vector)
        cast_queries(0, gpsimd)
        for j in range(LANES):
            gather(0, j, scalar)
            turn(0, j)
            if j == 1:
                gather_tokens("ts", 1, scalar)
                turn_tokens(0, 2, vector)
        for j in range(LANES):
            load_pool(2, j)
        load_chans()
        weave(0, gpsimd)
        copy_values(0, 0, vector)
        copy_values(0, 1, vector)
        gather(1, 0, scalar)
        turn(1, 0)
        quantize_queries(0)
        quantize_keys(0)
        score(0)
        quantize_values(0)
        for j in range(1, LANES):
            gather(1, j, scalar)
            turn(1, j)
        for j in range(LANES):
            load_pool(3, j)
        weave(1, gpsimd)
        gather(2, 0, vector)
        turn(2, 0)
        copy_values(1, 0, vector)
        copy_values(1, 1, vector)
        gather(2, 1, scalar)
        turn(2, 1)
        sigmoid(0)
        for j in range(2, LANES):
            gather(2, j, scalar)
            turn(2, j)
        quantize_keys(1)
        score(1)
        weigh(0, vector)
        quantize_values(1)
        quantize_weights(0)
        multiply(0)
        weave(2, gpsimd)
        gather(3, 0, scalar)
        copy_values(2, 0, vector)
        copy_values(2, 1, vector)
        turn_tokens(2, B, vector)
        finish(0)
        sigmoid(1)
        gather(3, 1, scalar)
        gather(3, 2, scalar)
        gather(3, 3, scalar)
        for j in range(LANES):
            turn(3, j)
        quantize_keys(2)
        score(2)
        weigh(1, vector)
        quantize_values(2)
        quantize_weights(1)
        multiply(1)
        weave(3, gpsimd, 0, 2)
        weave(3, scalar, 2, 4)
        finish(1)
        copy_values(3, 0, vector)
        copy_values(3, 1, scalar)
        quantize_keys(3, 0, 2)
        score(3, 0, 2)
        sigmoid(2)
        quantize_keys(3, 1, 2)
        score(3, 1, 2)
        quantize_values(3)
        weigh(2, vector)
        sigmoid(3, 0, 2)
        sigmoid(3, 1, 2)
        quantize_weights(2)
        multiply(2)
        weigh(3, vector)
        quantize_weights(3)
        finish(2)
        multiply(3, 0, 2)
        multiply(3, 1, 2)
        finish(3, 0, 2)
        finish(3, 1, 2)
